import numpy as np
import ml_dtypes


def mxq(x, axis, fmt="e4m3"):
    dtype, down = {"e4m3": (ml_dtypes.float8_e4m3fn, 7), "e5m2": (ml_dtypes.float8_e5m2, 14)}[fmt]
    v = np.moveaxis(np.asarray(x, np.float32).astype(ml_dtypes.bfloat16).astype(np.float64), axis, -1)
    blocks = v.reshape(v.shape[:-1] + (-1, 32))
    amax = np.abs(blocks).max(-1, keepdims=True)
    byte = np.maximum(np.where(amax > 0, np.frexp(amax)[1] - 1 + 127, 0) - down, 1)
    scale = np.exp2(byte - 127.0)
    codes = (blocks / scale).astype(np.float32).astype(dtype).astype(np.float64)
    return np.moveaxis((codes * scale).reshape(v.shape), -1, axis)


WIDE = False


def mx_kscale(k):
    if not WIDE:
        return np.ones(k)
    levels = np.array([24, -24, 12, -12, 0])
    if k % 512:
        return np.exp2(np.random.permutation(np.resize(levels, k // 32))).repeat(32)
    a = np.empty((k // 512, 16))
    for p in range(k // 512):
        a[p, :8] = np.random.permutation(np.resize(levels, 8))
        for g in range(8):
            far = levels[np.abs(levels - a[p, g]) >= 10]
            a[p, g + 8] = far[np.random.randint(len(far))]
    return np.exp2(a.ravel()).repeat(32)


def f64(x):
    return np.asarray(x).astype(np.float64)


def striped(idx):
    return np.tile(idx.reshape(-1, 16).T, (8, 1)).astype(np.uint16)


def unstriped(offs):
    return offs[:16].T.reshape(-1).astype(np.int64)


E2M1 = np.array([0.0, 0.5, 1.0, 1.5, 2.0, 3.0, 4.0, 6.0, -0.0, -0.5, -1.0, -1.5, -2.0, -3.0, -4.0, -6.0])


def pack_weight(w, fmt):
    k, n = w.shape
    w = f64(np.asarray(w, np.float32).astype(ml_dtypes.bfloat16)).reshape(k // 32, 32, n)
    amax = np.abs(w).max(1)
    if fmt == "e4m3":
        byte = np.frexp(amax)[1] - 1 + 127 - 7
    else:
        mant, ex = np.frexp(amax / 6.0)
        byte = np.where(mant > 0.5, ex, ex - 1) + 127
    byte = np.clip(np.where(amax > 0, byte, 1), 1, 254)
    scaled = (w * np.exp2(127.0 - byte)[:, None, :]).reshape(k, n).astype(np.float32)
    by_word = np.ascontiguousarray(scaled.reshape(k // 512, 128, 4, n).transpose(0, 1, 3, 2))
    if fmt == "e4m3":
        words = by_word.astype(ml_dtypes.float8_e4m3fn).view(np.uint8)
    else:
        c = by_word.astype(ml_dtypes.float4_e2m1fn).view(np.uint8) & 0xF
        words = (c[..., 0::2] | (c[..., 1::2] << 4)).reshape(k // 512, 128, 2 * n)
    return np.ascontiguousarray(words), np.ascontiguousarray(byte.astype(np.uint8).reshape(k // 512, 16, n))


def unpack_weight(words, scales, fmt):
    g, _, n = scales.shape
    words = np.ascontiguousarray(words).reshape(g, 128, n, -1)
    if fmt == "e4m3":
        vals = words.view(ml_dtypes.float8_e4m3fn).astype(np.float64)
    else:
        nib = np.empty((g, 128, n, 4), np.uint8)
        nib[..., 0::2] = words & 0xF
        nib[..., 1::2] = words >> 4
        vals = E2M1[nib]
    vals = vals * np.repeat(np.exp2(scales.astype(np.float64) - 127.0), 8, axis=1)[..., None]
    return vals.transpose(0, 1, 3, 2).reshape(g * 512, n)


def pack_table4(v):
    words, scales = pack_weight(v, "e2m1")
    g, t = words.shape[0] // 2, v.shape[1]
    return np.ascontiguousarray(words.reshape(g, 2, 128, t, 2).transpose(0, 2, 3, 1, 4).reshape(g, 128, t, 4)), scales


def unpack_table4(words, scales):
    g, _, t, _ = words.shape
    return unpack_weight(words.reshape(g, 128, t, 2, 2).transpose(0, 3, 1, 2, 4).reshape(2 * g, 128, 2 * t), scales, "e2m1")


def planes(y):
    n, m = y.shape
    v = y.astype(np.float32).astype(ml_dtypes.bfloat16).astype(np.float64).reshape(n // 32, 32, m)
    top = np.abs(v).max(1)
    byte = np.clip(np.where(top > 0, np.frexp(top)[1] - 1 + 127 - 7, 1), 1, 254)
    codes = (v * np.exp2(127.0 - byte)[:, None, :]).reshape(n, m).astype(np.float32).astype(ml_dtypes.float8_e4m3fn).view(np.uint8)
    words = codes.reshape(n // 512, 128, 4, m).transpose(0, 1, 3, 2)
    return np.ascontiguousarray(words), np.ascontiguousarray(byte.astype(np.uint8).reshape(n // 512, 16, m))


K, M, N, T, J = 1024, 1024, 1024, 2048, 1024


def setup_inputs():
    n = np.random.standard_normal
    s = mx_kscale(K)[:, None]
    s2 = mx_kscale(M)[:, None]
    h = np.tanh(n((N, T)))
    p_tab = pack_table4(h * s2)
    return {
        "x": (n((K, J)) * s).astype(np.float32),
        "tab_words": p_tab[0],
        "tab_scales": p_tab[1],
        "wn": (n((K, N)) / np.sqrt(K) / s).astype(np.float32),
        "un": (n((M, N)) / np.sqrt(M) / s2).astype(np.float32),
        "bn": (0.3 * n(N)).astype(np.float32),
        "hT": (h).astype(np.float32),
        "wgo": np.tile(np.random.uniform(0.5, 2.0, J), (128, 1)).astype(np.float32),
        "offs": striped(np.random.permutation(T)[:J]),
    }


def reference(x, tab_words, tab_scales, wn, un, bn, hT, wgo, offs):
    idx = unstriped(offs)
    x_ = mxq(f64(x), 0, "e4m3")
    tab_ = unpack_table4(tab_words, tab_scales)[:, idx]
    wn_ = mxq(f64(wn), 0, "e4m3")
    un_ = mxq(f64(un), 0, "e4m3")
    sn = wn_.T @ x_ + un_.T @ tab_
    out = np.zeros((N, T))
    out[:, idx] = f64(wgo)[0] * (np.tanh(sn + f64(bn)[:, None]) + f64(hT)[:, idx])
    return (out,) + planes(out)

@@ -1,0 +1,281 @@
+from contextlib import ExitStack
+
+import concourse.mybir as mybir
+from concourse.masks import make_identity
+
+K, M, N, T, J = 1024, 1024, 1024, 2048, 1024
+FLOPS = 2 * (K + M) * N * J
+
+F32 = mybir.dt.float32
+BF16 = mybir.dt.bfloat16
+I32 = mybir.dt.int32
+U32 = mybir.dt.uint32
+U16 = mybir.dt.uint16
+U8 = mybir.dt.uint8
+FP8X4 = mybir.dt.float8_e4m3fn_x4
+FP4X4 = mybir.dt.float4_e2m1fn_x4
+ALU = mybir.AluOpType
+ACT = mybir.ActivationFunctionType
+
+P = 128
+PACK = 4
+K_PASS = P * PACK
+BANK = 512
+TILES = N // P
+HALVES = J // BANK
+CHUNKS = T // BANK
+LIST_ROWS = 16
+QUARTER = J // 4
+
+
+def tile_list_tgn_rnnP_kernel(
+    tc, x, tab_words, tab_scales, wn, un, bn, hT, wgo, offs, out_0, out_1, out_2
+):
+    nc = tc.nc
+    with ExitStack() as ctx:
+        keep = ctx.enter_context(tc.tile_pool(name="keep", bufs=1))
+        psum = ctx.enter_context(tc.psum_pool(name="psum", bufs=1))
+
+        def tiles(count, shape, dtype, name):
+            return [keep.tile(shape, dtype, name=name + str(i), align_bytes=64) for i in range(count)]
+
+        offsets = keep.tile([P, J // LIST_ROWS], U16, name="offsets")
+        tab_w = keep.tile([P, T], I32, name="tab_w", align_bytes=64)
+        tab_s = keep.tile([P, 2 * T], U8, name="tab_s", align_bytes=64)
+        picked_w = keep.tile([P, J], U32, name="picked_w", align_bytes=64)
+        picked_s = tiles(2, [P, J], U8, "picked_s")
+        parted_w = keep.tile([P, 2 * 2 * J], U8, name="parted_w", align_bytes=64)
+        ident = keep.tile([P, P], F32, name="ident", align_bytes=64)
+        bn_rows = keep.tile([P, P], F32, name="bn_rows", align_bytes=64)
+        bias = keep.tile([P, 2 * TILES], F32, name="bias", align_bytes=64)
+        weight = keep.tile([P, J], F32, name="weight", align_bytes=64)
+        x_raw = tiles(8, [P, PACK * QUARTER], F32, "x_raw")
+        x_bf = tiles(3, [P, PACK * QUARTER], BF16, "x_bf")
+        x_codes = tiles(2, [P, J], U32, "x_codes")
+        x_scales = tiles(2, [P, J], U8, "x_scales")
+        w_raw = tiles(3, [P, PACK * BANK], F32, "w_raw")
+        w_bf = tiles(2, [P, PACK * BANK], BF16, "w_bf")
+        w_codes = tiles(2, [P, BANK], U32, "w_codes")
+        w_scales = tiles(2, [P, BANK], U8, "w_scales")
+        h_rows = tiles(2, [P, T], F32, "h_rows")
+        summed = tiles(2, [P, J], F32, "summed")
+        pages = tiles(2, [P, T], F32, "pages")
+        y_turned = tiles(2, [P, T], BF16, "y_turned")
+        y_bf = tiles(2, [P, T], BF16, "y_bf")
+        y_codes = tiles(2, [P, BANK], I32, "y_codes")
+        y_scales = tiles(2, [P, BANK], U8, "y_scales")
+        banks = [psum.tile([P, BANK], F32, name="bank" + str(i)) for i in range(8)]
+
+        def interleave(dst, src):
+            nc.scalar.copy(
+                out=dst.rearrange("p (c i t) -> p c t i", i=4, t=PACK),
+                in_=src.rearrange("p t (c i) -> p c t i", i=4),
+            )
+
+        def load_x(q):
+            for a in range(2):
+                nc.sync.dma_start(
+                    out=x_raw[2 * q + a][:].rearrange("p (t c) -> p t c", t=PACK),
+                    in_=x[a * K_PASS : (a + 1) * K_PASS, q * QUARTER : (q + 1) * QUARTER].rearrange(
+                        "(p t) c -> p t c", t=PACK
+                    ),
+                )
+
+        def quantise_x(q):
+            cols = slice(q * QUARTER, (q + 1) * QUARTER)
+            for a in range(2):
+                staged = x_bf[(2 * q + a) % 3]
+                interleave(staged[:], x_raw[2 * q + a][:].rearrange("p (t c) -> p t c", t=PACK))
+                nc.vector.quantize_mx(out=x_codes[a][:, cols].bitcast(FP8X4), scales=x_scales[a][:, cols], in_=staged[:])
+
+        def load_w(k):
+            raw = w_raw[k % 3][:].rearrange("p (t c) -> p t c", t=PACK)
+            for g in (2, 3, 0, 1):
+                source = (wn, un)[g // 2]
+                a = g % 2
+                nc.sync.dma_start(
+                    out=raw[:, :, g * P : (g + 1) * P],
+                    in_=source[a * K_PASS : (a + 1) * K_PASS, k * P : (k + 1) * P].rearrange("(p t) c -> p t c", t=PACK),
+                )
+
+        def quantise_w(k, pieces):
+            raw = w_raw[k % 3][:].rearrange("p (t c) -> p t c", t=PACK)
+            width = BANK // pieces
+            for piece in sorted(range(pieces), key=lambda i: (i + pieces // 2) % pieces):
+                cols = slice(piece * width, (piece + 1) * width)
+                staged = w_bf[k % 2][:, PACK * piece * width : PACK * (piece + 1) * width]
+                interleave(staged, raw[:, :, cols])
+                nc.vector.quantize_mx(out=w_codes[k % 2][:, cols].bitcast(FP8X4), scales=w_scales[k % 2][:, cols], in_=staged)
+
+        def load_h(k):
+            nc.sync.dma_start(out=h_rows[k % 2][:], in_=hT[k * P : (k + 1) * P, :])
+
+        def tanh_part(k, first, count):
+            if k == 0 and first < 3 * QUARTER:
+                return x_raw[2 * (first // QUARTER + 1) + 1][:, 0:count]
+            return w_raw[(k + (1 if k < 2 else 1)) % 3][:, first : first + count]
+
+        def multiply(k, first, count, width, bank):
+            for start in range(first, first + count, width):
+                cols = slice(start, start + width)
+                for g in (2, 3, 0, 1):
+                    a = g % 2
+                    if g < 2:
+                        rhs = x_codes[a][:, cols].bitcast(FP8X4)
+                        rhs_scale = x_scales[a][:, cols]
+                    else:
+                        rhs = parted_w[:, 2 * (a * J + start) : 2 * (a * J + start + width)].bitcast(FP4X4)
+                        rhs_scale = picked_s[a][:, cols]
+                    nc.tensor.matmul_mx(
+                        out=bank[:, start - first : start - first + width],
+                        lhsT=w_codes[k % 2][:, g * P : (g + 1) * P].bitcast(FP8X4),
+                        lhsT_scale=w_scales[k % 2][:, g * P : (g + 1) * P],
+                        rhs=rhs,
+                        rhs_scale=rhs_scale,
+                        start=(g == 2),
+                        stop=(g == 1),
+                    )
+            nc.scalar.activation(
+                out=tanh_part(k, first, count), in_=bank[:, 0:count], func=ACT.Tanh, bias=bias[:, k : k + 1]
+            )
+
+        def gather_add(k, first, count):
+            part = offsets[:, first // LIST_ROWS : (first + count) // LIST_ROWS]
+            nc.vector.tensor_tensor(
+                out=summed[k % 2][:, first : first + count],
+                in0=h_rows[k % 2][:].indirect(part),
+                in1=tanh_part(k, first, count),
+                op=ALU.add,
+            )
+
+        def scatter(k, first, count):
+            cols = slice(first, first + count)
+            part = offsets[:, first // LIST_ROWS : (first + count) // LIST_ROWS]
+            nc.vector.tensor_tensor(
+                out=pages[k % 2][:].indirect(part), in0=summed[k % 2][:, cols], in1=weight[:, cols], op=ALU.mult
+            )
+
+        def turn(k, first_banks, first_copies):
+            turned = y_turned[k % 2]
+            for b in range(4):
+                bank = first_banks[b]
+                for g in range(CHUNKS):
+                    first = g * BANK + b * P
+                    nc.tensor.transpose(bank[:, g * P : (g + 1) * P], pages[k % 2][:, first : first + P], ident[:])
+                first_copies[b](
+                    out=turned[:, b * BANK : (b + 1) * BANK].rearrange("p (u r e) -> p u r e", u=2, e=2),
+                    in_=bank[:].rearrange("p (r u e) -> p u r e", u=2, e=2),
+                )
+
+        def turn_back(k, second_banks, second_copies, pieces, queues):
+            a, w = divmod(k, 4)
+            staged = y_bf[k % 2]
+            words = y_turned[k % 2][:].bitcast(F32)
+            width = BANK // pieces
+            span = 4 // len(second_banks)
+            for i, bank in enumerate(second_banks):
+                for s in range(2 * span):
+                    first = (2 * span * i + s) * P
+                    nc.tensor.transpose(bank[:, s * P : (s + 1) * P], words[:, first : first + P], ident[:])
+                second_copies[i](
+                    out=staged[:].bitcast(F32)[:, 2 * P * span * i : 2 * P * span * (i + 1)].rearrange(
+                        "p (b c u) -> p b c u", b=span, u=2
+                    ),
+                    in_=bank[:, 0 : 2 * P * span].rearrange("p (b u c) -> p b c u", b=span, u=2),
+                )
+            for piece in range(pieces):
+                cols = slice(piece * width, (piece + 1) * width)
+                nc.vector.quantize_mx(
+                    out=y_codes[k % 2][:, cols].bitcast(FP8X4),
+                    scales=y_scales[a][4 * w : P, cols],
+                    in_=staged[:, PACK * piece * width : PACK * (piece + 1) * width],
+                )
+            codes_out = out_1[a].rearrange("p t b -> p (t b)").bitcast(I32)
+            for g in range(CHUNKS):
+                queues[g % 2].dma_start(
+                    out=codes_out[32 * w : 32 * w + 32, g * BANK : (g + 1) * BANK], in_=y_codes[k % 2][32 * g : 32 * g + 32, :]
+                )
+            if w == 3:
+                for g in range(CHUNKS):
+                    queues[g % 2].dma_start(
+                        out=out_2[a, :, g * BANK : (g + 1) * BANK].bitcast(I32),
+                        in_=y_scales[a][32 * g : 32 * g + 16, :].bitcast(I32),
+                    )
+
+        nc.vector.memset(tab_s[:].bitcast(I32), 0)
+        nc.gpsimd.memset(bn_rows[:], 0.0)
+        make_identity(nc, ident[:])
+        nc.sync.dma_start(offsets[:], offs)
+        for q in range(4):
+            nc.sync.dma_start(
+                out=tab_s[32 * q : 32 * q + 4, :].bitcast(I32).rearrange("r (a t) -> r a t", a=2),
+                in_=tab_scales[:, 4 * q : 4 * q + 4, :].bitcast(I32).rearrange("a r t -> r a t"),
+            )
+        nc.sync.dma_start(out=tab_w[:], in_=tab_words[0].rearrange("p t b -> p (t b)").bitcast(I32))
+        nc.sync.dma_start(out=bn_rows[0:TILES, :], in_=bn.rearrange("(i p) -> i p", p=P))
+        nc.sync.dma_start(out=bn_rows[TILES : 2 * TILES, :], in_=wgo[0].rearrange("(i p) -> i p", p=P))
+        for page in pages:
+            nc.vector.memset(page[:], 0.0)
+        load_x(0)
+        load_w(0)
+        load_h(0)
+        for q in range(1, 4):
+            load_x(q)
+        load_w(1)
+        load_h(1)
+        load_w(2)
+
+        for a in range(2):
+            nc.vector.tensor_copy(picked_s[a][:], tab_s[:, a * T : (a + 1) * T].indirect(offsets[:]))
+        nc.vector.tensor_copy(picked_w[:], tab_w[:].bitcast(U32).indirect(offsets[:]))
+        nc.vector.tensor_copy(
+            out=parted_w[:].bitcast(U16).rearrange("p (d j) -> p d j", d=2),
+            in_=picked_w[:].bitcast(U16).rearrange("p (j d) -> p d j", d=2),
+        )
+        nc.tensor.transpose(banks[2][:, 0:P], bn_rows[:], ident[:])
+        nc.scalar.copy(out=bias[:], in_=banks[2][:, 0 : 2 * TILES])
+        for h in range(HALVES):
+            for b in range(4):
+                column = TILES + 4 * h + b
+                nc.tensor.transpose(
+                    banks[h][:, b * P : (b + 1) * P], bias[:, column : column + 1].to_broadcast([P, P]), ident[:]
+                )
+            nc.scalar.copy(out=weight[:, h * BANK : (h + 1) * BANK], in_=banks[h][:])
+
+        quantise_x(0)
+        quantise_w(0, 4)
+        load_w(3)
+        for q in range(4):
+            if q < 3:
+                quantise_x(q + 1)
+            else:
+                quantise_w(1, 2)
+            multiply(0, q * QUARTER, QUARTER, P, banks[4 + q])
+            gather_add(0, q * QUARTER, QUARTER)
+            scatter(0, q * QUARTER, QUARTER)
+        load_h(2)
+        load_w(4)
+        nc.sync.dma_start(out=out_0[0:P, :], in_=pages[0][:])
+
+        copy_s, copy_v = nc.scalar.copy, nc.vector.tensor_copy
+        both_sync = (nc.sync, nc.sync)
+        for k in range(1, TILES):
+            pair = banks[2 * (k % 2) : 2 * (k % 2) + 2]
+            for ahead in [k + 1]:
+                if ahead < TILES:
+                    quantise_w(ahead, 1)
+            for h in range(HALVES):
+                multiply(k, h * BANK, BANK, BANK, pair[h])
+            gather_add(k, 0, J)
+            scatter(k, 0, J)
+            if k + 2 < TILES:
+                load_h(k + 2)
+            if k + 4 < TILES and k + 4 > 4:
+                load_w(k + 4)
+            if k >= 2:
+                turn_back(k - 2, pair, [copy_s] * 2, 1, both_sync)
+            turn(k - 1, pair[::-1] * 2, [copy_s] * 4)
+            nc.sync.dma_start(out=out_0[k * P : (k + 1) * P, :], in_=pages[k % 2][:])
+        turn_back(TILES - 2, banks[0:2] + banks[6:8], [copy_s] * 4, 1, both_sync)
+        turn(TILES - 1, banks[0:2] + banks[6:8], [copy_s, copy_v] * 2)
+        turn_back(TILES - 1, banks[2:6], [copy_s, copy_v, copy_s, copy_s], 2, (nc.sync, nc.scalar))

@@ -42,8 +42,7 @@ def tile_list_tgn_rnnP_kernel(
         offsets = keep.tile([P, J // LIST_ROWS], U16, name="offsets")
         tab_w = keep.tile([P, T], I32, name="tab_w", align_bytes=64)
         tab_s = keep.tile([P, 2 * T], U8, name="tab_s", align_bytes=64)
-        picked_w = keep.tile([P, J], U32, name="picked_w", align_bytes=64)
-        picked_s = tiles(2, [P, J], U8, "picked_s")
+        picked_w = keep.tile([P, J], U32, name="picked_w", tag="picked", align_bytes=64)
         parted_w = keep.tile([P, 2 * 2 * J], U8, name="parted_w", align_bytes=64)
         ident = keep.tile([P, P], F32, name="ident", align_bytes=64)
         bn_rows = keep.tile([P, P], F32, name="bn_rows", align_bytes=64)
@@ -125,7 +124,7 @@ def tile_list_tgn_rnnP_kernel(
                         rhs_scale = x_scales[a][:, cols]
                     else:
                         rhs = parted_w[:, 2 * (a * J + start) : 2 * (a * J + start + width)].bitcast(FP4X4)
-                        rhs_scale = picked_s[a][:, cols]
+                        rhs_scale = picked_s[:, a * J + start : a * J + start + width]
                     nc.tensor.matmul_mx(
                         out=bank[:, start - first : start - first + width],
                         lhsT=w_codes[k % 2][:, g * P : (g + 1) * P].bitcast(FP8X4),
@@ -225,13 +224,14 @@ def tile_list_tgn_rnnP_kernel(
         load_h(1)
         load_w(2)
 
-        for a in range(2):
-            nc.vector.tensor_copy(picked_s[a][:], tab_s[:, a * T : (a + 1) * T].indirect(offsets[:]))
         nc.vector.tensor_copy(picked_w[:], tab_w[:].bitcast(U32).indirect(offsets[:]))
         nc.vector.tensor_copy(
             out=parted_w[:].bitcast(U16).rearrange("p (d j) -> p d j", d=2),
             in_=picked_w[:].bitcast(U16).rearrange("p (j d) -> p d j", d=2),
         )
+        picked_s = keep.tile([P, 2 * J], U8, name="picked_s", tag="picked", align_bytes=64)
+        for a in range(2):
+            nc.vector.tensor_copy(picked_s[:, a * J : (a + 1) * J], tab_s[:, a * T : (a + 1) * T].indirect(offsets[:]))
         nc.tensor.transpose(banks[2][:, 0:P], bn_rows[:], ident[:])
         nc.scalar.copy(out=bias[:], in_=banks[2][:, 0 : 2 * TILES])
         for h in range(HALVES):
@@ -259,23 +259,32 @@ def tile_list_tgn_rnnP_kernel(
 
         copy_s, copy_v = nc.scalar.copy, nc.vector.tensor_copy
         both_sync = (nc.sync, nc.sync)
-        for k in range(1, TILES):
-            pair = banks[2 * (k % 2) : 2 * (k % 2) + 2]
-            for ahead in [k + 1]:
-                if ahead < TILES:
-                    quantise_w(ahead, 1)
-            for h in range(HALVES):
-                multiply(k, h * BANK, BANK, BANK, pair[h])
-            gather_add(k, 0, J)
-            scatter(k, 0, J)
-            if k + 2 < TILES:
-                load_h(k + 2)
-            if k + 4 < TILES and k + 4 > 4:
-                load_w(k + 4)
-            if k >= 2:
-                turn_back(k - 2, pair, [copy_s] * 2, 1, both_sync)
-            turn(k - 1, pair[::-1] * 2, [copy_s] * 4)
-            nc.sync.dma_start(out=out_0[k * P : (k + 1) * P, :], in_=pages[k % 2][:])
+        quantise_w(2, 1)
+        for h in range(HALVES):
+            multiply(1, h * BANK, BANK, BANK, banks[h])
+        gather_add(1, 0, J)
+        load_h(3)
+        load_w(5)
+        for p in range(1, TILES):
+            k = p + 1
+            if k + 1 < TILES:
+                quantise_w(k + 1, 1)
+            if p >= 3:
+                turn_back(p - 3, banks[2:4], [copy_s] * 2, 1, both_sync)
+            if k < TILES:
+                for h in range(HALVES):
+                    multiply(k, h * BANK, BANK, BANK, banks[h])
+                gather_add(k, 0, J)
+                if k + 2 < TILES:
+                    load_h(k + 2)
+                if k + 4 < TILES:
+                    load_w(k + 4)
+            if p >= 2:
+                turn(p - 2, banks[1::-1] * 2, [copy_s] * 4)
+            scatter(p, 0, J)
+            nc.sync.dma_start(out=out_0[p * P : (p + 1) * P, :], in_=pages[p % 2][:])
+        turn_back(TILES - 3, banks[0:2], [copy_s] * 2, 1, both_sync)
+        turn(TILES - 2, banks[0:2] * 2, [copy_s] * 4)
         turn_back(TILES - 2, banks[0:2] + banks[6:8], [copy_s] * 4, 1, both_sync)
         turn(TILES - 1, banks[0:2] + banks[6:8], [copy_s, copy_v] * 2)
         turn_back(TILES - 1, banks[2:6], [copy_s, copy_v, copy_s, copy_s], 2, (nc.sync, nc.scalar))

@@ -26,6 +26,7 @@ HALVES = J // BANK
 CHUNKS = T // BANK
 LIST_ROWS = 16
 QUARTER = J // 4
+STORE_FROM = {3: 0, 4: 4, 6: 5, 7: 7}
 
 
 def tile_list_tgn_rnnP_kernel(
@@ -61,7 +62,7 @@ def tile_list_tgn_rnnP_kernel(
         pages = tiles(2, [P, T], F32, "pages")
         y_turned = tiles(2, [P, T], BF16, "y_turned")
         y_bf = tiles(2, [P, T], BF16, "y_bf")
-        y_codes = tiles(2, [P, BANK], I32, "y_codes")
+        y_codes = tiles(2, [P, 4 * BANK], I32, "y_codes")
         y_scales = tiles(2, [P, BANK], U8, "y_scales")
         banks = [psum.tile([P, BANK], F32, name="bank" + str(i)) for i in range(8)]
 
@@ -185,15 +186,18 @@ def tile_list_tgn_rnnP_kernel(
             for piece in range(pieces):
                 cols = slice(piece * width, (piece + 1) * width)
                 nc.vector.quantize_mx(
-                    out=y_codes[k % 2][:, cols].bitcast(FP8X4),
+                    out=y_codes[a][:, w * BANK + piece * width : w * BANK + (piece + 1) * width].bitcast(FP8X4),
                     scales=y_scales[a][4 * w : P, cols],
                     in_=staged[:, PACK * piece * width : PACK * (piece + 1) * width],
                 )
-            codes_out = out_1[a].rearrange("p t b -> p (t b)").bitcast(I32)
-            for g in range(CHUNKS):
-                queues[g % 2].dma_start(
-                    out=codes_out[32 * w : 32 * w + 32, g * BANK : (g + 1) * BANK], in_=y_codes[k % 2][32 * g : 32 * g + 32, :]
-                )
+            if k in STORE_FROM:
+                held = slice(STORE_FROM[k] % 4, w + 1)
+                codes_out = out_1[a].rearrange("p t b -> p (t b)").bitcast(I32).rearrange("(w q) t -> q w t", q=32)
+                for g in range(CHUNKS):
+                    queues[g % 2].dma_start(
+                        out=codes_out[:, held, g * BANK : (g + 1) * BANK],
+                        in_=y_codes[a][32 * g : 32 * g + 32, :].rearrange("q (w c) -> q w c", w=4)[:, held, :],
+                    )
             if w == 3:
                 for g in range(CHUNKS):
                     queues[g % 2].dma_start(
@@ -217,11 +221,11 @@ def tile_list_tgn_rnnP_kernel(
             nc.vector.memset(page[:], 0.0)
         load_x(0)
         load_w(0)
+        load_x(1)
         load_h(0)
-        for q in range(1, 4):
-            load_x(q)
+        load_x(2)
+        load_x(3)
         load_w(1)
-        load_h(1)
         load_w(2)
 
         nc.vector.tensor_copy(picked_w[:], tab_w[:].bitcast(U32).indirect(offsets[:]))
@@ -245,6 +249,7 @@ def tile_list_tgn_rnnP_kernel(
         quantise_x(0)
         quantise_w(0, 4)
         load_w(3)
+        load_h(1)
         for q in range(4):
             if q < 3:
                 quantise_x(q + 1)
@@ -287,4 +292,4 @@ def tile_list_tgn_rnnP_kernel(
         turn(TILES - 2, banks[0:2] * 2, [copy_s] * 4)
         turn_back(TILES - 2, banks[0:2] + banks[6:8], [copy_s] * 4, 1, both_sync)
         turn(TILES - 1, banks[0:2] + banks[6:8], [copy_s, copy_v] * 2)
-        turn_back(TILES - 1, banks[2:6], [copy_s, copy_v, copy_s, copy_s], 2, (nc.sync, nc.scalar))
+        turn_back(TILES - 1, banks[2:6], [copy_s, copy_v, copy_s, copy_s], 4, (nc.sync, nc.scalar))

@@ -20,12 +20,21 @@ ACT = mybir.ActivationFunctionType
 P = 128
 PACK = 4
 K_PASS = P * PACK
+PASSES = K // K_PASS
 BANK = 512
 TILES = N // P
+TILES_A_PASS = K_PASS // P
 HALVES = J // BANK
-CHUNKS = T // BANK
+GROUPS = T // BANK
+BLOCKS = BANK // P
+QUADRANT = 32
+QUADRANTS = P // QUADRANT
+SCALE_ROWS = 4
 LIST_ROWS = 16
-QUARTER = J // 4
+QUARTERS = 4
+QUARTER = J // QUARTERS
+RUN = 4
+OPERAND_ORDER = (2, 3, 0, 1)
 STORE_FROM = {3: 0, 4: 4, 6: 5, 7: 7}
 
 
@@ -42,85 +51,95 @@ def tile_list_tgn_rnnP_kernel(
 
         offsets = keep.tile([P, J // LIST_ROWS], U16, name="offsets")
         tab_w = keep.tile([P, T], I32, name="tab_w", align_bytes=64)
-        tab_s = keep.tile([P, 2 * T], U8, name="tab_s", align_bytes=64)
+        tab_s = keep.tile([P, PASSES * T], U8, name="tab_s", align_bytes=64)
         picked_w = keep.tile([P, J], U32, name="picked_w", tag="picked", align_bytes=64)
-        parted_w = keep.tile([P, 2 * 2 * J], U8, name="parted_w", align_bytes=64)
+        parted_w = keep.tile([P, PASSES * 2 * J], U8, name="parted_w", align_bytes=64)
         ident = keep.tile([P, P], F32, name="ident", align_bytes=64)
         bn_rows = keep.tile([P, P], F32, name="bn_rows", align_bytes=64)
         bias = keep.tile([P, 2 * TILES], F32, name="bias", align_bytes=64)
         weight = keep.tile([P, J], F32, name="weight", align_bytes=64)
-        x_raw = tiles(8, [P, PACK * QUARTER], F32, "x_raw")
+        x_raw = tiles(QUARTERS * PASSES, [P, PACK * QUARTER], F32, "x_raw")
         x_bf = tiles(3, [P, PACK * QUARTER], BF16, "x_bf")
-        x_codes = tiles(2, [P, J], U32, "x_codes")
-        x_scales = tiles(2, [P, J], U8, "x_scales")
+        x_codes = tiles(PASSES, [P, J], U32, "x_codes")
+        x_scales = tiles(PASSES, [P, J], U8, "x_scales")
         w_raw = tiles(3, [P, PACK * BANK], F32, "w_raw")
         w_bf = tiles(2, [P, PACK * BANK], BF16, "w_bf")
-        w_codes = tiles(2, [P, BANK], U32, "w_codes")
-        w_scales = tiles(2, [P, BANK], U8, "w_scales")
+        w_codes = tiles(3, [P, BANK], U32, "w_codes")
+        w_scales = tiles(3, [P, BANK], U8, "w_scales")
         h_rows = tiles(2, [P, T], F32, "h_rows")
         summed = tiles(2, [P, J], F32, "summed")
         pages = tiles(2, [P, T], F32, "pages")
         y_turned = tiles(2, [P, T], BF16, "y_turned")
         y_bf = tiles(2, [P, T], BF16, "y_bf")
-        y_codes = tiles(2, [P, 4 * BANK], I32, "y_codes")
-        y_scales = tiles(2, [P, BANK], U8, "y_scales")
+        y_codes = tiles(PASSES, [P, TILES_A_PASS * BANK], I32, "y_codes")
+        y_scales = tiles(PASSES, [P, BANK], U8, "y_scales")
         banks = [psum.tile([P, BANK], F32, name="bank" + str(i)) for i in range(8)]
+        copy_s, copy_v = nc.scalar.copy, nc.vector.tensor_copy
+        both_sync = (nc.sync, nc.sync)
+
+        def by_row(flat):
+            return flat.rearrange("p (t c) -> p t c", t=PACK)
+
+        def pass_rows(source, a, cols):
+            return source[a * K_PASS : (a + 1) * K_PASS, cols].rearrange("(p t) c -> p t c", t=PACK)
 
         def interleave(dst, src):
             nc.scalar.copy(
-                out=dst.rearrange("p (c i t) -> p c t i", i=4, t=PACK),
-                in_=src.rearrange("p t (c i) -> p c t i", i=4),
+                out=dst.rearrange("p (c i t) -> p c t i", i=RUN, t=PACK),
+                in_=src.rearrange("p t (c i) -> p c t i", i=RUN),
             )
 
         def load_x(q):
-            for a in range(2):
+            for a in range(PASSES):
                 nc.sync.dma_start(
-                    out=x_raw[2 * q + a][:].rearrange("p (t c) -> p t c", t=PACK),
-                    in_=x[a * K_PASS : (a + 1) * K_PASS, q * QUARTER : (q + 1) * QUARTER].rearrange(
-                        "(p t) c -> p t c", t=PACK
-                    ),
+                    out=by_row(x_raw[PASSES * q + a][:]), in_=pass_rows(x, a, slice(q * QUARTER, (q + 1) * QUARTER))
                 )
 
         def quantise_x(q):
             cols = slice(q * QUARTER, (q + 1) * QUARTER)
-            for a in range(2):
-                staged = x_bf[(2 * q + a) % 3]
-                interleave(staged[:], x_raw[2 * q + a][:].rearrange("p (t c) -> p t c", t=PACK))
+            for a in range(PASSES):
+                staged = x_bf[(PASSES * q + a) % len(x_bf)]
+                interleave(staged[:], by_row(x_raw[PASSES * q + a][:]))
                 nc.vector.quantize_mx(out=x_codes[a][:, cols].bitcast(FP8X4), scales=x_scales[a][:, cols], in_=staged[:])
 
         def load_w(k):
-            raw = w_raw[k % 3][:].rearrange("p (t c) -> p t c", t=PACK)
-            for g in (2, 3, 0, 1):
-                source = (wn, un)[g // 2]
-                a = g % 2
+            raw = by_row(w_raw[k % len(w_raw)][:])
+            for operand in OPERAND_ORDER:
+                source = (wn, un)[operand // PASSES]
                 nc.sync.dma_start(
-                    out=raw[:, :, g * P : (g + 1) * P],
-                    in_=source[a * K_PASS : (a + 1) * K_PASS, k * P : (k + 1) * P].rearrange("(p t) c -> p t c", t=PACK),
+                    out=raw[:, :, operand * P : (operand + 1) * P],
+                    in_=pass_rows(source, operand % PASSES, slice(k * P, (k + 1) * P)),
                 )
 
         def quantise_w(k, pieces):
-            raw = w_raw[k % 3][:].rearrange("p (t c) -> p t c", t=PACK)
+            raw = by_row(w_raw[k % len(w_raw)][:])
             width = BANK // pieces
-            for piece in sorted(range(pieces), key=lambda i: (i + pieces // 2) % pieces):
+            for step in range(pieces):
+                piece = (step + pieces // 2) % pieces
                 cols = slice(piece * width, (piece + 1) * width)
                 staged = w_bf[k % 2][:, PACK * piece * width : PACK * (piece + 1) * width]
                 interleave(staged, raw[:, :, cols])
-                nc.vector.quantize_mx(out=w_codes[k % 2][:, cols].bitcast(FP8X4), scales=w_scales[k % 2][:, cols], in_=staged)
+                nc.vector.quantize_mx(
+                    out=w_codes[k % len(w_codes)][:, cols].bitcast(FP8X4),
+                    scales=w_scales[k % len(w_scales)][:, cols],
+                    in_=staged,
+                )
 
         def load_h(k):
             nc.sync.dma_start(out=h_rows[k % 2][:], in_=hT[k * P : (k + 1) * P, :])
 
         def tanh_part(k, first, count):
-            if k == 0 and first < 3 * QUARTER:
-                return x_raw[2 * (first // QUARTER + 1) + 1][:, 0:count]
-            return w_raw[(k + (1 if k < 2 else 1)) % 3][:, first : first + count]
+            if k == 0 and first < J - QUARTER:
+                return x_raw[PASSES * (first // QUARTER + 1) + 1][:, 0:count]
+            later = 4 if k == 2 else k + 1
+            return w_raw[later % len(w_raw)][:, first : first + count]
 
-        def multiply(k, first, count, width, bank):
+        def product(k, first, count, width, bank):
             for start in range(first, first + count, width):
                 cols = slice(start, start + width)
-                for g in (2, 3, 0, 1):
-                    a = g % 2
-                    if g < 2:
+                for operand in OPERAND_ORDER:
+                    a = operand % PASSES
+                    if operand < PASSES:
                         rhs = x_codes[a][:, cols].bitcast(FP8X4)
                         rhs_scale = x_scales[a][:, cols]
                     else:
@@ -128,91 +147,106 @@ def tile_list_tgn_rnnP_kernel(
                         rhs_scale = picked_s[:, a * J + start : a * J + start + width]
                     nc.tensor.matmul_mx(
                         out=bank[:, start - first : start - first + width],
-                        lhsT=w_codes[k % 2][:, g * P : (g + 1) * P].bitcast(FP8X4),
-                        lhsT_scale=w_scales[k % 2][:, g * P : (g + 1) * P],
+                        lhsT=w_codes[k % len(w_codes)][:, operand * P : (operand + 1) * P].bitcast(FP8X4),
+                        lhsT_scale=w_scales[k % len(w_scales)][:, operand * P : (operand + 1) * P],
                         rhs=rhs,
                         rhs_scale=rhs_scale,
-                        start=(g == 2),
-                        stop=(g == 1),
+                        start=(operand == OPERAND_ORDER[0]),
+                        stop=(operand == OPERAND_ORDER[-1]),
                     )
+
+        def activate(k, first, count, bank):
             nc.scalar.activation(
                 out=tanh_part(k, first, count), in_=bank[:, 0:count], func=ACT.Tanh, bias=bias[:, k : k + 1]
             )
 
+        def multiply(k):
+            for h in range(HALVES):
+                product(k, h * BANK, BANK, BANK, banks[h])
+                activate(k, h * BANK, BANK, banks[h])
+
+        def list_part(first, count):
+            return offsets[:, first // LIST_ROWS : (first + count) // LIST_ROWS]
+
         def gather_add(k, first, count):
-            part = offsets[:, first // LIST_ROWS : (first + count) // LIST_ROWS]
             nc.vector.tensor_tensor(
                 out=summed[k % 2][:, first : first + count],
-                in0=h_rows[k % 2][:].indirect(part),
+                in0=h_rows[k % 2][:].indirect(list_part(first, count)),
                 in1=tanh_part(k, first, count),
                 op=ALU.add,
             )
 
         def scatter(k, first, count):
             cols = slice(first, first + count)
-            part = offsets[:, first // LIST_ROWS : (first + count) // LIST_ROWS]
             nc.vector.tensor_tensor(
-                out=pages[k % 2][:].indirect(part), in0=summed[k % 2][:, cols], in1=weight[:, cols], op=ALU.mult
+                out=pages[k % 2][:].indirect(list_part(first, count)),
+                in0=summed[k % 2][:, cols],
+                in1=weight[:, cols],
+                op=ALU.mult,
             )
 
-        def turn(k, first_banks, first_copies):
-            turned = y_turned[k % 2]
-            for b in range(4):
-                bank = first_banks[b]
-                for g in range(CHUNKS):
+        def store_page(k):
+            nc.sync.dma_start(out=out_0[k * P : (k + 1) * P, :], in_=pages[k % 2][:])
+
+        def turn(k, by_block, copies):
+            for b in range(BLOCKS):
+                bank = by_block[b]
+                for g in range(GROUPS):
                     first = g * BANK + b * P
                     nc.tensor.transpose(bank[:, g * P : (g + 1) * P], pages[k % 2][:, first : first + P], ident[:])
-                first_copies[b](
-                    out=turned[:, b * BANK : (b + 1) * BANK].rearrange("p (u r e) -> p u r e", u=2, e=2),
+                copies[b](
+                    out=y_turned[k % 2][:, b * BANK : (b + 1) * BANK].rearrange("p (u r e) -> p u r e", u=2, e=2),
                     in_=bank[:].rearrange("p (r u e) -> p u r e", u=2, e=2),
                 )
 
-        def turn_back(k, second_banks, second_copies, pieces, queues):
-            a, w = divmod(k, 4)
+        def turn_back(k, used, copies, pieces, queues):
+            a, w = divmod(k, TILES_A_PASS)
             staged = y_bf[k % 2]
             words = y_turned[k % 2][:].bitcast(F32)
-            width = BANK // pieces
-            span = 4 // len(second_banks)
-            for i, bank in enumerate(second_banks):
+            span = BLOCKS // len(used)
+            for i, bank in enumerate(used):
                 for s in range(2 * span):
                     first = (2 * span * i + s) * P
                     nc.tensor.transpose(bank[:, s * P : (s + 1) * P], words[:, first : first + P], ident[:])
-                second_copies[i](
+                copies[i](
                     out=staged[:].bitcast(F32)[:, 2 * P * span * i : 2 * P * span * (i + 1)].rearrange(
                         "p (b c u) -> p b c u", b=span, u=2
                     ),
                     in_=bank[:, 0 : 2 * P * span].rearrange("p (b u c) -> p b c u", b=span, u=2),
                 )
+            width = BANK // pieces
             for piece in range(pieces):
-                cols = slice(piece * width, (piece + 1) * width)
+                first = piece * width
                 nc.vector.quantize_mx(
-                    out=y_codes[a][:, w * BANK + piece * width : w * BANK + (piece + 1) * width].bitcast(FP8X4),
-                    scales=y_scales[a][4 * w : P, cols],
-                    in_=staged[:, PACK * piece * width : PACK * (piece + 1) * width],
+                    out=y_codes[a][:, w * BANK + first : w * BANK + first + width].bitcast(FP8X4),
+                    scales=y_scales[a][SCALE_ROWS * w : P, first : first + width],
+                    in_=staged[:, PACK * first : PACK * (first + width)],
                 )
             if k in STORE_FROM:
-                held = slice(STORE_FROM[k] % 4, w + 1)
-                codes_out = out_1[a].rearrange("p t b -> p (t b)").bitcast(I32).rearrange("(w q) t -> q w t", q=32)
-                for g in range(CHUNKS):
-                    queues[g % 2].dma_start(
-                        out=codes_out[:, held, g * BANK : (g + 1) * BANK],
-                        in_=y_codes[a][32 * g : 32 * g + 32, :].rearrange("q (w c) -> q w c", w=4)[:, held, :],
-                    )
-            if w == 3:
-                for g in range(CHUNKS):
+                held = slice(STORE_FROM[k] % TILES_A_PASS, w + 1)
+                codes_out = out_1[a].rearrange("p t b -> p (t b)").bitcast(I32).rearrange("(w q) t -> q w t", q=QUADRANT)
+                for g in range(GROUPS):
+                    codes = y_codes[a][QUADRANT * g : QUADRANT * (g + 1), :].rearrange("q (w c) -> q w c", w=TILES_A_PASS)
+                    queues[g % 2].dma_start(out=codes_out[:, held, g * BANK : (g + 1) * BANK], in_=codes[:, held, :])
+            if w == TILES_A_PASS - 1:
+                for g in range(GROUPS):
                     queues[g % 2].dma_start(
                         out=out_2[a, :, g * BANK : (g + 1) * BANK].bitcast(I32),
-                        in_=y_scales[a][32 * g : 32 * g + 16, :].bitcast(I32),
+                        in_=y_scales[a][QUADRANT * g : QUADRANT * g + SCALE_ROWS * TILES_A_PASS, :].bitcast(I32),
                     )
 
         nc.vector.memset(tab_s[:].bitcast(I32), 0)
         nc.gpsimd.memset(bn_rows[:], 0.0)
         make_identity(nc, ident[:])
         nc.sync.dma_start(offsets[:], offs)
-        for q in range(4):
+        for quadrant in range(QUADRANTS):
             nc.sync.dma_start(
-                out=tab_s[32 * q : 32 * q + 4, :].bitcast(I32).rearrange("r (a t) -> r a t", a=2),
-                in_=tab_scales[:, 4 * q : 4 * q + 4, :].bitcast(I32).rearrange("a r t -> r a t"),
+                out=tab_s[QUADRANT * quadrant : QUADRANT * quadrant + SCALE_ROWS, :]
+                .bitcast(I32)
+                .rearrange("r (a t) -> r a t", a=PASSES),
+                in_=tab_scales[:, SCALE_ROWS * quadrant : SCALE_ROWS * (quadrant + 1), :]
+                .bitcast(I32)
+                .rearrange("a r t -> r a t"),
             )
         nc.sync.dma_start(out=tab_w[:], in_=tab_words[0].rearrange("p t b -> p (t b)").bitcast(I32))
         nc.sync.dma_start(out=bn_rows[0:TILES, :], in_=bn.rearrange("(i p) -> i p", p=P))
@@ -230,17 +264,18 @@ def tile_list_tgn_rnnP_kernel(
 
         nc.vector.tensor_copy(picked_w[:], tab_w[:].bitcast(U32).indirect(offsets[:]))
         nc.vector.tensor_copy(
-            out=parted_w[:].bitcast(U16).rearrange("p (d j) -> p d j", d=2),
-            in_=picked_w[:].bitcast(U16).rearrange("p (j d) -> p d j", d=2),
+            out=parted_w[:].bitcast(U16).rearrange("p (d j) -> p d j", d=PASSES),
+            in_=picked_w[:].bitcast(U16).rearrange("p (j d) -> p d j", d=PASSES),
         )
-        picked_s = keep.tile([P, 2 * J], U8, name="picked_s", tag="picked", align_bytes=64)
-        for a in range(2):
+        picked_s = keep.tile([P, PASSES * J], U8, name="picked_s", tag="picked", align_bytes=64)
+        for a in range(PASSES):
             nc.vector.tensor_copy(picked_s[:, a * J : (a + 1) * J], tab_s[:, a * T : (a + 1) * T].indirect(offsets[:]))
+
         nc.tensor.transpose(banks[2][:, 0:P], bn_rows[:], ident[:])
         nc.scalar.copy(out=bias[:], in_=banks[2][:, 0 : 2 * TILES])
         for h in range(HALVES):
-            for b in range(4):
-                column = TILES + 4 * h + b
+            for b in range(BLOCKS):
+                column = TILES + BLOCKS * h + b
                 nc.tensor.transpose(
                     banks[h][:, b * P : (b + 1) * P], bias[:, column : column + 1].to_broadcast([P, P]), ident[:]
                 )
@@ -248,48 +283,63 @@ def tile_list_tgn_rnnP_kernel(
 
         quantise_x(0)
         quantise_w(0, 4)
-        load_w(3)
         load_h(1)
-        for q in range(4):
-            if q < 3:
+        load_w(3)
+        for q in range(QUARTERS):
+            if q + 1 < QUARTERS:
                 quantise_x(q + 1)
             else:
                 quantise_w(1, 2)
-            multiply(0, q * QUARTER, QUARTER, P, banks[4 + q])
+            product(0, q * QUARTER, QUARTER, P, banks[4 + q])
+            activate(0, q * QUARTER, QUARTER, banks[4 + q])
             gather_add(0, q * QUARTER, QUARTER)
             scatter(0, q * QUARTER, QUARTER)
-        load_h(2)
         load_w(4)
-        nc.sync.dma_start(out=out_0[0:P, :], in_=pages[0][:])
+        load_h(2)
+        store_page(0)
 
-        copy_s, copy_v = nc.scalar.copy, nc.vector.tensor_copy
-        both_sync = (nc.sync, nc.sync)
-        quantise_w(2, 1)
-        for h in range(HALVES):
-            multiply(1, h * BANK, BANK, BANK, banks[h])
+        turning = banks[1::-1] * 2
+        quantise_w(2, 2)
+        multiply(1)
         gather_add(1, 0, J)
         load_h(3)
         load_w(5)
-        for p in range(1, TILES):
-            k = p + 1
+        scatter(1, 0, J)
+        store_page(1)
+        quantise_w(3, 1)
+        for h in range(HALVES):
+            product(2, h * BANK, BANK, BANK, banks[6 + h])
+        quantise_w(4, 1)
+        for h in range(HALVES):
+            activate(2, h * BANK, BANK, banks[6 + h])
+        gather_add(2, 0, J)
+        load_h(4)
+        turn(0, turning, [copy_s] * BLOCKS)
+        scatter(2, 0, J)
+        store_page(2)
+        multiply(3)
+        load_w(6)
+        gather_add(3, 0, J)
+        load_h(5)
+        load_w(7)
+
+        for k in range(3, TILES):
+            if k + 2 < TILES:
+                quantise_w(k + 2, 1)
+            turn_back(k - 3, banks[2:4], [copy_s] * 2, 1, both_sync)
             if k + 1 < TILES:
-                quantise_w(k + 1, 1)
-            if p >= 3:
-                turn_back(p - 3, banks[2:4], [copy_s] * 2, 1, both_sync)
-            if k < TILES:
-                for h in range(HALVES):
-                    multiply(k, h * BANK, BANK, BANK, banks[h])
-                gather_add(k, 0, J)
-                if k + 2 < TILES:
-                    load_h(k + 2)
-                if k + 4 < TILES:
-                    load_w(k + 4)
-            if p >= 2:
-                turn(p - 2, banks[1::-1] * 2, [copy_s] * 4)
-            scatter(p, 0, J)
-            nc.sync.dma_start(out=out_0[p * P : (p + 1) * P, :], in_=pages[p % 2][:])
-        turn_back(TILES - 3, banks[0:2], [copy_s] * 2, 1, both_sync)
-        turn(TILES - 2, banks[0:2] * 2, [copy_s] * 4)
-        turn_back(TILES - 2, banks[0:2] + banks[6:8], [copy_s] * 4, 1, both_sync)
-        turn(TILES - 1, banks[0:2] + banks[6:8], [copy_s, copy_v] * 2)
-        turn_back(TILES - 1, banks[2:6], [copy_s, copy_v, copy_s, copy_s], 4, (nc.sync, nc.scalar))
+                multiply(k + 1)
+                gather_add(k + 1, 0, J)
+            if k + 3 < TILES:
+                load_h(k + 3)
+            turn(k - 2, turning, [copy_s] * BLOCKS)
+            scatter(k, 0, J)
+            store_page(k)
+
+        last = TILES - 1
+        handed = banks[0:2] + banks[6:8]
+        turn_back(last - 2, banks[0:2], [copy_s] * 2, 1, both_sync)
+        turn(last - 1, banks[0:2] * 2, [copy_s] * BLOCKS)
+        turn_back(last - 1, handed, [copy_s] * BLOCKS, 1, both_sync)
+        turn(last, handed, [copy_s, copy_v] * 2)
+        turn_back(last, banks[2:6], [copy_s, copy_v, copy_s, copy_s], BLOCKS, (nc.sync, nc.scalar))

@@ -35,7 +35,7 @@ QUARTERS = 4
 QUARTER = J // QUARTERS
 RUN = 4
 OPERAND_ORDER = (2, 3, 0, 1)
-STORE_FROM = {3: 0, 4: 4, 6: 5, 7: 7}
+STORE_FROM = {3: 0, 4: 4, 5: 5, 6: 6, 7: 7}
 
 
 def tile_list_tgn_rnnP_kernel(
@@ -59,11 +59,11 @@ def tile_list_tgn_rnnP_kernel(
         bias = keep.tile([P, 2 * TILES], F32, name="bias", align_bytes=64)
         weight = keep.tile([P, J], F32, name="weight", align_bytes=64)
         x_raw = tiles(QUARTERS * PASSES, [P, PACK * QUARTER], F32, "x_raw")
-        x_bf = tiles(3, [P, PACK * QUARTER], BF16, "x_bf")
+        x_bf = tiles(4, [P, PACK * QUARTER], BF16, "x_bf")
         x_codes = tiles(PASSES, [P, J], U32, "x_codes")
         x_scales = tiles(PASSES, [P, J], U8, "x_scales")
         w_raw = tiles(3, [P, PACK * BANK], F32, "w_raw")
-        w_bf = tiles(2, [P, PACK * BANK], BF16, "w_bf")
+        w_bf = keep.tile([P, PACK * BANK], BF16, name="w_bf", align_bytes=64)
         w_codes = tiles(3, [P, BANK], U32, "w_codes")
         w_scales = tiles(3, [P, BANK], U8, "w_scales")
         h_rows = tiles(2, [P, T], F32, "h_rows")
@@ -89,8 +89,13 @@ def tile_list_tgn_rnnP_kernel(
                 in_=src.rearrange("p t (c i) -> p c t i", i=RUN),
             )
 
-        def load_x(q):
-            for a in range(PASSES):
+        def head_buffer(step, role):
+            if step == 0:
+                return x_bf[role]
+            return x_bf[(2, 3, 0)[(step - 1 + role) % 3]]
+
+        def load_x(q, which):
+            for a in which:
                 nc.sync.dma_start(
                     out=by_row(x_raw[PASSES * q + a][:]), in_=pass_rows(x, a, slice(q * QUARTER, (q + 1) * QUARTER))
                 )
@@ -98,7 +103,7 @@ def tile_list_tgn_rnnP_kernel(
         def quantise_x(q):
             cols = slice(q * QUARTER, (q + 1) * QUARTER)
             for a in range(PASSES):
-                staged = x_bf[(PASSES * q + a) % len(x_bf)]
+                staged = head_buffer(q, a)
                 interleave(staged[:], by_row(x_raw[PASSES * q + a][:]))
                 nc.vector.quantize_mx(out=x_codes[a][:, cols].bitcast(FP8X4), scales=x_scales[a][:, cols], in_=staged[:])
 
@@ -117,7 +122,11 @@ def tile_list_tgn_rnnP_kernel(
             for step in range(pieces):
                 piece = (step + pieces // 2) % pieces
                 cols = slice(piece * width, (piece + 1) * width)
-                staged = w_bf[k % 2][:, PACK * piece * width : PACK * (piece + 1) * width]
+                if k == 1:
+                    staged = head_buffer(QUARTERS, step)[:]
+                else:
+                    whole = w_bf if k < TILES_A_PASS else y_turned[k % 2]
+                    staged = whole[:, PACK * piece * width : PACK * (piece + 1) * width]
                 interleave(staged, raw[:, :, cols])
                 nc.vector.quantize_mx(
                     out=w_codes[k % len(w_codes)][:, cols].bitcast(FP8X4),
@@ -129,31 +138,35 @@ def tile_list_tgn_rnnP_kernel(
             nc.sync.dma_start(out=h_rows[k % 2][:], in_=hT[k * P : (k + 1) * P, :])
 
         def tanh_part(k, first, count):
-            if k == 0 and first < J - QUARTER:
-                return x_raw[PASSES * (first // QUARTER + 1) + 1][:, 0:count]
-            later = 4 if k == 2 else k + 1
-            return w_raw[later % len(w_raw)][:, first : first + count]
+            if k == 0:
+                return head_buffer(first // QUARTER + 1, 2)[:].bitcast(F32)[:, 0:count]
+            if k == 1 and first < BANK:
+                return w_bf[:].bitcast(F32)[:, first : first + count]
+            return w_raw[(k + 1) % len(w_raw)][:, first : first + count]
 
-        def product(k, first, count, width, bank):
-            for start in range(first, first + count, width):
-                cols = slice(start, start + width)
-                for operand in OPERAND_ORDER:
-                    a = operand % PASSES
-                    if operand < PASSES:
-                        rhs = x_codes[a][:, cols].bitcast(FP8X4)
-                        rhs_scale = x_scales[a][:, cols]
-                    else:
-                        rhs = parted_w[:, 2 * (a * J + start) : 2 * (a * J + start + width)].bitcast(FP4X4)
-                        rhs_scale = picked_s[:, a * J + start : a * J + start + width]
-                    nc.tensor.matmul_mx(
-                        out=bank[:, start - first : start - first + width],
-                        lhsT=w_codes[k % len(w_codes)][:, operand * P : (operand + 1) * P].bitcast(FP8X4),
-                        lhsT_scale=w_scales[k % len(w_scales)][:, operand * P : (operand + 1) * P],
-                        rhs=rhs,
-                        rhs_scale=rhs_scale,
-                        start=(operand == OPERAND_ORDER[0]),
-                        stop=(operand == OPERAND_ORDER[-1]),
-                    )
+        def product(k, first, count, bank):
+            passes = []
+            for operand in OPERAND_ORDER:
+                width = P if operand >= PASSES and count < BANK else count
+                passes.extend((operand, start, width) for start in range(first, first + count, width))
+            for i, (operand, start, width) in enumerate(passes):
+                a = operand % PASSES
+                if operand < PASSES:
+                    rhs = x_codes[a][:, start : start + width].bitcast(FP8X4)
+                    rhs_scale = x_scales[a][:, start : start + width]
+                else:
+                    rhs = parted_w[:, 2 * (a * J + start) : 2 * (a * J + start + width)].bitcast(FP4X4)
+                    half, inside = divmod(start, BANK)
+                    rhs_scale = picked_s[half][:, a * BANK + inside : a * BANK + inside + width]
+                nc.tensor.matmul_mx(
+                    out=bank[:, start - first : start - first + width],
+                    lhsT=w_codes[k % len(w_codes)][:, operand * P : (operand + 1) * P].bitcast(FP8X4),
+                    lhsT_scale=w_scales[k % len(w_scales)][:, operand * P : (operand + 1) * P],
+                    rhs=rhs,
+                    rhs_scale=rhs_scale,
+                    start=(i == 0),
+                    stop=(i == len(passes) - 1),
+                )
 
         def activate(k, first, count, bank):
             nc.scalar.activation(
@@ -162,15 +175,22 @@ def tile_list_tgn_rnnP_kernel(
 
         def multiply(k):
             for h in range(HALVES):
-                product(k, h * BANK, BANK, BANK, banks[h])
+                product(k, h * BANK, BANK, banks[h])
                 activate(k, h * BANK, BANK, banks[h])
 
         def list_part(first, count):
             return offsets[:, first // LIST_ROWS : (first + count) // LIST_ROWS]
 
+        def sum_part(k, first, count):
+            if k == 0 and first < J - QUARTER:
+                return x_raw[PASSES * (first // QUARTER + 1) + 1][:, 0:count]
+            if k == 0:
+                return w_raw[1][:, 0:count]
+            return summed[k % 2][:, first : first + count]
+
         def gather_add(k, first, count):
             nc.vector.tensor_tensor(
-                out=summed[k % 2][:, first : first + count],
+                out=sum_part(k, first, count),
                 in0=h_rows[k % 2][:].indirect(list_part(first, count)),
                 in1=tanh_part(k, first, count),
                 op=ALU.add,
@@ -180,7 +200,7 @@ def tile_list_tgn_rnnP_kernel(
             cols = slice(first, first + count)
             nc.vector.tensor_tensor(
                 out=pages[k % 2][:].indirect(list_part(first, count)),
-                in0=summed[k % 2][:, cols],
+                in0=sum_part(k, first, count),
                 in1=weight[:, cols],
                 op=ALU.mult,
             )
@@ -225,17 +245,17 @@ def tile_list_tgn_rnnP_kernel(
             if k in STORE_FROM:
                 held = slice(STORE_FROM[k] % TILES_A_PASS, w + 1)
                 codes_out = out_1[a].rearrange("p t b -> p (t b)").bitcast(I32).rearrange("(w q) t -> q w t", q=QUADRANT)
-                for g in range(GROUPS):
+                for g in (0, 2, 1, 3):
                     codes = y_codes[a][QUADRANT * g : QUADRANT * (g + 1), :].rearrange("q (w c) -> q w c", w=TILES_A_PASS)
-                    queues[g % 2].dma_start(out=codes_out[:, held, g * BANK : (g + 1) * BANK], in_=codes[:, held, :])
+                    queues[g // 2].dma_start(out=codes_out[:, held, g * BANK : (g + 1) * BANK], in_=codes[:, held, :])
             if w == TILES_A_PASS - 1:
                 for g in range(GROUPS):
-                    queues[g % 2].dma_start(
+                    queues[g // 2].dma_start(
                         out=out_2[a, :, g * BANK : (g + 1) * BANK].bitcast(I32),
                         in_=y_scales[a][QUADRANT * g : QUADRANT * g + SCALE_ROWS * TILES_A_PASS, :].bitcast(I32),
                     )
 
-        nc.vector.memset(tab_s[:].bitcast(I32), 0)
+        nc.gpsimd.memset(tab_s[:].bitcast(I32), 0)
         nc.gpsimd.memset(bn_rows[:], 0.0)
         make_identity(nc, ident[:])
         nc.sync.dma_start(offsets[:], offs)
@@ -248,18 +268,21 @@ def tile_list_tgn_rnnP_kernel(
                 .bitcast(I32)
                 .rearrange("a r t -> r a t"),
             )
-        nc.sync.dma_start(out=tab_w[:], in_=tab_words[0].rearrange("p t b -> p (t b)").bitcast(I32))
+        table = tab_words[0].rearrange("p t b -> p (t b)").bitcast(I32)
+        nc.sync.dma_start(out=tab_w[:], in_=table)
         nc.sync.dma_start(out=bn_rows[0:TILES, :], in_=bn.rearrange("(i p) -> i p", p=P))
         nc.sync.dma_start(out=bn_rows[TILES : 2 * TILES, :], in_=wgo[0].rearrange("(i p) -> i p", p=P))
-        for page in pages:
-            nc.vector.memset(page[:], 0.0)
-        load_x(0)
+        nc.vector.memset(pages[0][:], 0.0)
+        nc.gpsimd.memset(pages[1][:], 0.0)
+        load_x(0, [0])
         load_w(0)
-        load_x(1)
+        load_x(0, [1])
+        load_x(1, range(PASSES))
         load_h(0)
-        load_x(2)
-        load_x(3)
+        load_x(2, range(PASSES))
+        load_x(3, range(PASSES))
         load_w(1)
+        load_h(1)
         load_w(2)
 
         nc.vector.tensor_copy(picked_w[:], tab_w[:].bitcast(U32).indirect(offsets[:]))
@@ -267,9 +290,17 @@ def tile_list_tgn_rnnP_kernel(
             out=parted_w[:].bitcast(U16).rearrange("p (d j) -> p d j", d=PASSES),
             in_=picked_w[:].bitcast(U16).rearrange("p (j d) -> p d j", d=PASSES),
         )
-        picked_s = keep.tile([P, PASSES * J], U8, name="picked_s", tag="picked", align_bytes=64)
-        for a in range(PASSES):
-            nc.vector.tensor_copy(picked_s[:, a * J : (a + 1) * J], tab_s[:, a * T : (a + 1) * T].indirect(offsets[:]))
+        picked_s = []
+
+        def gather_scales(half, tag):
+            picked_s.append(keep.tile([P, PASSES * BANK], U8, name="picked_s" + str(half), tag=tag, align_bytes=64))
+            for a in range(PASSES):
+                nc.vector.tensor_copy(
+                    picked_s[half][:, a * BANK : (a + 1) * BANK],
+                    tab_s[:, a * T : (a + 1) * T].indirect(list_part(half * BANK, BANK)),
+                )
+
+        gather_scales(0, "picked_s0")
 
         nc.tensor.transpose(banks[2][:, 0:P], bn_rows[:], ident[:])
         nc.scalar.copy(out=bias[:], in_=banks[2][:, 0 : 2 * TILES])
@@ -281,65 +312,53 @@ def tile_list_tgn_rnnP_kernel(
                 )
             nc.scalar.copy(out=weight[:, h * BANK : (h + 1) * BANK], in_=banks[h][:])
 
+        quantise_w(0, 2)
         quantise_x(0)
-        quantise_w(0, 4)
-        load_h(1)
+        gather_scales(1, "x_bf1")
         load_w(3)
         for q in range(QUARTERS):
             if q + 1 < QUARTERS:
                 quantise_x(q + 1)
             else:
                 quantise_w(1, 2)
-            product(0, q * QUARTER, QUARTER, P, banks[4 + q])
-            activate(0, q * QUARTER, QUARTER, banks[4 + q])
+            product(0, q * QUARTER, QUARTER, banks[4 + q % 2])
+            activate(0, q * QUARTER, QUARTER, banks[4 + q % 2])
             gather_add(0, q * QUARTER, QUARTER)
             scatter(0, q * QUARTER, QUARTER)
-        load_w(4)
         load_h(2)
         store_page(0)
+        load_w(4)
 
-        turning = banks[1::-1] * 2
-        quantise_w(2, 2)
-        multiply(1)
-        gather_add(1, 0, J)
+        turning = banks[0:2] * 2
+        for q in range(2):
+            product(1, q * QUARTER, QUARTER, banks[q])
+            activate(1, q * QUARTER, QUARTER, banks[q])
+            gather_add(1, q * QUARTER, QUARTER)
+        scatter(1, 0, BANK)
+        product(1, BANK, BANK, banks[1])
+        quantise_w(2, 1)
+        activate(1, BANK, BANK, banks[1])
+        gather_add(1, BANK, BANK)
+        scatter(1, BANK, BANK)
+        turn(0, banks[4:8], [copy_s] * BLOCKS)
         load_h(3)
-        load_w(5)
-        scatter(1, 0, J)
         store_page(1)
-        quantise_w(3, 1)
-        for h in range(HALVES):
-            product(2, h * BANK, BANK, BANK, banks[6 + h])
-        quantise_w(4, 1)
-        for h in range(HALVES):
-            activate(2, h * BANK, BANK, banks[6 + h])
-        gather_add(2, 0, J)
-        load_h(4)
-        turn(0, turning, [copy_s] * BLOCKS)
-        scatter(2, 0, J)
-        store_page(2)
-        multiply(3)
-        load_w(6)
-        gather_add(3, 0, J)
-        load_h(5)
-        load_w(7)
 
-        for k in range(3, TILES):
-            if k + 2 < TILES:
-                quantise_w(k + 2, 1)
-            turn_back(k - 3, banks[2:4], [copy_s] * 2, 1, both_sync)
+        for k in range(2, TILES):
             if k + 1 < TILES:
-                multiply(k + 1)
-                gather_add(k + 1, 0, J)
+                quantise_w(k + 1, 1)
+            multiply(k)
+            gather_add(k, 0, J)
             if k + 3 < TILES:
-                load_h(k + 3)
-            turn(k - 2, turning, [copy_s] * BLOCKS)
+                load_w(k + 3)
+            if k + 2 < TILES:
+                load_h(k + 2)
+            turn_back(k - 2, banks[0:2], [copy_s] * 2, 2, both_sync)
             scatter(k, 0, J)
+            turn(k - 1, turning, [copy_s] * BLOCKS)
             store_page(k)
-
         last = TILES - 1
         handed = banks[0:2] + banks[6:8]
-        turn_back(last - 2, banks[0:2], [copy_s] * 2, 1, both_sync)
-        turn(last - 1, banks[0:2] * 2, [copy_s] * BLOCKS)
         turn_back(last - 1, handed, [copy_s] * BLOCKS, 1, both_sync)
         turn(last, handed, [copy_s, copy_v] * 2)
         turn_back(last, banks[2:6], [copy_s, copy_v, copy_s, copy_s], BLOCKS, (nc.sync, nc.scalar))

@@ -35,7 +35,7 @@ QUARTERS = 4
 QUARTER = J // QUARTERS
 RUN = 4
 OPERAND_ORDER = (2, 3, 0, 1)
-STORE_FROM = {3: 0, 4: 4, 5: 5, 6: 6, 7: 7}
+STORE_FROM = {1: 0, 3: 2, 4: 4, 6: 5, 7: 7}
 
 
 def tile_list_tgn_rnnP_kernel(
@@ -69,8 +69,8 @@ def tile_list_tgn_rnnP_kernel(
         h_rows = tiles(2, [P, T], F32, "h_rows")
         summed = tiles(2, [P, J], F32, "summed")
         pages = tiles(2, [P, T], F32, "pages")
-        y_turned = tiles(2, [P, T], BF16, "y_turned")
-        y_bf = tiles(2, [P, T], BF16, "y_bf")
+        last_turned = tiles(2, [P, T], BF16, "last_turned")
+        y_bf = tiles(3, [P, T], BF16, "y_bf")
         y_codes = tiles(PASSES, [P, TILES_A_PASS * BANK], I32, "y_codes")
         y_scales = tiles(PASSES, [P, BANK], U8, "y_scales")
         banks = [psum.tile([P, BANK], F32, name="bank" + str(i)) for i in range(8)]
@@ -125,8 +125,7 @@ def tile_list_tgn_rnnP_kernel(
                 if k == 1:
                     staged = head_buffer(QUARTERS, step)[:]
                 else:
-                    whole = w_bf if k < TILES_A_PASS else y_turned[k % 2]
-                    staged = whole[:, PACK * piece * width : PACK * (piece + 1) * width]
+                    staged = w_bf[:, PACK * piece * width : PACK * (piece + 1) * width]
                 interleave(staged, raw[:, :, cols])
                 nc.vector.quantize_mx(
                     out=w_codes[k % len(w_codes)][:, cols].bitcast(FP8X4),
@@ -143,6 +142,13 @@ def tile_list_tgn_rnnP_kernel(
             if k == 1 and first < BANK:
                 return w_bf[:].bitcast(F32)[:, first : first + count]
             return w_raw[(k + 1) % len(w_raw)][:, first : first + count]
+
+        def turned(k):
+            if 0 < k < TILES - 3:
+                return w_raw[k % len(w_raw)][:, J : 2 * J].bitcast(BF16)
+            if k + 3 == TILES:
+                return w_bf[:]
+            return last_turned[k % 2][:]
 
         def product(k, first, count, bank):
             passes = []
@@ -215,14 +221,13 @@ def tile_list_tgn_rnnP_kernel(
                     first = g * BANK + b * P
                     nc.tensor.transpose(bank[:, g * P : (g + 1) * P], pages[k % 2][:, first : first + P], ident[:])
                 copies[b](
-                    out=y_turned[k % 2][:, b * BANK : (b + 1) * BANK].rearrange("p (u r e) -> p u r e", u=2, e=2),
+                    out=turned(k)[:, b * BANK : (b + 1) * BANK].rearrange("p (u r e) -> p u r e", u=2, e=2),
                     in_=bank[:].rearrange("p (r u e) -> p u r e", u=2, e=2),
                 )
 
-        def turn_back(k, used, copies, pieces, queues):
-            a, w = divmod(k, TILES_A_PASS)
-            staged = y_bf[k % 2]
-            words = y_turned[k % 2][:].bitcast(F32)
+        def turn_words(k, used, copies):
+            staged = y_bf[k % len(y_bf)]
+            words = turned(k).bitcast(F32)
             span = BLOCKS // len(used)
             for i, bank in enumerate(used):
                 for s in range(2 * span):
@@ -234,14 +239,24 @@ def tile_list_tgn_rnnP_kernel(
                     ),
                     in_=bank[:, 0 : 2 * P * span].rearrange("p (b u c) -> p b c u", b=span, u=2),
                 )
+
+        def turn_back(k, used, copies, pieces, queues):
+            turn_words(k, used, copies)
+            quantise_y(k, pieces, queues, range(pieces))
+
+        def quantise_y(k, pieces, queues, which):
+            a, w = divmod(k, TILES_A_PASS)
+            staged = y_bf[k % len(y_bf)]
             width = BANK // pieces
-            for piece in range(pieces):
+            for piece in which:
                 first = piece * width
                 nc.vector.quantize_mx(
                     out=y_codes[a][:, w * BANK + first : w * BANK + first + width].bitcast(FP8X4),
                     scales=y_scales[a][SCALE_ROWS * w : P, first : first + width],
                     in_=staged[:, PACK * first : PACK * (first + width)],
                 )
+            if piece + 1 < pieces:
+                return
             if k in STORE_FROM:
                 held = slice(STORE_FROM[k] % TILES_A_PASS, w + 1)
                 codes_out = out_1[a].rearrange("p t b -> p (t b)").bitcast(I32).rearrange("(w q) t -> q w t", q=QUADRANT)
@@ -258,6 +273,8 @@ def tile_list_tgn_rnnP_kernel(
         nc.gpsimd.memset(tab_s[:].bitcast(I32), 0)
         nc.gpsimd.memset(bn_rows[:], 0.0)
         make_identity(nc, ident[:])
+        warm = keep.tile([P, 8], F32, name="warm")
+        nc.scalar.activation(out=warm[:, 0:1], in_=ident[:, 0:1], func=ACT.Tanh)
         nc.sync.dma_start(offsets[:], offs)
         for quadrant in range(QUADRANTS):
             nc.sync.dma_start(
@@ -341,24 +358,28 @@ def tile_list_tgn_rnnP_kernel(
         gather_add(1, BANK, BANK)
         scatter(1, BANK, BANK)
         turn(0, banks[4:8], [copy_s] * BLOCKS)
+        load_w(5)
         load_h(3)
         store_page(1)
 
+        last = TILES - 1
         for k in range(2, TILES):
-            if k + 1 < TILES:
+            if k < last:
                 quantise_w(k + 1, 1)
             multiply(k)
             gather_add(k, 0, J)
-            if k + 3 < TILES:
-                load_w(k + 3)
             if k + 2 < TILES:
                 load_h(k + 2)
-            turn_back(k - 2, banks[0:2], [copy_s] * 2, 2, both_sync)
+            if k >= 3:
+                turn_back(k - 3, banks[0:2], [copy_s] * 2, 2, both_sync)
+                turn(k - 2, banks[4:8], [copy_s] * BLOCKS)
+            if k in (2, 4):
+                load_w(6 if k == 2 else 7)
             scatter(k, 0, J)
-            turn(k - 1, turning, [copy_s] * BLOCKS)
             store_page(k)
-        last = TILES - 1
         handed = banks[0:2] + banks[6:8]
-        turn_back(last - 1, handed, [copy_s] * BLOCKS, 1, both_sync)
+        turn_back(last - 2, banks[0:2], [copy_s] * 2, 1, both_sync)
+        turn(last - 1, turning, [copy_s] * BLOCKS)
+        turn_back(last - 1, handed, [copy_s] * BLOCKS, BLOCKS, both_sync)
         turn(last, handed, [copy_s, copy_v] * 2)
         turn_back(last, banks[2:6], [copy_s, copy_v, copy_s, copy_s], BLOCKS, (nc.sync, nc.scalar))

@@ -140,7 +140,8 @@ def tile_list_tgn_rnnP_kernel(
             if k == 0:
                 return head_buffer(first // QUARTER + 1, 2)[:].bitcast(F32)[:, 0:count]
             if k == 1 and first < BANK:
-                return w_bf[:].bitcast(F32)[:, first : first + count]
+                place = BANK if first == 0 else 0
+                return w_bf[:].bitcast(F32)[:, place : place + count]
             return w_raw[(k + 1) % len(w_raw)][:, first : first + count]
 
         def turned(k):
@@ -276,14 +277,10 @@ def tile_list_tgn_rnnP_kernel(
         warm = keep.tile([P, 8], F32, name="warm")
         nc.scalar.activation(out=warm[:, 0:1], in_=ident[:, 0:1], func=ACT.Tanh)
         nc.sync.dma_start(offsets[:], offs)
-        for quadrant in range(QUADRANTS):
+        for row in range(SCALE_ROWS):
             nc.sync.dma_start(
-                out=tab_s[QUADRANT * quadrant : QUADRANT * quadrant + SCALE_ROWS, :]
-                .bitcast(I32)
-                .rearrange("r (a t) -> r a t", a=PASSES),
-                in_=tab_scales[:, SCALE_ROWS * quadrant : SCALE_ROWS * (quadrant + 1), :]
-                .bitcast(I32)
-                .rearrange("a r t -> r a t"),
+                out=tab_s[row:P:QUADRANT, :].bitcast(I32).rearrange("q (a t) -> q a t", a=PASSES),
+                in_=tab_scales[:, row : QUADRANTS * SCALE_ROWS : SCALE_ROWS, :].bitcast(I32).rearrange("a q t -> q a t"),
             )
         table = tab_words[0].rearrange("p t b -> p (t b)").bitcast(I32)
         nc.sync.dma_start(out=tab_w[:], in_=table)
@@ -353,7 +350,7 @@ def tile_list_tgn_rnnP_kernel(
             gather_add(1, q * QUARTER, QUARTER)
         scatter(1, 0, BANK)
         product(1, BANK, BANK, banks[1])
-        quantise_w(2, 1)
+        quantise_w(2, 2)
         activate(1, BANK, BANK, banks[1])
         gather_add(1, BANK, BANK)
         scatter(1, BANK, BANK)
@@ -372,7 +369,7 @@ def tile_list_tgn_rnnP_kernel(
                 load_h(k + 2)
             if k >= 3:
                 turn_back(k - 3, banks[0:2], [copy_s] * 2, 2, both_sync)
-                turn(k - 2, banks[4:8], [copy_s] * BLOCKS)
+                turn(k - 2, banks[4:8] if k < last else banks[4:7] + banks[1:2], [copy_s] * BLOCKS)
             if k in (2, 4):
                 load_w(6 if k == 2 else 7)
             scatter(k, 0, J)

@@ -33,9 +33,10 @@ SCALE_ROWS = 4
 LIST_ROWS = 16
 QUARTERS = 4
 QUARTER = J // QUARTERS
+WARM_PASSES = 6
 RUN = 4
 OPERAND_ORDER = (2, 3, 0, 1)
-STORE_FROM = {1: 0, 3: 2, 4: 4, 6: 5, 7: 7}
+STORE_FROM = {1: 0, 3: 2, 4: 4, 5: 5, 6: 6, 7: 7}
 
 
 def tile_list_tgn_rnnP_kernel(
@@ -193,6 +194,8 @@ def tile_list_tgn_rnnP_kernel(
                 return x_raw[PASSES * (first // QUARTER + 1) + 1][:, 0:count]
             if k == 0:
                 return w_raw[1][:, 0:count]
+            if k == TILES - 1:
+                return w_bf[:].bitcast(F32)[:, first : first + count]
             return summed[k % 2][:, first : first + count]
 
         def gather_add(k, first, count):
@@ -226,8 +229,13 @@ def tile_list_tgn_rnnP_kernel(
                     in_=bank[:].rearrange("p (r u e) -> p u r e", u=2, e=2),
                 )
 
+        def staged_y(k, first, count):
+            if k == TILES - 2:
+                freed = w_bf[:] if first < J else weight[:].bitcast(BF16)
+                return freed[:, first % J : first % J + count]
+            return y_bf[k % len(y_bf)][:, first : first + count]
+
         def turn_words(k, used, copies):
-            staged = y_bf[k % len(y_bf)]
             words = turned(k).bitcast(F32)
             span = BLOCKS // len(used)
             for i, bank in enumerate(used):
@@ -235,7 +243,7 @@ def tile_list_tgn_rnnP_kernel(
                     first = (2 * span * i + s) * P
                     nc.tensor.transpose(bank[:, s * P : (s + 1) * P], words[:, first : first + P], ident[:])
                 copies[i](
-                    out=staged[:].bitcast(F32)[:, 2 * P * span * i : 2 * P * span * (i + 1)].rearrange(
+                    out=staged_y(k, BANK * span * i, BANK * span).bitcast(F32).rearrange(
                         "p (b c u) -> p b c u", b=span, u=2
                     ),
                     in_=bank[:, 0 : 2 * P * span].rearrange("p (b u c) -> p b c u", b=span, u=2),
@@ -247,14 +255,13 @@ def tile_list_tgn_rnnP_kernel(
 
         def quantise_y(k, pieces, queues, which):
             a, w = divmod(k, TILES_A_PASS)
-            staged = y_bf[k % len(y_bf)]
             width = BANK // pieces
             for piece in which:
                 first = piece * width
                 nc.vector.quantize_mx(
                     out=y_codes[a][:, w * BANK + first : w * BANK + first + width].bitcast(FP8X4),
                     scales=y_scales[a][SCALE_ROWS * w : P, first : first + width],
-                    in_=staged[:, PACK * first : PACK * (first + width)],
+                    in_=staged_y(k, PACK * first, PACK * width),
                 )
             if piece + 1 < pieces:
                 return
@@ -286,8 +293,8 @@ def tile_list_tgn_rnnP_kernel(
         nc.sync.dma_start(out=tab_w[:], in_=table)
         nc.sync.dma_start(out=bn_rows[0:TILES, :], in_=bn.rearrange("(i p) -> i p", p=P))
         nc.sync.dma_start(out=bn_rows[TILES : 2 * TILES, :], in_=wgo[0].rearrange("(i p) -> i p", p=P))
-        nc.vector.memset(pages[0][:], 0.0)
-        nc.gpsimd.memset(pages[1][:], 0.0)
+        for page in pages:
+            nc.vector.memset(page[:], 0.0)
         load_x(0, [0])
         load_w(0)
         load_x(0, [1])
@@ -360,23 +367,41 @@ def tile_list_tgn_rnnP_kernel(
         store_page(1)
 
         last = TILES - 1
-        for k in range(2, TILES):
-            if k < last:
-                quantise_w(k + 1, 1)
+        for k in range(2, last):
+            quantise_w(k + 1, 1)
             multiply(k)
             gather_add(k, 0, J)
             if k + 2 < TILES:
                 load_h(k + 2)
             if k >= 3:
                 turn_back(k - 3, banks[0:2], [copy_s] * 2, 2, both_sync)
-                turn(k - 2, banks[4:8] if k < last else banks[4:7] + banks[1:2], [copy_s] * BLOCKS)
+                turn(k - 2, banks[4:8], [copy_s] * BLOCKS)
             if k in (2, 4):
                 load_w(6 if k == 2 else 7)
             scatter(k, 0, J)
             store_page(k)
+        turn_back(last - 3, banks[2:4], [copy_s] * 2, 1, both_sync)
+        multiply(last)
+        turn(last - 2, banks[4:8], [copy_s] * BLOCKS)
+        turn_words(last - 2, banks[0:2], [copy_s] * 2)
+        gather_add(last, 0, J)
+        for h in range(HALVES):
+            quantise_y(last - 2, HALVES, both_sync, [h])
+            scatter(last, h * BANK, BANK)
+        store_page(last)
         handed = banks[0:2] + banks[6:8]
-        turn_back(last - 2, banks[0:2], [copy_s] * 2, 1, both_sync)
         turn(last - 1, turning, [copy_s] * BLOCKS)
-        turn_back(last - 1, handed, [copy_s] * BLOCKS, BLOCKS, both_sync)
+        turn_words(last - 1, handed, [copy_s] * BLOCKS)
+        for i in range(WARM_PASSES):
+            nc.tensor.matmul_mx(
+                out=handed[i // 2][:],
+                lhsT=w_codes[last % len(w_codes)][:, 0:P].bitcast(FP8X4),
+                lhsT_scale=w_scales[last % len(w_scales)][:, 0:P],
+                rhs=x_codes[0][:, 0:BANK].bitcast(FP8X4),
+                rhs_scale=x_scales[0][:, 0:BANK],
+                start=True,
+                stop=True,
+            )
+        quantise_y(last - 1, BLOCKS, both_sync, range(BLOCKS))
         turn(last, handed, [copy_s, copy_v] * 2)
         turn_back(last, banks[2:6], [copy_s, copy_v, copy_s, copy_s], BLOCKS, (nc.sync, nc.scalar))

@@ -34,6 +34,7 @@ LIST_ROWS = 16
 QUARTERS = 4
 QUARTER = J // QUARTERS
 WARM_PASSES = 6
+RAW_START = 640
 RUN = 4
 OPERAND_ORDER = (2, 3, 0, 1)
 STORE_FROM = {1: 0, 3: 2, 4: 4, 5: 5, 6: 6, 7: 7}
@@ -63,7 +64,8 @@ def tile_list_tgn_rnnP_kernel(
         x_bf = tiles(4, [P, PACK * QUARTER], BF16, "x_bf")
         x_codes = tiles(PASSES, [P, J], U32, "x_codes")
         x_scales = tiles(PASSES, [P, J], U8, "x_scales")
-        w_raw = tiles(3, [P, PACK * BANK], F32, "w_raw")
+        slots = tiles(3, [P, 3 * J], F32, "slots")
+        w_raw = [slot[:, RAW_START : RAW_START + PACK * BANK] for slot in slots]
         w_bf = keep.tile([P, PACK * BANK], BF16, name="w_bf", align_bytes=64)
         w_codes = tiles(3, [P, BANK], U32, "w_codes")
         w_scales = tiles(3, [P, BANK], U8, "w_scales")
@@ -71,7 +73,7 @@ def tile_list_tgn_rnnP_kernel(
         summed = tiles(2, [P, J], F32, "summed")
         pages = tiles(2, [P, T], F32, "pages")
         last_turned = tiles(2, [P, T], BF16, "last_turned")
-        y_bf = tiles(3, [P, T], BF16, "y_bf")
+        y_bf = tiles(2, [P, T], BF16, "y_bf")
         y_codes = tiles(PASSES, [P, TILES_A_PASS * BANK], I32, "y_codes")
         y_scales = tiles(PASSES, [P, BANK], U8, "y_scales")
         banks = [psum.tile([P, BANK], F32, name="bank" + str(i)) for i in range(8)]
@@ -93,7 +95,9 @@ def tile_list_tgn_rnnP_kernel(
         def head_buffer(step, role):
             if step == 0:
                 return x_bf[role]
-            return x_bf[(2, 3, 0)[(step - 1 + role) % 3]]
+            if role == 0:
+                return x_bf[2]
+            return x_bf[3 if (step + role) % 2 == 0 else 0]
 
         def load_x(q, which):
             for a in which:
@@ -101,15 +105,17 @@ def tile_list_tgn_rnnP_kernel(
                     out=by_row(x_raw[PASSES * q + a][:]), in_=pass_rows(x, a, slice(q * QUARTER, (q + 1) * QUARTER))
                 )
 
-        def quantise_x(q):
+        def round_x(q, a):
+            interleave(head_buffer(q, a)[:], by_row(x_raw[PASSES * q + a][:]))
+
+        def quantise_x(q, a):
             cols = slice(q * QUARTER, (q + 1) * QUARTER)
-            for a in range(PASSES):
-                staged = head_buffer(q, a)
-                interleave(staged[:], by_row(x_raw[PASSES * q + a][:]))
-                nc.vector.quantize_mx(out=x_codes[a][:, cols].bitcast(FP8X4), scales=x_scales[a][:, cols], in_=staged[:])
+            nc.vector.quantize_mx(
+                out=x_codes[a][:, cols].bitcast(FP8X4), scales=x_scales[a][:, cols], in_=head_buffer(q, a)[:]
+            )
 
         def load_w(k):
-            raw = by_row(w_raw[k % len(w_raw)][:])
+            raw = by_row(w_raw[k % len(w_raw)])
             for operand in OPERAND_ORDER:
                 source = (wn, un)[operand // PASSES]
                 nc.sync.dma_start(
@@ -117,22 +123,24 @@ def tile_list_tgn_rnnP_kernel(
                     in_=pass_rows(source, operand % PASSES, slice(k * P, (k + 1) * P)),
                 )
 
-        def quantise_w(k, pieces):
-            raw = by_row(w_raw[k % len(w_raw)][:])
+        def w_piece(k, pieces, step):
             width = BANK // pieces
-            for step in range(pieces):
-                piece = (step + pieces // 2) % pieces
-                cols = slice(piece * width, (piece + 1) * width)
-                if k == 1:
-                    staged = head_buffer(QUARTERS, step)[:]
-                else:
-                    staged = w_bf[:, PACK * piece * width : PACK * (piece + 1) * width]
-                interleave(staged, raw[:, :, cols])
-                nc.vector.quantize_mx(
-                    out=w_codes[k % len(w_codes)][:, cols].bitcast(FP8X4),
-                    scales=w_scales[k % len(w_scales)][:, cols],
-                    in_=staged,
-                )
+            first = (step + pieces // 2) % pieces * width
+            if k == 1:
+                return slice(first, first + width), head_buffer(QUARTERS, step)[:]
+            return slice(first, first + width), w_bf[:, PACK * first : PACK * (first + width)]
+
+        def round_w(k, pieces, step):
+            cols, staged = w_piece(k, pieces, step)
+            interleave(staged, by_row(w_raw[k % len(w_raw)])[:, :, cols])
+
+        def quantise_w(k, pieces, step):
+            cols, staged = w_piece(k, pieces, step)
+            nc.vector.quantize_mx(
+                out=w_codes[k % len(w_codes)][:, cols].bitcast(FP8X4),
+                scales=w_scales[k % len(w_scales)][:, cols],
+                in_=staged,
+            )
 
         def load_h(k):
             nc.sync.dma_start(out=h_rows[k % 2][:], in_=hT[k * P : (k + 1) * P, :])
@@ -143,11 +151,13 @@ def tile_list_tgn_rnnP_kernel(
             if k == 1 and first < BANK:
                 place = BANK if first == 0 else 0
                 return w_bf[:].bitcast(F32)[:, place : place + count]
-            return w_raw[(k + 1) % len(w_raw)][:, first : first + count]
+            if k == 1:
+                return x_raw[0][:, 0:count]
+            return slots[(k + 1) % len(slots)][:, first : first + count]
 
         def turned(k):
             if 0 < k < TILES - 3:
-                return w_raw[k % len(w_raw)][:, J : 2 * J].bitcast(BF16)
+                return slots[k % len(slots)][:, J : 2 * J].bitcast(BF16)
             if k + 3 == TILES:
                 return w_bf[:]
             return last_turned[k % 2][:]
@@ -194,6 +204,8 @@ def tile_list_tgn_rnnP_kernel(
                 return x_raw[PASSES * (first // QUARTER + 1) + 1][:, 0:count]
             if k == 0:
                 return w_raw[1][:, 0:count]
+            if k == 1 and first == BANK:
+                return w_raw[2][:, 0:count]
             if k == TILES - 1:
                 return w_bf[:].bitcast(F32)[:, first : first + count]
             return summed[k % 2][:, first : first + count]
@@ -233,12 +245,17 @@ def tile_list_tgn_rnnP_kernel(
             if k == TILES - 2:
                 freed = w_bf[:] if first < J else weight[:].bitcast(BF16)
                 return freed[:, first % J : first % J + count]
+            if k == 0 and first == 0:
+                return slots[0][:, 2 * J : 3 * J].bitcast(BF16)[:, 0:count]
+            if k < TILES_A_PASS:
+                return slots[(k + 1) % len(slots)][:, 2 * J : 3 * J].bitcast(BF16)[:, first : first + count]
             return y_bf[k % len(y_bf)][:, first : first + count]
 
-        def turn_words(k, used, copies):
+        def turn_words(k, used, copies, which=None):
             words = turned(k).bitcast(F32)
             span = BLOCKS // len(used)
-            for i, bank in enumerate(used):
+            for i in range(len(used)) if which is None else which:
+                bank = used[i]
                 for s in range(2 * span):
                     first = (2 * span * i + s) * P
                     nc.tensor.transpose(bank[:, s * P : (s + 1) * P], words[:, first : first + P], ident[:])
@@ -333,15 +350,25 @@ def tile_list_tgn_rnnP_kernel(
                 )
             nc.scalar.copy(out=weight[:, h * BANK : (h + 1) * BANK], in_=banks[h][:])
 
-        quantise_w(0, 2)
-        quantise_x(0)
+        for step in range(2):
+            round_w(0, 2, step)
+            quantise_w(0, 2, step)
+        for a in range(PASSES):
+            round_x(0, a)
+            quantise_x(0, a)
         gather_scales(1, "x_bf1")
         load_w(3)
         for q in range(QUARTERS):
             if q + 1 < QUARTERS:
-                quantise_x(q + 1)
+                round_next = [lambda a=a: round_x(q + 1, a) for a in range(PASSES)]
+                quantise_next = [lambda a=a: quantise_x(q + 1, a) for a in range(PASSES)]
             else:
-                quantise_w(1, 2)
+                round_next = [lambda a=a: round_w(1, 2, a) for a in range(PASSES)]
+                quantise_next = [lambda a=a: quantise_w(1, 2, a) for a in range(PASSES)]
+            round_next[0]()
+            quantise_next[0]()
+            round_next[1]()
+            quantise_next[1]()
             product(0, q * QUARTER, QUARTER, banks[4 + q % 2])
             activate(0, q * QUARTER, QUARTER, banks[4 + q % 2])
             gather_add(0, q * QUARTER, QUARTER)
@@ -357,9 +384,12 @@ def tile_list_tgn_rnnP_kernel(
             gather_add(1, q * QUARTER, QUARTER)
         scatter(1, 0, BANK)
         product(1, BANK, BANK, banks[1])
-        quantise_w(2, 2)
         activate(1, BANK, BANK, banks[1])
+        round_w(2, 2, 0)
+        quantise_w(2, 2, 0)
+        round_w(2, 2, 1)
         gather_add(1, BANK, BANK)
+        quantise_w(2, 2, 1)
         scatter(1, BANK, BANK)
         turn(0, banks[4:8], [copy_s] * BLOCKS)
         load_w(5)
@@ -367,17 +397,30 @@ def tile_list_tgn_rnnP_kernel(
         store_page(1)
 
         last = TILES - 1
-        for k in range(2, last):
-            quantise_w(k + 1, 1)
+        for step in range(2):
+            round_w(3, 2, step)
+            quantise_w(3, 2, step)
+        multiply(2)
+        gather_add(2, 0, J)
+        load_h(4)
+        turn_words(0, banks[2:4], [copy_s] * 2, [0])
+        quantise_y(0, HALVES, both_sync, [0])
+        scatter(2, 0, J)
+        store_page(2)
+        load_w(6)
+        for k in range(3, last):
+            round_w(k + 1, 1, 0)
+            quantise_w(k + 1, 1, 0)
             multiply(k)
             gather_add(k, 0, J)
             if k + 2 < TILES:
                 load_h(k + 2)
-            if k >= 3:
-                turn_back(k - 3, banks[0:2], [copy_s] * 2, 2, both_sync)
-                turn(k - 2, banks[4:8], [copy_s] * BLOCKS)
-            if k in (2, 4):
-                load_w(6 if k == 2 else 7)
+            halves = [1] if k == 3 else range(HALVES)
+            turn_words(k - 3, banks[2:4], [copy_s] * 2, halves)
+            quantise_y(k - 3, HALVES, both_sync, halves)
+            turn(k - 2, banks[4:8], [copy_s] * BLOCKS)
+            if k + 3 == last:
+                load_w(last)
             scatter(k, 0, J)
             store_page(k)
         turn_back(last - 3, banks[2:4], [copy_s] * 2, 1, both_sync)

@@ -35,6 +35,8 @@ QUARTERS = 4
 QUARTER = J // QUARTERS
 WARM_PASSES = 6
 RAW_START = 640
+ROWS_FROM = P - 2 * TILES
+SCALES_FROM = P - QUADRANT
 RUN = 4
 OPERAND_ORDER = (2, 3, 0, 1)
 STORE_FROM = {1: 0, 3: 2, 4: 4, 5: 5, 6: 6, 7: 7}
@@ -53,12 +55,14 @@ def tile_list_tgn_rnnP_kernel(
 
         offsets = keep.tile([P, J // LIST_ROWS], U16, name="offsets")
         tab_w = keep.tile([P, T], I32, name="tab_w", align_bytes=64)
-        tab_s = keep.tile([P, PASSES * T], U8, name="tab_s", align_bytes=64)
+        tab_s = keep.tile([P, T], U8, name="tab_s", align_bytes=64)
+        picked_s = keep.tile([P, J], U8, name="picked_s", align_bytes=64)
+        planes_s = keep.tile([P, PASSES * J], U8, name="planes_s", align_bytes=64)
         picked_w = keep.tile([P, J], U32, name="picked_w", tag="picked", align_bytes=64)
         parted_w = keep.tile([P, PASSES * 2 * J], U8, name="parted_w", align_bytes=64)
         ident = keep.tile([P, P], F32, name="ident", align_bytes=64)
         bn_rows = keep.tile([P, P], F32, name="bn_rows", align_bytes=64)
-        bias = keep.tile([P, 2 * TILES], F32, name="bias", align_bytes=64)
+        bias = keep.tile([P, TILES], F32, name="bias", align_bytes=64)
         weight = keep.tile([P, J], F32, name="weight", align_bytes=64)
         x_raw = tiles(QUARTERS * PASSES, [P, PACK * QUARTER], F32, "x_raw")
         x_bf = tiles(4, [P, PACK * QUARTER], BF16, "x_bf")
@@ -86,18 +90,14 @@ def tile_list_tgn_rnnP_kernel(
         def pass_rows(source, a, cols):
             return source[a * K_PASS : (a + 1) * K_PASS, cols].rearrange("(p t) c -> p t c", t=PACK)
 
-        def interleave(dst, src):
-            nc.scalar.copy(
+        def interleave(dst, src, copy=copy_s):
+            copy(
                 out=dst.rearrange("p (c i t) -> p c t i", i=RUN, t=PACK),
                 in_=src.rearrange("p t (c i) -> p c t i", i=RUN),
             )
 
-        def head_buffer(step, role):
-            if step == 0:
-                return x_bf[role]
-            if role == 0:
-                return x_bf[2]
-            return x_bf[3 if (step + role) % 2 == 0 else 0]
+        def head_buffer(step, piece):
+            return x_bf[(PASSES * step + piece) % len(x_bf)]
 
         def load_x(q, which):
             for a in which:
@@ -106,7 +106,7 @@ def tile_list_tgn_rnnP_kernel(
                 )
 
         def round_x(q, a):
-            interleave(head_buffer(q, a)[:], by_row(x_raw[PASSES * q + a][:]))
+            interleave(head_buffer(q, a)[:], by_row(x_raw[PASSES * q + a][:]), copy_v if q == 0 else copy_s)
 
         def quantise_x(q, a):
             cols = slice(q * QUARTER, (q + 1) * QUARTER)
@@ -146,8 +146,10 @@ def tile_list_tgn_rnnP_kernel(
             nc.sync.dma_start(out=h_rows[k % 2][:], in_=hT[k * P : (k + 1) * P, :])
 
         def tanh_part(k, first, count):
+            if k == 0 and first < J - QUARTER:
+                return x_raw[PASSES * (first // QUARTER + 1)][:, 0:count]
             if k == 0:
-                return head_buffer(first // QUARTER + 1, 2)[:].bitcast(F32)[:, 0:count]
+                return w_raw[1][:, count : 2 * count]
             if k == 1 and first < BANK:
                 place = BANK if first == 0 else 0
                 return w_bf[:].bitcast(F32)[:, place : place + count]
@@ -174,8 +176,7 @@ def tile_list_tgn_rnnP_kernel(
                     rhs_scale = x_scales[a][:, start : start + width]
                 else:
                     rhs = parted_w[:, 2 * (a * J + start) : 2 * (a * J + start + width)].bitcast(FP4X4)
-                    half, inside = divmod(start, BANK)
-                    rhs_scale = picked_s[half][:, a * BANK + inside : a * BANK + inside + width]
+                    rhs_scale = planes_s[:, a * J + start : a * J + start + width]
                 nc.tensor.matmul_mx(
                     out=bank[:, start - first : start - first + width],
                     lhsT=w_codes[k % len(w_codes)][:, operand * P : (operand + 1) * P].bitcast(FP8X4),
@@ -295,27 +296,31 @@ def tile_list_tgn_rnnP_kernel(
                         in_=y_scales[a][QUADRANT * g : QUADRANT * g + SCALE_ROWS * TILES_A_PASS, :].bitcast(I32),
                     )
 
-        nc.gpsimd.memset(tab_s[:].bitcast(I32), 0)
-        nc.gpsimd.memset(bn_rows[:], 0.0)
         make_identity(nc, ident[:])
-        warm = keep.tile([P, 8], F32, name="warm")
-        nc.scalar.activation(out=warm[:, 0:1], in_=ident[:, 0:1], func=ACT.Tanh)
+        nc.vector.memset(bn_rows[0:ROWS_FROM, :], 0.0)
+        nc.vector.memset(tab_s[0:SCALES_FROM, :].bitcast(I32), 0)
+        nc.scalar.activation(out=bias[0:ROWS_FROM, 0:1], in_=bn_rows[0:ROWS_FROM, 0:1], func=ACT.Tanh)
         nc.sync.dma_start(offsets[:], offs)
-        for row in range(SCALE_ROWS):
-            nc.sync.dma_start(
-                out=tab_s[row:P:QUADRANT, :].bitcast(I32).rearrange("q (a t) -> q a t", a=PASSES),
-                in_=tab_scales[:, row : QUADRANTS * SCALE_ROWS : SCALE_ROWS, :].bitcast(I32).rearrange("a q t -> q a t"),
-            )
+        nc.sync.dma_start(out=tab_s[SCALES_FROM:P, :].bitcast(I32), in_=tab_scales.bitcast(I32).rearrange("a q t -> q a t"))
         table = tab_words[0].rearrange("p t b -> p (t b)").bitcast(I32)
+        nc.sync.dma_start(out=bn_rows[ROWS_FROM : ROWS_FROM + TILES, :], in_=bn.rearrange("(i p) -> i p", p=P))
+        nc.sync.dma_start(out=bn_rows[ROWS_FROM + TILES : P, :], in_=wgo[0].rearrange("(i p) -> i p", p=P))
         nc.sync.dma_start(out=tab_w[:], in_=table)
-        nc.sync.dma_start(out=bn_rows[0:TILES, :], in_=bn.rearrange("(i p) -> i p", p=P))
-        nc.sync.dma_start(out=bn_rows[TILES : 2 * TILES, :], in_=wgo[0].rearrange("(i p) -> i p", p=P))
+        nc.vector.memset(planes_s[:].bitcast(I32), 0)
         for page in pages:
-            nc.vector.memset(page[:], 0.0)
-        load_x(0, [0])
+            nc.gpsimd.memset(page[:], 0.0)
         load_w(0)
-        load_x(0, [1])
+        load_x(0, range(PASSES))
         load_x(1, range(PASSES))
+        nc.vector.tensor_copy(picked_s[:], tab_s[:].indirect(offsets[:]))
+        for quadrant in range(QUADRANTS):
+            rows = PASSES * SCALE_ROWS
+            nc.sync.dma_start(
+                out=planes_s[QUADRANT * quadrant : QUADRANT * quadrant + SCALE_ROWS, :]
+                .bitcast(I32)
+                .rearrange("r (a j) -> r a j", a=PASSES),
+                in_=picked_s[SCALES_FROM + rows * quadrant : SCALES_FROM + rows * (quadrant + 1), :].bitcast(I32),
+            )
         load_h(0)
         load_x(2, range(PASSES))
         load_x(3, range(PASSES))
@@ -328,25 +333,16 @@ def tile_list_tgn_rnnP_kernel(
             out=parted_w[:].bitcast(U16).rearrange("p (d j) -> p d j", d=PASSES),
             in_=picked_w[:].bitcast(U16).rearrange("p (j d) -> p d j", d=PASSES),
         )
-        picked_s = []
-
-        def gather_scales(half, tag):
-            picked_s.append(keep.tile([P, PASSES * BANK], U8, name="picked_s" + str(half), tag=tag, align_bytes=64))
-            for a in range(PASSES):
-                nc.vector.tensor_copy(
-                    picked_s[half][:, a * BANK : (a + 1) * BANK],
-                    tab_s[:, a * T : (a + 1) * T].indirect(list_part(half * BANK, BANK)),
-                )
-
-        gather_scales(0, "picked_s0")
 
         nc.tensor.transpose(banks[2][:, 0:P], bn_rows[:], ident[:])
-        nc.scalar.copy(out=bias[:], in_=banks[2][:, 0 : 2 * TILES])
+        wgo_cols = w_bf[:].bitcast(F32)[:, BANK : BANK + TILES]
+        nc.scalar.copy(out=wgo_cols, in_=banks[2][:, ROWS_FROM + TILES : P])
+        nc.scalar.copy(out=bias[:], in_=banks[2][:, ROWS_FROM : ROWS_FROM + TILES])
         for h in range(HALVES):
             for b in range(BLOCKS):
-                column = TILES + BLOCKS * h + b
+                column = BLOCKS * h + b
                 nc.tensor.transpose(
-                    banks[h][:, b * P : (b + 1) * P], bias[:, column : column + 1].to_broadcast([P, P]), ident[:]
+                    banks[h][:, b * P : (b + 1) * P], wgo_cols[:, column : column + 1].to_broadcast([P, P]), ident[:]
                 )
             nc.scalar.copy(out=weight[:, h * BANK : (h + 1) * BANK], in_=banks[h][:])
 
@@ -356,7 +352,6 @@ def tile_list_tgn_rnnP_kernel(
         for a in range(PASSES):
             round_x(0, a)
             quantise_x(0, a)
-        gather_scales(1, "x_bf1")
         load_w(3)
         for q in range(QUARTERS):
             if q + 1 < QUARTERS:
@@ -368,10 +363,10 @@ def tile_list_tgn_rnnP_kernel(
             round_next[0]()
             quantise_next[0]()
             round_next[1]()
-            quantise_next[1]()
             product(0, q * QUARTER, QUARTER, banks[4 + q % 2])
             activate(0, q * QUARTER, QUARTER, banks[4 + q % 2])
             gather_add(0, q * QUARTER, QUARTER)
+            quantise_next[1]()
             scatter(0, q * QUARTER, QUARTER)
         load_h(2)
         store_page(0)

@@ -33,13 +33,12 @@ SCALE_ROWS = 4
 LIST_ROWS = 16
 QUARTERS = 4
 QUARTER = J // QUARTERS
-WARM_PASSES = 6
 RAW_START = 640
-ROWS_FROM = P - 2 * TILES
+ROWS_FROM = P - TILES - TILES_A_PASS
 SCALES_FROM = P - QUADRANT
 RUN = 4
 OPERAND_ORDER = (2, 3, 0, 1)
-STORE_FROM = {1: 0, 3: 2, 4: 4, 5: 5, 6: 6, 7: 7}
+STORE_FROM = {1: 0, 3: 2}
 
 
 def tile_list_tgn_rnnP_kernel(
@@ -62,9 +61,15 @@ def tile_list_tgn_rnnP_kernel(
         parted_w = keep.tile([P, PASSES * 2 * J], U8, name="parted_w", align_bytes=64)
         ident = keep.tile([P, P], F32, name="ident", align_bytes=64)
         bn_rows = keep.tile([P, P], F32, name="bn_rows", align_bytes=64)
-        bias = keep.tile([P, TILES], F32, name="bias", align_bytes=64)
+        bias = keep.tile([P, TILES_A_PASS], F32, name="bias", align_bytes=64)
+        dealt_bias = keep.tile([P, PACK], F32, name="dealt_bias", align_bytes=64)
         weight = keep.tile([P, J], F32, name="weight", align_bytes=64)
-        x_raw = tiles(QUARTERS * PASSES, [P, PACK * QUARTER], F32, "x_raw")
+        x_half = tiles(PASSES, [P, PACK * BANK], F32, "x_half")
+        x_rest = tiles(2, [P, PACK * BANK], F32, "x_rest")
+        dealt_raw = [x_half[1], x_rest[0], x_rest[1], x_half[0]]
+        dealt_codes = tiles(4, [P, BANK], U32, "dealt_codes")
+        dealt_scales = tiles(4, [P, BANK], U8, "dealt_scales")
+        woven = keep.tile([P, PACK * T], BF16, name="woven", align_bytes=64)
         x_bf = tiles(4, [P, PACK * QUARTER], BF16, "x_bf")
         x_codes = tiles(PASSES, [P, J], U32, "x_codes")
         x_scales = tiles(PASSES, [P, J], U8, "x_scales")
@@ -75,11 +80,10 @@ def tile_list_tgn_rnnP_kernel(
         w_scales = tiles(3, [P, BANK], U8, "w_scales")
         h_rows = tiles(2, [P, T], F32, "h_rows")
         summed = tiles(2, [P, J], F32, "summed")
-        pages = tiles(2, [P, T], F32, "pages")
-        last_turned = tiles(2, [P, T], BF16, "last_turned")
-        y_bf = tiles(2, [P, T], BF16, "y_bf")
+        pages = tiles(3, [P, T], F32, "pages")
         y_codes = tiles(PASSES, [P, TILES_A_PASS * BANK], I32, "y_codes")
-        y_scales = tiles(PASSES, [P, BANK], U8, "y_scales")
+        woven_scales = keep.tile([P, T], U8, name="woven_scales", align_bytes=64)
+        y_scales = tiles(1, [P, BANK], U8, "y_scales")
         banks = [psum.tile([P, BANK], F32, name="bank" + str(i)) for i in range(8)]
         copy_s, copy_v = nc.scalar.copy, nc.vector.tensor_copy
         both_sync = (nc.sync, nc.sync)
@@ -99,14 +103,17 @@ def tile_list_tgn_rnnP_kernel(
         def head_buffer(step, piece):
             return x_bf[(PASSES * step + piece) % len(x_bf)]
 
-        def load_x(q, which):
-            for a in which:
-                nc.sync.dma_start(
-                    out=by_row(x_raw[PASSES * q + a][:]), in_=pass_rows(x, a, slice(q * QUARTER, (q + 1) * QUARTER))
-                )
+        def x_raw(q, a):
+            if q < 2:
+                return by_row(x_half[a][:])[:, :, q * QUARTER : (q + 1) * QUARTER]
+            return by_row(x_rest[q - 2][:, a * J : (a + 1) * J])
+
+        def load_x(q):
+            for a in range(PASSES):
+                nc.sync.dma_start(out=x_raw(q, a), in_=pass_rows(x, a, slice(q * QUARTER, (q + 1) * QUARTER)))
 
         def round_x(q, a):
-            interleave(head_buffer(q, a)[:], by_row(x_raw[PASSES * q + a][:]), copy_v if q == 0 else copy_s)
+            interleave(head_buffer(q, a)[:], x_raw(q, a), copy_v if q == 0 else copy_s)
 
         def quantise_x(q, a):
             cols = slice(q * QUARTER, (q + 1) * QUARTER)
@@ -142,27 +149,65 @@ def tile_list_tgn_rnnP_kernel(
                 in_=staged,
             )
 
+        def tile_rows(source, k):
+            if k < TILES_A_PASS:
+                return source[k * P : (k + 1) * P, :]
+            return pass_rows(source, 1, slice(0, T))[:, k - TILES_A_PASS, :]
+
+        def load_dealt(i):
+            operand = OPERAND_ORDER[i]
+            source = (wn, un)[operand // PASSES]
+            nc.sync.dma_start(out=by_row(dealt_raw[i][:]), in_=pass_rows(source, operand % PASSES, slice(K_PASS, N)))
+
+        def dealt_staged(i):
+            if i < 2:
+                return slots[0][:, (i + 1) * J : (i + 2) * J].bitcast(BF16)
+            return dealt_raw[i - 2][:, 0:J].bitcast(BF16)
+
+        def round_dealt(i):
+            nc.scalar.copy(
+                out=dealt_staged(i).rearrange("p (t m j) -> p m j t", t=PACK, j=PACK),
+                in_=dealt_raw[i][:].rearrange("p (j m t) -> p m j t", t=PACK, j=PACK),
+            )
+
+        def quantise_dealt(i):
+            operand = OPERAND_ORDER[i]
+            nc.vector.quantize_mx(
+                out=dealt_codes[operand][:].bitcast(FP8X4), scales=dealt_scales[operand][:], in_=dealt_staged(i)
+            )
+
+        def stationary(k, operand):
+            if k < TILES_A_PASS:
+                cols = slice(operand * P, (operand + 1) * P)
+                return w_codes[k % len(w_codes)][:, cols], w_scales[k % len(w_scales)][:, cols]
+            cols = slice((k - TILES_A_PASS) * P, (k - TILES_A_PASS + 1) * P)
+            return dealt_codes[operand][:, cols], dealt_scales[operand][:, cols]
+
         def load_h(k):
-            nc.sync.dma_start(out=h_rows[k % 2][:], in_=hT[k * P : (k + 1) * P, :])
+            nc.sync.dma_start(out=h_rows[k % 2][:], in_=tile_rows(hT, k))
 
         def tanh_part(k, first, count):
             if k == 0 and first < J - QUARTER:
-                return x_raw[PASSES * (first // QUARTER + 1)][:, 0:count]
+                return x_raw(first // QUARTER + 1, 0)[:, 0, :]
             if k == 0:
                 return w_raw[1][:, count : 2 * count]
             if k == 1 and first < BANK:
                 place = BANK if first == 0 else 0
                 return w_bf[:].bitcast(F32)[:, place : place + count]
             if k == 1:
-                return x_raw[0][:, 0:count]
-            return slots[(k + 1) % len(slots)][:, first : first + count]
+                return x_half[0][:, BANK : BANK + count]
+            if k == 2:
+                return slots[0][:, first : first + count]
+            if k == 3:
+                return dealt_raw[1][:, J + first : J + first + count]
+            return slots[1 + k % 2][:, first : first + count]
 
         def turned(k):
-            if 0 < k < TILES - 3:
-                return slots[k % len(slots)][:, J : 2 * J].bitcast(BF16)
-            if k + 3 == TILES:
-                return w_bf[:]
-            return last_turned[k % 2][:]
+            if k == 0:
+                return dealt_raw[3][:, J : 2 * J].bitcast(BF16)
+            if k == TILES_A_PASS - 1:
+                return woven[:, 0:T]
+            return slots[1 + k % 2][:, J : 2 * J].bitcast(BF16)
 
         def product(k, first, count, bank):
             passes = []
@@ -179,8 +224,8 @@ def tile_list_tgn_rnnP_kernel(
                     rhs_scale = planes_s[:, a * J + start : a * J + start + width]
                 nc.tensor.matmul_mx(
                     out=bank[:, start - first : start - first + width],
-                    lhsT=w_codes[k % len(w_codes)][:, operand * P : (operand + 1) * P].bitcast(FP8X4),
-                    lhsT_scale=w_scales[k % len(w_scales)][:, operand * P : (operand + 1) * P],
+                    lhsT=stationary(k, operand)[0].bitcast(FP8X4),
+                    lhsT_scale=stationary(k, operand)[1],
                     rhs=rhs,
                     rhs_scale=rhs_scale,
                     start=(i == 0),
@@ -188,9 +233,9 @@ def tile_list_tgn_rnnP_kernel(
                 )
 
         def activate(k, first, count, bank):
-            nc.scalar.activation(
-                out=tanh_part(k, first, count), in_=bank[:, 0:count], func=ACT.Tanh, bias=bias[:, k : k + 1]
-            )
+            column = k % TILES_A_PASS
+            row_bias = (bias, dealt_bias)[k // TILES_A_PASS][:, column : column + 1]
+            nc.scalar.activation(out=tanh_part(k, first, count), in_=bank[:, 0:count], func=ACT.Tanh, bias=row_bias)
 
         def multiply(k):
             for h in range(HALVES):
@@ -202,13 +247,13 @@ def tile_list_tgn_rnnP_kernel(
 
         def sum_part(k, first, count):
             if k == 0 and first < J - QUARTER:
-                return x_raw[PASSES * (first // QUARTER + 1) + 1][:, 0:count]
+                return x_raw(first // QUARTER + 1, 1)[:, 0, :]
             if k == 0:
                 return w_raw[1][:, 0:count]
             if k == 1 and first == BANK:
                 return w_raw[2][:, 0:count]
-            if k == TILES - 1:
-                return w_bf[:].bitcast(F32)[:, first : first + count]
+            if k == 3:
+                return dealt_raw[3][:, first : first + count]
             return summed[k % 2][:, first : first + count]
 
         def gather_add(k, first, count):
@@ -222,35 +267,28 @@ def tile_list_tgn_rnnP_kernel(
         def scatter(k, first, count):
             cols = slice(first, first + count)
             nc.vector.tensor_tensor(
-                out=pages[k % 2][:].indirect(list_part(first, count)),
+                out=pages[k % len(pages)][:].indirect(list_part(first, count)),
                 in0=sum_part(k, first, count),
                 in1=weight[:, cols],
                 op=ALU.mult,
             )
 
         def store_page(k):
-            nc.sync.dma_start(out=out_0[k * P : (k + 1) * P, :], in_=pages[k % 2][:])
+            nc.sync.dma_start(out=tile_rows(out_0, k), in_=pages[k % len(pages)][:])
 
         def turn(k, by_block, copies):
             for b in range(BLOCKS):
                 bank = by_block[b]
                 for g in range(GROUPS):
                     first = g * BANK + b * P
-                    nc.tensor.transpose(bank[:, g * P : (g + 1) * P], pages[k % 2][:, first : first + P], ident[:])
+                    nc.tensor.transpose(bank[:, g * P : (g + 1) * P], pages[k % len(pages)][:, first : first + P], ident[:])
                 copies[b](
                     out=turned(k)[:, b * BANK : (b + 1) * BANK].rearrange("p (u r e) -> p u r e", u=2, e=2),
                     in_=bank[:].rearrange("p (r u e) -> p u r e", u=2, e=2),
                 )
 
         def staged_y(k, first, count):
-            if k == TILES - 2:
-                freed = w_bf[:] if first < J else weight[:].bitcast(BF16)
-                return freed[:, first % J : first % J + count]
-            if k == 0 and first == 0:
-                return slots[0][:, 2 * J : 3 * J].bitcast(BF16)[:, 0:count]
-            if k < TILES_A_PASS:
-                return slots[(k + 1) % len(slots)][:, 2 * J : 3 * J].bitcast(BF16)[:, first : first + count]
-            return y_bf[k % len(y_bf)][:, first : first + count]
+            return slots[1 + k % 2][:, 2 * J : 3 * J].bitcast(BF16)[:, first : first + count]
 
         def turn_words(k, used, copies, which=None):
             words = turned(k).bitcast(F32)
@@ -266,10 +304,6 @@ def tile_list_tgn_rnnP_kernel(
                     ),
                     in_=bank[:, 0 : 2 * P * span].rearrange("p (b u c) -> p b c u", b=span, u=2),
                 )
-
-        def turn_back(k, used, copies, pieces, queues):
-            turn_words(k, used, copies)
-            quantise_y(k, pieces, queues, range(pieces))
 
         def quantise_y(k, pieces, queues, which):
             a, w = divmod(k, TILES_A_PASS)
@@ -296,6 +330,25 @@ def tile_list_tgn_rnnP_kernel(
                         in_=y_scales[a][QUADRANT * g : QUADRANT * g + SCALE_ROWS * TILES_A_PASS, :].bitcast(I32),
                     )
 
+        def weave(k, cols, copy, doubled=False):
+            t = k - TILES_A_PASS
+            page = pages[k % len(pages)][:, cols]
+            by_column = woven[:].rearrange("p (c t) -> p c t", t=PACK)
+            if doubled:
+                copy(out=by_column[:, cols, t : t + 2], in_=page.unsqueeze(2).to_broadcast([P, cols.stop - cols.start, 2]))
+            else:
+                copy(out=by_column[:, cols, t], in_=page)
+
+        def quantise_woven(cols):
+            nc.vector.quantize_mx(
+                out=y_codes[1][:, cols].bitcast(FP8X4),
+                scales=woven_scales[:, cols],
+                in_=woven[:, PACK * cols.start : PACK * cols.stop],
+            )
+
+        def store_woven(cols, queue):
+            queue.dma_start(out=out_1[1].rearrange("p t b -> p (t b)").bitcast(I32)[:, cols], in_=y_codes[1][:, cols])
+
         make_identity(nc, ident[:])
         nc.vector.memset(bn_rows[0:ROWS_FROM, :], 0.0)
         nc.vector.memset(tab_s[0:SCALES_FROM, :].bitcast(I32), 0)
@@ -303,15 +356,15 @@ def tile_list_tgn_rnnP_kernel(
         nc.sync.dma_start(offsets[:], offs)
         nc.sync.dma_start(out=tab_s[SCALES_FROM:P, :].bitcast(I32), in_=tab_scales.bitcast(I32).rearrange("a q t -> q a t"))
         table = tab_words[0].rearrange("p t b -> p (t b)").bitcast(I32)
-        nc.sync.dma_start(out=bn_rows[ROWS_FROM : ROWS_FROM + TILES, :], in_=bn.rearrange("(i p) -> i p", p=P))
-        nc.sync.dma_start(out=bn_rows[ROWS_FROM + TILES : P, :], in_=wgo[0].rearrange("(i p) -> i p", p=P))
+        nc.sync.dma_start(out=bn_rows[ROWS_FROM : P - TILES, :], in_=bn[0:K_PASS].rearrange("(i p) -> i p", p=P))
+        nc.sync.dma_start(out=bn_rows[P - TILES : P, :], in_=wgo[0].rearrange("(i p) -> i p", p=P))
         nc.sync.dma_start(out=tab_w[:], in_=table)
         nc.vector.memset(planes_s[:].bitcast(I32), 0)
         for page in pages:
             nc.gpsimd.memset(page[:], 0.0)
         load_w(0)
-        load_x(0, range(PASSES))
-        load_x(1, range(PASSES))
+        load_x(0)
+        load_x(1)
         nc.vector.tensor_copy(picked_s[:], tab_s[:].indirect(offsets[:]))
         for quadrant in range(QUADRANTS):
             rows = PASSES * SCALE_ROWS
@@ -322,8 +375,8 @@ def tile_list_tgn_rnnP_kernel(
                 in_=picked_s[SCALES_FROM + rows * quadrant : SCALES_FROM + rows * (quadrant + 1), :].bitcast(I32),
             )
         load_h(0)
-        load_x(2, range(PASSES))
-        load_x(3, range(PASSES))
+        load_x(2)
+        load_x(3)
         load_w(1)
         load_h(1)
         load_w(2)
@@ -336,8 +389,8 @@ def tile_list_tgn_rnnP_kernel(
 
         nc.tensor.transpose(banks[2][:, 0:P], bn_rows[:], ident[:])
         wgo_cols = w_bf[:].bitcast(F32)[:, BANK : BANK + TILES]
-        nc.scalar.copy(out=wgo_cols, in_=banks[2][:, ROWS_FROM + TILES : P])
-        nc.scalar.copy(out=bias[:], in_=banks[2][:, ROWS_FROM : ROWS_FROM + TILES])
+        nc.scalar.copy(out=wgo_cols, in_=banks[2][:, P - TILES : P])
+        nc.scalar.copy(out=bias[:], in_=banks[2][:, ROWS_FROM : P - TILES])
         for h in range(HALVES):
             for b in range(BLOCKS):
                 column = BLOCKS * h + b
@@ -369,10 +422,11 @@ def tile_list_tgn_rnnP_kernel(
             quantise_next[1]()
             scatter(0, q * QUARTER, QUARTER)
         load_h(2)
+        for i in range(3):
+            load_dealt(i)
+        nc.sync.dma_start(out=dealt_bias[:], in_=bn[K_PASS:N].rearrange("(p t) -> p t", t=PACK))
         store_page(0)
-        load_w(4)
 
-        turning = banks[0:2] * 2
         for q in range(2):
             product(1, q * QUARTER, QUARTER, banks[q])
             activate(1, q * QUARTER, QUARTER, banks[q])
@@ -384,62 +438,58 @@ def tile_list_tgn_rnnP_kernel(
         quantise_w(2, 2, 0)
         round_w(2, 2, 1)
         gather_add(1, BANK, BANK)
+        load_dealt(3)
+        load_h(3)
         quantise_w(2, 2, 1)
         scatter(1, BANK, BANK)
-        turn(0, banks[4:8], [copy_s] * BLOCKS)
-        load_w(5)
-        load_h(3)
         store_page(1)
 
-        last = TILES - 1
         for step in range(2):
             round_w(3, 2, step)
             quantise_w(3, 2, step)
         multiply(2)
         gather_add(2, 0, J)
         load_h(4)
-        turn_words(0, banks[2:4], [copy_s] * 2, [0])
-        quantise_y(0, HALVES, both_sync, [0])
         scatter(2, 0, J)
         store_page(2)
-        load_w(6)
-        for k in range(3, last):
-            round_w(k + 1, 1, 0)
-            quantise_w(k + 1, 1, 0)
+
+        for i in range(3):
+            round_dealt(i)
+            quantise_dealt(i)
+        multiply(3)
+        round_dealt(3)
+        gather_add(3, 0, J)
+        load_h(5)
+        quantise_dealt(3)
+        turn(0, banks[4:8], [copy_s] * BLOCKS)
+        scatter(3, 0, J)
+        store_page(3)
+        turn(1, banks[4:8], [copy_s] * BLOCKS)
+
+        last = TILES - 1
+        for k in range(TILES_A_PASS, TILES):
             multiply(k)
             gather_add(k, 0, J)
             if k + 2 < TILES:
                 load_h(k + 2)
-            halves = [1] if k == 3 else range(HALVES)
-            turn_words(k - 3, banks[2:4], [copy_s] * 2, halves)
-            quantise_y(k - 3, HALVES, both_sync, halves)
-            turn(k - 2, banks[4:8], [copy_s] * BLOCKS)
-            if k + 3 == last:
-                load_w(last)
+            turn_words(k - TILES_A_PASS, banks[2:4], [copy_s] * 2)
+            quantise_y(k - TILES_A_PASS, HALVES, both_sync, range(HALVES))
+            if k == last:
+                weave(last - 3, slice(0, T), copy_s)
             scatter(k, 0, J)
             store_page(k)
-        turn_back(last - 3, banks[2:4], [copy_s] * 2, 1, both_sync)
-        multiply(last)
-        turn(last - 2, banks[4:8], [copy_s] * BLOCKS)
-        turn_words(last - 2, banks[0:2], [copy_s] * 2)
-        gather_add(last, 0, J)
-        for h in range(HALVES):
-            quantise_y(last - 2, HALVES, both_sync, [h])
-            scatter(last, h * BANK, BANK)
-        store_page(last)
-        handed = banks[0:2] + banks[6:8]
-        turn(last - 1, turning, [copy_s] * BLOCKS)
-        turn_words(last - 1, handed, [copy_s] * BLOCKS)
-        for i in range(WARM_PASSES):
-            nc.tensor.matmul_mx(
-                out=handed[i // 2][:],
-                lhsT=w_codes[last % len(w_codes)][:, 0:P].bitcast(FP8X4),
-                lhsT_scale=w_scales[last % len(w_scales)][:, 0:P],
-                rhs=x_codes[0][:, 0:BANK].bitcast(FP8X4),
-                rhs_scale=x_scales[0][:, 0:BANK],
-                start=True,
-                stop=True,
+            if k - 2 < TILES_A_PASS:
+                turn(k - 2, banks[4:8], [copy_s] * BLOCKS)
+        weave(last - 2, slice(0, T), copy_s)
+        weave(last - 1, slice(0, T), copy_s, doubled=True)
+        groups = [slice(g * BANK, (g + 1) * BANK) for g in range(GROUPS)]
+        for g in range(GROUPS):
+            weave(last, groups[g], copy_v if g < 2 else copy_s)
+        for g in range(GROUPS):
+            quantise_woven(groups[g])
+            store_woven(groups[g], nc.sync)
+        for quadrant in range(QUADRANTS):
+            nc.sync.dma_start(
+                out=out_2[1, SCALE_ROWS * quadrant : SCALE_ROWS * (quadrant + 1), :].bitcast(I32),
+                in_=woven_scales[QUADRANT * quadrant : QUADRANT * quadrant + SCALE_ROWS, :].bitcast(I32),
             )
-        quantise_y(last - 1, BLOCKS, both_sync, range(BLOCKS))
-        turn(last, handed, [copy_s, copy_v] * 2)
-        turn_back(last, banks[2:6], [copy_s, copy_v, copy_s, copy_s], BLOCKS, (nc.sync, nc.scalar))

@@ -24,6 +24,7 @@ PASSES = K // K_PASS
 BANK = 512
 TILES = N // P
 TILES_A_PASS = K_PASS // P
+OPERANDS = 2 * PASSES
 HALVES = J // BANK
 GROUPS = T // BANK
 BLOCKS = BANK // P
@@ -34,11 +35,14 @@ LIST_ROWS = 16
 QUARTERS = 4
 QUARTER = J // QUARTERS
 RAW_START = 640
-ROWS_FROM = P - TILES - TILES_A_PASS
+ROWS_FROM = P - J // P - TILES_A_PASS
+WGO_FROM = P - J // P
 SCALES_FROM = P - QUADRANT
 RUN = 4
 OPERAND_ORDER = (2, 3, 0, 1)
-STORE_FROM = {1: 0, 3: 2}
+PAGES_A_STORE = 2
+VECTOR_WEAVES = 2 * BANK - P
+WOVEN_EDGES = (0, BANK, 2 * BANK, 3 * BANK, T - BANK // 2, T)
 
 
 def tile_list_tgn_rnnP_kernel(
@@ -57,7 +61,7 @@ def tile_list_tgn_rnnP_kernel(
         tab_s = keep.tile([P, T], U8, name="tab_s", align_bytes=64)
         picked_s = keep.tile([P, J], U8, name="picked_s", align_bytes=64)
         planes_s = keep.tile([P, PASSES * J], U8, name="planes_s", align_bytes=64)
-        picked_w = keep.tile([P, J], U32, name="picked_w", tag="picked", align_bytes=64)
+        picked_w = keep.tile([P, J], U32, name="picked_w", align_bytes=64)
         parted_w = keep.tile([P, PASSES * 2 * J], U8, name="parted_w", align_bytes=64)
         ident = keep.tile([P, P], F32, name="ident", align_bytes=64)
         bn_rows = keep.tile([P, P], F32, name="bn_rows", align_bytes=64)
@@ -67,10 +71,10 @@ def tile_list_tgn_rnnP_kernel(
         x_half = tiles(PASSES, [P, PACK * BANK], F32, "x_half")
         x_rest = tiles(2, [P, PACK * BANK], F32, "x_rest")
         dealt_raw = [x_half[1], x_rest[0], x_rest[1], x_half[0]]
-        dealt_codes = tiles(4, [P, BANK], U32, "dealt_codes")
-        dealt_scales = tiles(4, [P, BANK], U8, "dealt_scales")
+        dealt_codes = tiles(OPERANDS, [P, BANK], U32, "dealt_codes")
+        dealt_scales = tiles(OPERANDS, [P, BANK], U8, "dealt_scales")
         woven = keep.tile([P, PACK * T], BF16, name="woven", align_bytes=64)
-        x_bf = tiles(4, [P, PACK * QUARTER], BF16, "x_bf")
+        x_bf = tiles(2 * PASSES, [P, PACK * QUARTER], BF16, "x_bf")
         x_codes = tiles(PASSES, [P, J], U32, "x_codes")
         x_scales = tiles(PASSES, [P, J], U8, "x_scales")
         slots = tiles(3, [P, 3 * J], F32, "slots")
@@ -81,12 +85,12 @@ def tile_list_tgn_rnnP_kernel(
         h_rows = tiles(2, [P, T], F32, "h_rows")
         summed = tiles(2, [P, J], F32, "summed")
         pages = tiles(3, [P, T], F32, "pages")
-        y_codes = tiles(PASSES, [P, TILES_A_PASS * BANK], I32, "y_codes")
+        plain_codes, woven_codes = tiles(PASSES, [P, T], I32, "y_codes")
         woven_scales = keep.tile([P, T], U8, name="woven_scales", align_bytes=64)
-        y_scales = tiles(1, [P, BANK], U8, "y_scales")
+        plain_scales = keep.tile([P, BANK], U8, name="y_scales0", align_bytes=64)
         banks = [psum.tile([P, BANK], F32, name="bank" + str(i)) for i in range(8)]
         copy_s, copy_v = nc.scalar.copy, nc.vector.tensor_copy
-        both_sync = (nc.sync, nc.sync)
+        sum_banks, word_banks, turn_banks = banks[0:2], banks[2:4], banks[4:8]
 
         def by_row(flat):
             return flat.rearrange("p (t c) -> p t c", t=PACK)
@@ -239,8 +243,8 @@ def tile_list_tgn_rnnP_kernel(
 
         def multiply(k):
             for h in range(HALVES):
-                product(k, h * BANK, BANK, banks[h])
-                activate(k, h * BANK, BANK, banks[h])
+                product(k, h * BANK, BANK, sum_banks[h])
+                activate(k, h * BANK, BANK, sum_banks[h])
 
         def list_part(first, count):
             return offsets[:, first // LIST_ROWS : (first + count) // LIST_ROWS]
@@ -276,78 +280,72 @@ def tile_list_tgn_rnnP_kernel(
         def store_page(k):
             nc.sync.dma_start(out=tile_rows(out_0, k), in_=pages[k % len(pages)][:])
 
-        def turn(k, by_block, copies):
+        def turn(k):
             for b in range(BLOCKS):
-                bank = by_block[b]
+                bank = turn_banks[b]
                 for g in range(GROUPS):
                     first = g * BANK + b * P
                     nc.tensor.transpose(bank[:, g * P : (g + 1) * P], pages[k % len(pages)][:, first : first + P], ident[:])
-                copies[b](
+                nc.scalar.copy(
                     out=turned(k)[:, b * BANK : (b + 1) * BANK].rearrange("p (u r e) -> p u r e", u=2, e=2),
                     in_=bank[:].rearrange("p (r u e) -> p u r e", u=2, e=2),
                 )
 
-        def staged_y(k, first, count):
-            return slots[1 + k % 2][:, 2 * J : 3 * J].bitcast(BF16)[:, first : first + count]
+        def staged_y(k):
+            return slots[1 + k % 2][:, 2 * J : 3 * J].bitcast(BF16)
 
-        def turn_words(k, used, copies, which=None):
+        def turn_words(k):
             words = turned(k).bitcast(F32)
-            span = BLOCKS // len(used)
-            for i in range(len(used)) if which is None else which:
-                bank = used[i]
+            span = BLOCKS // len(word_banks)
+            for i, bank in enumerate(word_banks):
                 for s in range(2 * span):
                     first = (2 * span * i + s) * P
                     nc.tensor.transpose(bank[:, s * P : (s + 1) * P], words[:, first : first + P], ident[:])
-                copies[i](
-                    out=staged_y(k, BANK * span * i, BANK * span).bitcast(F32).rearrange(
-                        "p (b c u) -> p b c u", b=span, u=2
-                    ),
-                    in_=bank[:, 0 : 2 * P * span].rearrange("p (b u c) -> p b c u", b=span, u=2),
+                staged = staged_y(k)[:, BANK * span * i : BANK * span * (i + 1)]
+                nc.scalar.copy(
+                    out=staged.bitcast(F32).rearrange("p (b c u) -> p b c u", b=span, u=2),
+                    in_=bank[:].rearrange("p (b u c) -> p b c u", b=span, u=2),
                 )
 
-        def quantise_y(k, pieces, queues, which):
-            a, w = divmod(k, TILES_A_PASS)
-            width = BANK // pieces
-            for piece in which:
-                first = piece * width
-                nc.vector.quantize_mx(
-                    out=y_codes[a][:, w * BANK + first : w * BANK + first + width].bitcast(FP8X4),
-                    scales=y_scales[a][SCALE_ROWS * w : P, first : first + width],
-                    in_=staged_y(k, PACK * first, PACK * width),
-                )
-            if piece + 1 < pieces:
-                return
-            if k in STORE_FROM:
-                held = slice(STORE_FROM[k] % TILES_A_PASS, w + 1)
-                codes_out = out_1[a].rearrange("p t b -> p (t b)").bitcast(I32).rearrange("(w q) t -> q w t", q=QUADRANT)
+        def codes_out(a):
+            return out_1[a].rearrange("p t b -> p (t b)").bitcast(I32)
+
+        def quantise_plain(k):
+            nc.vector.quantize_mx(
+                out=plain_codes[:, k * BANK : (k + 1) * BANK].bitcast(FP8X4),
+                scales=plain_scales[SCALE_ROWS * k : P, :],
+                in_=staged_y(k),
+            )
+            if (k + 1) % PAGES_A_STORE == 0:
+                held = slice(k + 1 - PAGES_A_STORE, k + 1)
+                by_page = codes_out(0).rearrange("(k q) t -> q k t", q=QUADRANT)
                 for g in (0, 2, 1, 3):
-                    codes = y_codes[a][QUADRANT * g : QUADRANT * (g + 1), :].rearrange("q (w c) -> q w c", w=TILES_A_PASS)
-                    queues[g // 2].dma_start(out=codes_out[:, held, g * BANK : (g + 1) * BANK], in_=codes[:, held, :])
-            if w == TILES_A_PASS - 1:
+                    codes = plain_codes[QUADRANT * g : QUADRANT * (g + 1), :].rearrange("q (k c) -> q k c", k=TILES_A_PASS)
+                    nc.sync.dma_start(out=by_page[:, held, g * BANK : (g + 1) * BANK], in_=codes[:, held, :])
+            if k == TILES_A_PASS - 1:
                 for g in range(GROUPS):
-                    queues[g // 2].dma_start(
-                        out=out_2[a, :, g * BANK : (g + 1) * BANK].bitcast(I32),
-                        in_=y_scales[a][QUADRANT * g : QUADRANT * g + SCALE_ROWS * TILES_A_PASS, :].bitcast(I32),
+                    nc.sync.dma_start(
+                        out=out_2[0, :, g * BANK : (g + 1) * BANK].bitcast(I32),
+                        in_=plain_scales[QUADRANT * g : QUADRANT * g + SCALE_ROWS * TILES_A_PASS, :].bitcast(I32),
                     )
 
-        def weave(k, cols, copy, doubled=False):
+        woven_columns = woven[:].rearrange("p (c t) -> p c t", t=PACK)
+
+        def weave(k, cols, copy):
+            copy(out=woven_columns[:, cols, k - TILES_A_PASS], in_=pages[k % len(pages)][:, cols])
+
+        def weave_twice(k):
             t = k - TILES_A_PASS
-            page = pages[k % len(pages)][:, cols]
-            by_column = woven[:].rearrange("p (c t) -> p c t", t=PACK)
-            if doubled:
-                copy(out=by_column[:, cols, t : t + 2], in_=page.unsqueeze(2).to_broadcast([P, cols.stop - cols.start, 2]))
-            else:
-                copy(out=by_column[:, cols, t], in_=page)
+            page = pages[k % len(pages)][:]
+            nc.scalar.copy(out=woven_columns[:, :, t : t + 2], in_=page.unsqueeze(2).to_broadcast([P, T, 2]))
 
         def quantise_woven(cols):
             nc.vector.quantize_mx(
-                out=y_codes[1][:, cols].bitcast(FP8X4),
+                out=woven_codes[:, cols].bitcast(FP8X4),
                 scales=woven_scales[:, cols],
                 in_=woven[:, PACK * cols.start : PACK * cols.stop],
             )
-
-        def store_woven(cols, queue):
-            queue.dma_start(out=out_1[1].rearrange("p t b -> p (t b)").bitcast(I32)[:, cols], in_=y_codes[1][:, cols])
+            nc.sync.dma_start(out=codes_out(1)[:, cols], in_=woven_codes[:, cols])
 
         make_identity(nc, ident[:])
         nc.vector.memset(bn_rows[0:ROWS_FROM, :], 0.0)
@@ -356,8 +354,8 @@ def tile_list_tgn_rnnP_kernel(
         nc.sync.dma_start(offsets[:], offs)
         nc.sync.dma_start(out=tab_s[SCALES_FROM:P, :].bitcast(I32), in_=tab_scales.bitcast(I32).rearrange("a q t -> q a t"))
         table = tab_words[0].rearrange("p t b -> p (t b)").bitcast(I32)
-        nc.sync.dma_start(out=bn_rows[ROWS_FROM : P - TILES, :], in_=bn[0:K_PASS].rearrange("(i p) -> i p", p=P))
-        nc.sync.dma_start(out=bn_rows[P - TILES : P, :], in_=wgo[0].rearrange("(i p) -> i p", p=P))
+        nc.sync.dma_start(out=bn_rows[ROWS_FROM:WGO_FROM, :], in_=bn[0:K_PASS].rearrange("(i p) -> i p", p=P))
+        nc.sync.dma_start(out=bn_rows[WGO_FROM:P, :], in_=wgo[0].rearrange("(i p) -> i p", p=P))
         nc.sync.dma_start(out=tab_w[:], in_=table)
         nc.vector.memset(planes_s[:].bitcast(I32), 0)
         for page in pages:
@@ -366,8 +364,8 @@ def tile_list_tgn_rnnP_kernel(
         load_x(0)
         load_x(1)
         nc.vector.tensor_copy(picked_s[:], tab_s[:].indirect(offsets[:]))
+        rows = PASSES * SCALE_ROWS
         for quadrant in range(QUADRANTS):
-            rows = PASSES * SCALE_ROWS
             nc.sync.dma_start(
                 out=planes_s[QUADRANT * quadrant : QUADRANT * quadrant + SCALE_ROWS, :]
                 .bitcast(I32)
@@ -387,17 +385,17 @@ def tile_list_tgn_rnnP_kernel(
             in_=picked_w[:].bitcast(U16).rearrange("p (j d) -> p d j", d=PASSES),
         )
 
-        nc.tensor.transpose(banks[2][:, 0:P], bn_rows[:], ident[:])
-        wgo_cols = w_bf[:].bitcast(F32)[:, BANK : BANK + TILES]
-        nc.scalar.copy(out=wgo_cols, in_=banks[2][:, P - TILES : P])
-        nc.scalar.copy(out=bias[:], in_=banks[2][:, ROWS_FROM : P - TILES])
+        nc.tensor.transpose(word_banks[0][:, 0:P], bn_rows[:], ident[:])
+        wgo_cols = w_bf[:].bitcast(F32)[:, BANK : BANK + J // P]
+        nc.scalar.copy(out=wgo_cols, in_=word_banks[0][:, WGO_FROM:P])
+        nc.scalar.copy(out=bias[:], in_=word_banks[0][:, ROWS_FROM:WGO_FROM])
         for h in range(HALVES):
             for b in range(BLOCKS):
                 column = BLOCKS * h + b
                 nc.tensor.transpose(
-                    banks[h][:, b * P : (b + 1) * P], wgo_cols[:, column : column + 1].to_broadcast([P, P]), ident[:]
+                    sum_banks[h][:, b * P : (b + 1) * P], wgo_cols[:, column : column + 1].to_broadcast([P, P]), ident[:]
                 )
-            nc.scalar.copy(out=weight[:, h * BANK : (h + 1) * BANK], in_=banks[h][:])
+            nc.scalar.copy(out=weight[:, h * BANK : (h + 1) * BANK], in_=sum_banks[h][:])
 
         for step in range(2):
             round_w(0, 2, step)
@@ -416,55 +414,54 @@ def tile_list_tgn_rnnP_kernel(
             round_next[0]()
             quantise_next[0]()
             round_next[1]()
-            product(0, q * QUARTER, QUARTER, banks[4 + q % 2])
-            activate(0, q * QUARTER, QUARTER, banks[4 + q % 2])
+            product(0, q * QUARTER, QUARTER, turn_banks[q % 2])
+            activate(0, q * QUARTER, QUARTER, turn_banks[q % 2])
             gather_add(0, q * QUARTER, QUARTER)
             quantise_next[1]()
             scatter(0, q * QUARTER, QUARTER)
         load_h(2)
-        for i in range(3):
+        for i in range(OPERANDS - 1):
             load_dealt(i)
         nc.sync.dma_start(out=dealt_bias[:], in_=bn[K_PASS:N].rearrange("(p t) -> p t", t=PACK))
         store_page(0)
 
         for q in range(2):
-            product(1, q * QUARTER, QUARTER, banks[q])
-            activate(1, q * QUARTER, QUARTER, banks[q])
+            product(1, q * QUARTER, QUARTER, sum_banks[q])
+            activate(1, q * QUARTER, QUARTER, sum_banks[q])
             gather_add(1, q * QUARTER, QUARTER)
         scatter(1, 0, BANK)
-        product(1, BANK, BANK, banks[1])
-        activate(1, BANK, BANK, banks[1])
+        product(1, BANK, BANK, sum_banks[1])
+        activate(1, BANK, BANK, sum_banks[1])
         round_w(2, 2, 0)
         quantise_w(2, 2, 0)
         round_w(2, 2, 1)
         gather_add(1, BANK, BANK)
-        load_dealt(3)
+        load_dealt(OPERANDS - 1)
         load_h(3)
         quantise_w(2, 2, 1)
         scatter(1, BANK, BANK)
         store_page(1)
 
-        for step in range(2):
-            round_w(3, 2, step)
-            quantise_w(3, 2, step)
+        round_w(3, 1, 0)
+        quantise_w(3, 1, 0)
         multiply(2)
         gather_add(2, 0, J)
         load_h(4)
         scatter(2, 0, J)
         store_page(2)
 
-        for i in range(3):
+        for i in range(OPERANDS - 1):
             round_dealt(i)
             quantise_dealt(i)
         multiply(3)
-        round_dealt(3)
+        round_dealt(OPERANDS - 1)
         gather_add(3, 0, J)
         load_h(5)
-        quantise_dealt(3)
-        turn(0, banks[4:8], [copy_s] * BLOCKS)
+        quantise_dealt(OPERANDS - 1)
+        turn(0)
         scatter(3, 0, J)
         store_page(3)
-        turn(1, banks[4:8], [copy_s] * BLOCKS)
+        turn(1)
 
         last = TILES - 1
         for k in range(TILES_A_PASS, TILES):
@@ -472,22 +469,25 @@ def tile_list_tgn_rnnP_kernel(
             gather_add(k, 0, J)
             if k + 2 < TILES:
                 load_h(k + 2)
-            turn_words(k - TILES_A_PASS, banks[2:4], [copy_s] * 2)
-            quantise_y(k - TILES_A_PASS, HALVES, both_sync, range(HALVES))
+            turn_words(k - TILES_A_PASS)
+            quantise_plain(k - TILES_A_PASS)
             if k == last:
-                weave(last - 3, slice(0, T), copy_s)
+                weave(last - len(pages), slice(0, T), copy_s)
             scatter(k, 0, J)
             store_page(k)
             if k - 2 < TILES_A_PASS:
-                turn(k - 2, banks[4:8], [copy_s] * BLOCKS)
+                turn(k - 2)
         weave(last - 2, slice(0, T), copy_s)
-        weave(last - 1, slice(0, T), copy_s, doubled=True)
-        groups = [slice(g * BANK, (g + 1) * BANK) for g in range(GROUPS)]
-        for g in range(GROUPS):
-            weave(last, groups[g], copy_v if g < 2 else copy_s)
-        for g in range(GROUPS):
-            quantise_woven(groups[g])
-            store_woven(groups[g], nc.sync)
+        weave_twice(last - 1)
+        pieces = [slice(first, end) for first, end in zip(WOVEN_EDGES, WOVEN_EDGES[1:])]
+        first_piece, shared_piece, *scalar_pieces = pieces
+        weave(last, first_piece, copy_v)
+        weave(last, slice(shared_piece.start, VECTOR_WEAVES), copy_v)
+        weave(last, slice(VECTOR_WEAVES, shared_piece.stop), copy_s)
+        for cols in scalar_pieces:
+            weave(last, cols, copy_s)
+        for cols in pieces:
+            quantise_woven(cols)
         for quadrant in range(QUADRANTS):
             nc.sync.dma_start(
                 out=out_2[1, SCALE_ROWS * quadrant : SCALE_ROWS * (quadrant + 1), :].bitcast(I32),

@@ -34,7 +34,8 @@ SCALE_ROWS = 4
 LIST_ROWS = 16
 QUARTERS = 4
 QUARTER = J // QUARTERS
-RAW_START = 640
+PAGES = 3
+W1_STEP = 2
 ROWS_FROM = P - J // P - TILES_A_PASS
 WGO_FROM = P - J // P
 SCALES_FROM = P - QUADRANT
@@ -70,7 +71,7 @@ def tile_list_tgn_rnnP_kernel(
         weight = keep.tile([P, J], F32, name="weight", align_bytes=64)
         x_half = tiles(PASSES, [P, PACK * BANK], F32, "x_half")
         x_rest = tiles(2, [P, PACK * BANK], F32, "x_rest")
-        dealt_raw = [x_half[1], x_rest[0], x_rest[1], x_half[0]]
+        dealt_raw = [x_half[0], x_half[1], x_rest[0], x_rest[1]]
         dealt_codes = tiles(OPERANDS, [P, BANK], U32, "dealt_codes")
         dealt_scales = tiles(OPERANDS, [P, BANK], U8, "dealt_scales")
         woven = keep.tile([P, PACK * T], BF16, name="woven", align_bytes=64)
@@ -78,13 +79,17 @@ def tile_list_tgn_rnnP_kernel(
         x_codes = tiles(PASSES, [P, J], U32, "x_codes")
         x_scales = tiles(PASSES, [P, J], U8, "x_scales")
         slots = tiles(3, [P, 3 * J], F32, "slots")
-        w_raw = [slot[:, RAW_START : RAW_START + PACK * BANK] for slot in slots]
+        wn_raw = [slot[:, J : 2 * J] for slot in slots]
+        un_raw = [slot[:, 2 * J : 3 * J] for slot in slots]
         w_bf = keep.tile([P, PACK * BANK], BF16, name="w_bf", align_bytes=64)
         w_codes = tiles(3, [P, BANK], U32, "w_codes")
         w_scales = tiles(3, [P, BANK], U8, "w_scales")
-        h_rows = tiles(2, [P, T], F32, "h_rows")
+        h_rows = tiles(3, [P, T], F32, "h_rows")
         summed = tiles(2, [P, J], F32, "summed")
-        pages = tiles(3, [P, T], F32, "pages")
+        pages = tiles(2, [P, T], F32, "pages")
+        first_staged = keep.tile([P, PACK * QUARTER], BF16, name="first_staged", align_bytes=64)
+        late_staged = keep.tile([P, PACK * QUARTER], BF16, name="late_staged", tag="late_page", align_bytes=64)
+        early_tanh = keep.tile([P, 2 * (J - QUARTER)], F32, name="early_tanh", align_bytes=64)
         plain_codes, woven_codes = tiles(PASSES, [P, T], I32, "y_codes")
         woven_scales = keep.tile([P, T], U8, name="woven_scales", align_bytes=64)
         plain_scales = keep.tile([P, BANK], U8, name="y_scales0", align_bytes=64)
@@ -105,7 +110,12 @@ def tile_list_tgn_rnnP_kernel(
             )
 
         def head_buffer(step, piece):
+            if step == 0 and piece == 1:
+                return first_staged
             return x_bf[(PASSES * step + piece) % len(x_bf)]
+
+        def x_step(q):
+            return q if q < W1_STEP else q + 1
 
         def x_raw(q, a):
             if q < 2:
@@ -117,20 +127,20 @@ def tile_list_tgn_rnnP_kernel(
                 nc.sync.dma_start(out=x_raw(q, a), in_=pass_rows(x, a, slice(q * QUARTER, (q + 1) * QUARTER)))
 
         def round_x(q, a):
-            interleave(head_buffer(q, a)[:], x_raw(q, a), copy_v if q == 0 else copy_s)
+            interleave(head_buffer(x_step(q), a)[:], x_raw(q, a), copy_v if (q, a) == (0, 1) else copy_s)
 
         def quantise_x(q, a):
             cols = slice(q * QUARTER, (q + 1) * QUARTER)
             nc.vector.quantize_mx(
-                out=x_codes[a][:, cols].bitcast(FP8X4), scales=x_scales[a][:, cols], in_=head_buffer(q, a)[:]
+                out=x_codes[a][:, cols].bitcast(FP8X4), scales=x_scales[a][:, cols], in_=head_buffer(x_step(q), a)[:]
             )
 
         def load_w(k):
-            raw = by_row(w_raw[k % len(w_raw)])
             for operand in OPERAND_ORDER:
                 source = (wn, un)[operand // PASSES]
+                raw = by_row((wn_raw, un_raw)[operand // PASSES][k % len(slots)])
                 nc.sync.dma_start(
-                    out=raw[:, :, operand * P : (operand + 1) * P],
+                    out=raw[:, :, operand % PASSES * P : (operand % PASSES + 1) * P],
                     in_=pass_rows(source, operand % PASSES, slice(k * P, (k + 1) * P)),
                 )
 
@@ -138,12 +148,14 @@ def tile_list_tgn_rnnP_kernel(
             width = BANK // pieces
             first = (step + pieces // 2) % pieces * width
             if k == 1:
-                return slice(first, first + width), head_buffer(QUARTERS, step)[:]
+                return slice(first, first + width), head_buffer(W1_STEP, step)[:]
+            if k == 2 and step == 1:
+                return slice(first, first + width), late_staged[:]
             return slice(first, first + width), w_bf[:, PACK * first : PACK * (first + width)]
 
         def round_w(k, pieces, step):
-            cols, staged = w_piece(k, pieces, step)
-            interleave(staged, by_row(w_raw[k % len(w_raw)])[:, :, cols])
+            staged = w_piece(k, pieces, step)[1]
+            interleave(staged, by_row((un_raw, wn_raw)[step][k % len(slots)]))
 
         def quantise_w(k, pieces, step):
             cols, staged = w_piece(k, pieces, step)
@@ -164,8 +176,10 @@ def tile_list_tgn_rnnP_kernel(
             nc.sync.dma_start(out=by_row(dealt_raw[i][:]), in_=pass_rows(source, operand % PASSES, slice(K_PASS, N)))
 
         def dealt_staged(i):
-            if i < 2:
-                return slots[0][:, (i + 1) * J : (i + 2) * J].bitcast(BF16)
+            if i == 0:
+                return slots[0][:, 0:J].bitcast(BF16)
+            if i == 1:
+                return early_tanh[:, 0:J].bitcast(BF16)
             return dealt_raw[i - 2][:, 0:J].bitcast(BF16)
 
         def round_dealt(i):
@@ -188,20 +202,18 @@ def tile_list_tgn_rnnP_kernel(
             return dealt_codes[operand][:, cols], dealt_scales[operand][:, cols]
 
         def load_h(k):
-            nc.sync.dma_start(out=h_rows[k % 2][:], in_=tile_rows(hT, k))
+            nc.sync.dma_start(out=h_rows[k % len(h_rows)][:], in_=tile_rows(hT, k))
 
         def tanh_part(k, first, count):
-            if k == 0 and first < J - QUARTER:
-                return x_raw(first // QUARTER + 1, 0)[:, 0, :]
-            if k == 0:
-                return w_raw[1][:, count : 2 * count]
-            if k == 1 and first < BANK:
-                place = BANK if first == 0 else 0
-                return w_bf[:].bitcast(F32)[:, place : place + count]
-            if k == 1:
-                return x_half[0][:, BANK : BANK + count]
+            if k == 0 and first == QUARTER:
+                return wn_raw[1][:, 0:count]
+            if k < 2 and first < J - QUARTER:
+                place = k * (J - QUARTER) + first
+                return early_tanh[:, place : place + count]
+            if k < 2:
+                return wn_raw[2][:, k * count : (k + 1) * count]
             if k == 2:
-                return slots[0][:, first : first + count]
+                return un_raw[0][:, first : first + count]
             if k == 3:
                 return dealt_raw[1][:, J + first : J + first + count]
             return slots[1 + k % 2][:, first : first + count]
@@ -250,12 +262,10 @@ def tile_list_tgn_rnnP_kernel(
             return offsets[:, first // LIST_ROWS : (first + count) // LIST_ROWS]
 
         def sum_part(k, first, count):
-            if k == 0 and first < J - QUARTER:
+            if k == 1 and QUARTER <= first < J - QUARTER:
                 return x_raw(first // QUARTER + 1, 1)[:, 0, :]
-            if k == 0:
-                return w_raw[1][:, 0:count]
-            if k == 1 and first == BANK:
-                return w_raw[2][:, 0:count]
+            if k == 2:
+                return wn_raw[0][:, first : first + count]
             if k == 3:
                 return dealt_raw[3][:, first : first + count]
             return summed[k % 2][:, first : first + count]
@@ -263,29 +273,37 @@ def tile_list_tgn_rnnP_kernel(
         def gather_add(k, first, count):
             nc.vector.tensor_tensor(
                 out=sum_part(k, first, count),
-                in0=h_rows[k % 2][:].indirect(list_part(first, count)),
+                in0=h_rows[k % len(h_rows)][:].indirect(list_part(first, count)),
                 in1=tanh_part(k, first, count),
+                op=ALU.add,
+            )
+
+        def add_picked(first, count):
+            nc.vector.tensor_tensor(
+                out=sum_part(0, first, count),
+                in0=summed[0][:, first : first + count],
+                in1=tanh_part(0, first, count),
                 op=ALU.add,
             )
 
         def scatter(k, first, count):
             cols = slice(first, first + count)
             nc.vector.tensor_tensor(
-                out=pages[k % len(pages)][:].indirect(list_part(first, count)),
+                out=pages[k % PAGES][:].indirect(list_part(first, count)),
                 in0=sum_part(k, first, count),
                 in1=weight[:, cols],
                 op=ALU.mult,
             )
 
         def store_page(k):
-            nc.sync.dma_start(out=tile_rows(out_0, k), in_=pages[k % len(pages)][:])
+            nc.sync.dma_start(out=tile_rows(out_0, k), in_=pages[k % PAGES][:])
 
         def turn(k):
             for b in range(BLOCKS):
-                bank = turn_banks[b]
+                bank = sum_banks[-1] if k > 0 and b == BLOCKS - 1 else turn_banks[b]
                 for g in range(GROUPS):
                     first = g * BANK + b * P
-                    nc.tensor.transpose(bank[:, g * P : (g + 1) * P], pages[k % len(pages)][:, first : first + P], ident[:])
+                    nc.tensor.transpose(bank[:, g * P : (g + 1) * P], pages[k % PAGES][:, first : first + P], ident[:])
                 nc.scalar.copy(
                     out=turned(k)[:, b * BANK : (b + 1) * BANK].rearrange("p (u r e) -> p u r e", u=2, e=2),
                     in_=bank[:].rearrange("p (r u e) -> p u r e", u=2, e=2),
@@ -296,8 +314,8 @@ def tile_list_tgn_rnnP_kernel(
 
         def turn_words(k):
             words = turned(k).bitcast(F32)
-            span = BLOCKS // len(word_banks)
-            for i, bank in enumerate(word_banks):
+            span = BLOCKS // len(sum_banks)
+            for i, bank in enumerate(sum_banks):
                 for s in range(2 * span):
                     first = (2 * span * i + s) * P
                     nc.tensor.transpose(bank[:, s * P : (s + 1) * P], words[:, first : first + P], ident[:])
@@ -332,11 +350,11 @@ def tile_list_tgn_rnnP_kernel(
         woven_columns = woven[:].rearrange("p (c t) -> p c t", t=PACK)
 
         def weave(k, cols, copy):
-            copy(out=woven_columns[:, cols, k - TILES_A_PASS], in_=pages[k % len(pages)][:, cols])
+            copy(out=woven_columns[:, cols, k - TILES_A_PASS], in_=pages[k % PAGES][:, cols])
 
         def weave_twice(k):
             t = k - TILES_A_PASS
-            page = pages[k % len(pages)][:]
+            page = pages[k % PAGES][:]
             nc.scalar.copy(out=woven_columns[:, :, t : t + 2], in_=page.unsqueeze(2).to_broadcast([P, T, 2]))
 
         def quantise_woven(cols):
@@ -347,9 +365,9 @@ def tile_list_tgn_rnnP_kernel(
             )
             nc.sync.dma_start(out=codes_out(1)[:, cols], in_=woven_codes[:, cols])
 
+        nc.gpsimd.memset(tab_s[0:SCALES_FROM, :].bitcast(I32), 0)
+        nc.gpsimd.memset(bn_rows[0:ROWS_FROM, :], 0.0)
         make_identity(nc, ident[:])
-        nc.vector.memset(bn_rows[0:ROWS_FROM, :], 0.0)
-        nc.vector.memset(tab_s[0:SCALES_FROM, :].bitcast(I32), 0)
         nc.scalar.activation(out=bias[0:ROWS_FROM, 0:1], in_=bn_rows[0:ROWS_FROM, 0:1], func=ACT.Tanh)
         nc.sync.dma_start(offsets[:], offs)
         nc.sync.dma_start(out=tab_s[SCALES_FROM:P, :].bitcast(I32), in_=tab_scales.bitcast(I32).rearrange("a q t -> q a t"))
@@ -357,33 +375,35 @@ def tile_list_tgn_rnnP_kernel(
         nc.sync.dma_start(out=bn_rows[ROWS_FROM:WGO_FROM, :], in_=bn[0:K_PASS].rearrange("(i p) -> i p", p=P))
         nc.sync.dma_start(out=bn_rows[WGO_FROM:P, :], in_=wgo[0].rearrange("(i p) -> i p", p=P))
         nc.sync.dma_start(out=tab_w[:], in_=table)
-        nc.vector.memset(planes_s[:].bitcast(I32), 0)
+        nc.gpsimd.memset(planes_s[:].bitcast(I32), 0)
         for page in pages:
             nc.gpsimd.memset(page[:], 0.0)
+        load_h(0)
         load_w(0)
-        load_x(0)
-        load_x(1)
         nc.vector.tensor_copy(picked_s[:], tab_s[:].indirect(offsets[:]))
         rows = PASSES * SCALE_ROWS
-        for quadrant in range(QUADRANTS):
+        for quadrant in (0, 2, 1, 3):
             nc.sync.dma_start(
                 out=planes_s[QUADRANT * quadrant : QUADRANT * quadrant + SCALE_ROWS, :]
                 .bitcast(I32)
                 .rearrange("r (a j) -> r a j", a=PASSES),
                 in_=picked_s[SCALES_FROM + rows * quadrant : SCALES_FROM + rows * (quadrant + 1), :].bitcast(I32),
             )
-        load_h(0)
-        load_x(2)
-        load_x(3)
+        load_x(0)
+        load_x(1)
         load_w(1)
         load_h(1)
+        load_x(2)
+        load_x(3)
         load_w(2)
+        load_h(2)
 
         nc.vector.tensor_copy(picked_w[:], tab_w[:].bitcast(U32).indirect(offsets[:]))
         nc.vector.tensor_copy(
             out=parted_w[:].bitcast(U16).rearrange("p (d j) -> p d j", d=PASSES),
             in_=picked_w[:].bitcast(U16).rearrange("p (j d) -> p d j", d=PASSES),
         )
+        nc.vector.tensor_copy(summed[0][:], h_rows[0][:].indirect(offsets[:]))
 
         nc.tensor.transpose(word_banks[0][:, 0:P], bn_rows[:], ident[:])
         wgo_cols = w_bf[:].bitcast(F32)[:, BANK : BANK + J // P]
@@ -403,50 +423,66 @@ def tile_list_tgn_rnnP_kernel(
         for a in range(PASSES):
             round_x(0, a)
             quantise_x(0, a)
+
+        def quarter_tanh(k, q):
+            bank = turn_banks[2 * k + q % 2]
+            product(k, q * QUARTER, QUARTER, bank)
+            activate(k, q * QUARTER, QUARTER, bank)
+
+        quarter_tanh(0, 0)
+        add_picked(0, QUARTER)
+        scatter(0, 0, QUARTER)
+        for a in range(PASSES):
+            round_x(1, a)
+            quantise_x(1, a)
         load_w(3)
-        for q in range(QUARTERS):
-            if q + 1 < QUARTERS:
-                round_next = [lambda a=a: round_x(q + 1, a) for a in range(PASSES)]
-                quantise_next = [lambda a=a: quantise_x(q + 1, a) for a in range(PASSES)]
-            else:
-                round_next = [lambda a=a: round_w(1, 2, a) for a in range(PASSES)]
-                quantise_next = [lambda a=a: quantise_w(1, 2, a) for a in range(PASSES)]
-            round_next[0]()
-            quantise_next[0]()
-            round_next[1]()
-            product(0, q * QUARTER, QUARTER, turn_banks[q % 2])
-            activate(0, q * QUARTER, QUARTER, turn_banks[q % 2])
-            gather_add(0, q * QUARTER, QUARTER)
-            quantise_next[1]()
-            scatter(0, q * QUARTER, QUARTER)
-        load_h(2)
-        for i in range(OPERANDS - 1):
-            load_dealt(i)
-        nc.sync.dma_start(out=dealt_bias[:], in_=bn[K_PASS:N].rearrange("(p t) -> p t", t=PACK))
-        store_page(0)
-
-        for q in range(2):
-            product(1, q * QUARTER, QUARTER, sum_banks[q])
-            activate(1, q * QUARTER, QUARTER, sum_banks[q])
-            gather_add(1, q * QUARTER, QUARTER)
-        scatter(1, 0, BANK)
-        product(1, BANK, BANK, sum_banks[1])
-        activate(1, BANK, BANK, sum_banks[1])
-        round_w(2, 2, 0)
-        quantise_w(2, 2, 0)
-        round_w(2, 2, 1)
-        gather_add(1, BANK, BANK)
-        load_dealt(OPERANDS - 1)
+        load_dealt(0)
+        load_dealt(1)
         load_h(3)
-        quantise_w(2, 2, 1)
-        scatter(1, BANK, BANK)
-        store_page(1)
-
-        round_w(3, 1, 0)
-        quantise_w(3, 1, 0)
-        multiply(2)
-        gather_add(2, 0, J)
+        nc.sync.dma_start(out=dealt_bias[:], in_=bn[K_PASS:N].rearrange("(p t) -> p t", t=PACK))
+        for step in range(2):
+            round_w(1, 2, step)
+            quantise_w(1, 2, step)
+        quarter_tanh(0, 1)
+        add_picked(QUARTER, QUARTER)
+        scatter(0, QUARTER, QUARTER)
+        quarter_tanh(1, 0)
+        gather_add(1, 0, QUARTER)
+        scatter(1, 0, QUARTER)
+        for q in (1, 2):
+            round_x(q + 1, 0)
+            quantise_x(q + 1, 0)
+            if q == 2:
+                quarter_tanh(0, q)
+                add_picked(q * QUARTER, QUARTER)
+                scatter(0, q * QUARTER, QUARTER)
+            round_x(q + 1, 1)
+            quarter_tanh(1, q)
+            gather_add(1, q * QUARTER, QUARTER)
+            quantise_x(q + 1, 1)
+            scatter(1, q * QUARTER, QUARTER)
+            load_dealt(q + 1)
+        for step in range(2):
+            round_w(2, 2, step)
+            quantise_w(2, 2, step)
+        pages.append(keep.tile([P, T], F32, name="pages2", tag="late_page", align_bytes=64))
+        nc.gpsimd.memset(pages[2][:], 0.0)
+        end = J - QUARTER
+        quarter_tanh(0, QUARTERS - 1)
+        quarter_tanh(1, QUARTERS - 1)
+        add_picked(end, QUARTER)
+        gather_add(1, end, QUARTER)
+        for k in range(2):
+            scatter(k, end, QUARTER)
+            store_page(k)
         load_h(4)
+
+        round_w(3, 2, 0)
+        multiply(2)
+        round_w(3, 2, 1)
+        gather_add(2, 0, J)
+        load_h(5)
+        quantise_w(3, 1, 0)
         scatter(2, 0, J)
         store_page(2)
 
@@ -456,27 +492,26 @@ def tile_list_tgn_rnnP_kernel(
         multiply(3)
         round_dealt(OPERANDS - 1)
         gather_add(3, 0, J)
-        load_h(5)
+        load_h(6)
         quantise_dealt(OPERANDS - 1)
         turn(0)
         scatter(3, 0, J)
         store_page(3)
-        turn(1)
 
         last = TILES - 1
         for k in range(TILES_A_PASS, TILES):
             multiply(k)
             gather_add(k, 0, J)
-            if k + 2 < TILES:
-                load_h(k + 2)
+            if k + len(h_rows) < TILES:
+                load_h(k + len(h_rows))
             turn_words(k - TILES_A_PASS)
             quantise_plain(k - TILES_A_PASS)
             if k == last:
-                weave(last - len(pages), slice(0, T), copy_s)
+                weave(last - PAGES, slice(0, T), copy_s)
+            else:
+                turn(k - PAGES)
             scatter(k, 0, J)
             store_page(k)
-            if k - 2 < TILES_A_PASS:
-                turn(k - 2)
         weave(last - 2, slice(0, T), copy_s)
         weave_twice(last - 1)
         pieces = [slice(first, end) for first, end in zip(WOVEN_EDGES, WOVEN_EDGES[1:])]

@@ -86,9 +86,12 @@ def tile_list_tgn_rnnP_kernel(
         w_scales = tiles(3, [P, BANK], U8, "w_scales")
         h_rows = tiles(3, [P, T], F32, "h_rows")
         summed = tiles(2, [P, J], F32, "summed")
-        pages = tiles(2, [P, T], F32, "pages")
+        pages = tiles(1, [P, T], F32, "pages")
         first_staged = keep.tile([P, PACK * QUARTER], BF16, name="first_staged", align_bytes=64)
-        late_staged = keep.tile([P, PACK * QUARTER], BF16, name="late_staged", tag="late_page", align_bytes=64)
+        late_staged = {
+            k: keep.tile([P, PACK * QUARTER], BF16, name="late_staged" + str(k), tag="page" + str(k), align_bytes=64)
+            for k in (1, 2)
+        }
         early_tanh = keep.tile([P, 2 * (J - QUARTER)], F32, name="early_tanh", align_bytes=64)
         plain_codes, woven_codes = tiles(PASSES, [P, T], I32, "y_codes")
         woven_scales = keep.tile([P, T], U8, name="woven_scales", align_bytes=64)
@@ -147,10 +150,10 @@ def tile_list_tgn_rnnP_kernel(
         def w_piece(k, pieces, step):
             width = BANK // pieces
             first = (step + pieces // 2) % pieces * width
+            if k in late_staged and step == 1:
+                return slice(first, first + width), late_staged[k][:]
             if k == 1:
                 return slice(first, first + width), head_buffer(W1_STEP, step)[:]
-            if k == 2 and step == 1:
-                return slice(first, first + width), late_staged[:]
             return slice(first, first + width), w_bf[:, PACK * first : PACK * (first + width)]
 
         def round_w(k, pieces, step):
@@ -295,6 +298,11 @@ def tile_list_tgn_rnnP_kernel(
                 op=ALU.mult,
             )
 
+        def add_page():
+            name = "page" + str(len(pages))
+            pages.append(keep.tile([P, T], F32, name=name, tag=name, align_bytes=64))
+            nc.gpsimd.memset(pages[-1][:], 0.0)
+
         def store_page(k):
             nc.sync.dma_start(out=tile_rows(out_0, k), in_=pages[k % PAGES][:])
 
@@ -365,9 +373,9 @@ def tile_list_tgn_rnnP_kernel(
             )
             nc.sync.dma_start(out=codes_out(1)[:, cols], in_=woven_codes[:, cols])
 
-        nc.gpsimd.memset(tab_s[0:SCALES_FROM, :].bitcast(I32), 0)
-        nc.gpsimd.memset(bn_rows[0:ROWS_FROM, :], 0.0)
         make_identity(nc, ident[:])
+        nc.vector.memset(bn_rows[0:ROWS_FROM, :], 0.0)
+        nc.vector.memset(tab_s[0:SCALES_FROM, :].bitcast(I32), 0)
         nc.scalar.activation(out=bias[0:ROWS_FROM, 0:1], in_=bn_rows[0:ROWS_FROM, 0:1], func=ACT.Tanh)
         nc.sync.dma_start(offsets[:], offs)
         nc.sync.dma_start(out=tab_s[SCALES_FROM:P, :].bitcast(I32), in_=tab_scales.bitcast(I32).rearrange("a q t -> q a t"))
@@ -375,9 +383,8 @@ def tile_list_tgn_rnnP_kernel(
         nc.sync.dma_start(out=bn_rows[ROWS_FROM:WGO_FROM, :], in_=bn[0:K_PASS].rearrange("(i p) -> i p", p=P))
         nc.sync.dma_start(out=bn_rows[WGO_FROM:P, :], in_=wgo[0].rearrange("(i p) -> i p", p=P))
         nc.sync.dma_start(out=tab_w[:], in_=table)
-        nc.gpsimd.memset(planes_s[:].bitcast(I32), 0)
-        for page in pages:
-            nc.gpsimd.memset(page[:], 0.0)
+        nc.vector.memset(planes_s[:].bitcast(I32), 0)
+        nc.vector.memset(pages[0][:], 0.0)
         load_h(0)
         load_w(0)
         nc.vector.tensor_copy(picked_s[:], tab_s[:].indirect(offsets[:]))
@@ -443,6 +450,7 @@ def tile_list_tgn_rnnP_kernel(
         for step in range(2):
             round_w(1, 2, step)
             quantise_w(1, 2, step)
+        add_page()
         quarter_tanh(0, 1)
         add_picked(QUARTER, QUARTER)
         scatter(0, QUARTER, QUARTER)
@@ -465,8 +473,7 @@ def tile_list_tgn_rnnP_kernel(
         for step in range(2):
             round_w(2, 2, step)
             quantise_w(2, 2, step)
-        pages.append(keep.tile([P, T], F32, name="pages2", tag="late_page", align_bytes=64))
-        nc.gpsimd.memset(pages[2][:], 0.0)
+        add_page()
         end = J - QUARTER
         quarter_tanh(0, QUARTERS - 1)
         quarter_tanh(1, QUARTERS - 1)

@@ -41,6 +41,7 @@ WGO_FROM = P - J // P
 SCALES_FROM = P - QUADRANT
 RUN = 4
 OPERAND_ORDER = (2, 3, 0, 1)
+DEALT_ELEMENT = (2, 0, 1, 3)
 PAGES_A_STORE = 2
 VECTOR_WEAVES = 2 * BANK - P
 WOVEN_EDGES = (0, BANK, 2 * BANK, 3 * BANK, T - BANK // 2, T)
@@ -87,7 +88,6 @@ def tile_list_tgn_rnnP_kernel(
         h_rows = tiles(3, [P, T], F32, "h_rows")
         summed = tiles(2, [P, J], F32, "summed")
         pages = tiles(1, [P, T], F32, "pages")
-        first_staged = keep.tile([P, PACK * QUARTER], BF16, name="first_staged", align_bytes=64)
         late_staged = {
             k: keep.tile([P, PACK * QUARTER], BF16, name="late_staged" + str(k), tag="page" + str(k), align_bytes=64)
             for k in (1, 2)
@@ -96,9 +96,9 @@ def tile_list_tgn_rnnP_kernel(
         plain_codes, woven_codes = tiles(PASSES, [P, T], I32, "y_codes")
         woven_scales = keep.tile([P, T], U8, name="woven_scales", align_bytes=64)
         plain_scales = keep.tile([P, BANK], U8, name="y_scales0", align_bytes=64)
-        banks = [psum.tile([P, BANK], F32, name="bank" + str(i)) for i in range(8)]
+        banks = [psum.tile([P, BANK], F32, name="bank" + str(i)) for i in range(HALVES + 1 + BLOCKS)]
         copy_s, copy_v = nc.scalar.copy, nc.vector.tensor_copy
-        sum_banks, word_banks, turn_banks = banks[0:2], banks[2:4], banks[4:8]
+        sum_banks, rows_bank, turn_banks = banks[0:HALVES], banks[HALVES], banks[HALVES + 1 :]
 
         def by_row(flat):
             return flat.rearrange("p (t c) -> p t c", t=PACK)
@@ -113,8 +113,6 @@ def tile_list_tgn_rnnP_kernel(
             )
 
         def head_buffer(step, piece):
-            if step == 0 and piece == 1:
-                return first_staged
             return x_bf[(PASSES * step + piece) % len(x_bf)]
 
         def x_step(q):
@@ -168,10 +166,13 @@ def tile_list_tgn_rnnP_kernel(
                 in_=staged,
             )
 
+        def element(k):
+            return DEALT_ELEMENT[k - TILES_A_PASS]
+
         def tile_rows(source, k):
             if k < TILES_A_PASS:
                 return source[k * P : (k + 1) * P, :]
-            return pass_rows(source, 1, slice(0, T))[:, k - TILES_A_PASS, :]
+            return pass_rows(source, 1, slice(0, T))[:, element(k), :]
 
         def load_dealt(i):
             operand = OPERAND_ORDER[i]
@@ -201,7 +202,7 @@ def tile_list_tgn_rnnP_kernel(
             if k < TILES_A_PASS:
                 cols = slice(operand * P, (operand + 1) * P)
                 return w_codes[k % len(w_codes)][:, cols], w_scales[k % len(w_scales)][:, cols]
-            cols = slice((k - TILES_A_PASS) * P, (k - TILES_A_PASS + 1) * P)
+            cols = slice(element(k) * P, (element(k) + 1) * P)
             return dealt_codes[operand][:, cols], dealt_scales[operand][:, cols]
 
         def load_h(k):
@@ -252,14 +253,21 @@ def tile_list_tgn_rnnP_kernel(
                 )
 
         def activate(k, first, count, bank):
-            column = k % TILES_A_PASS
-            row_bias = (bias, dealt_bias)[k // TILES_A_PASS][:, column : column + 1]
+            if k < TILES_A_PASS:
+                row_bias = bias[:, k : k + 1]
+            else:
+                row_bias = dealt_bias[:, element(k) : element(k) + 1]
             nc.scalar.activation(out=tanh_part(k, first, count), in_=bank[:, 0:count], func=ACT.Tanh, bias=row_bias)
 
         def multiply(k):
             for h in range(HALVES):
                 product(k, h * BANK, BANK, sum_banks[h])
                 activate(k, h * BANK, BANK, sum_banks[h])
+
+        def quarter_tanh(k, q):
+            bank = turn_banks[2 * k + q % 2]
+            product(k, q * QUARTER, QUARTER, bank)
+            activate(k, q * QUARTER, QUARTER, bank)
 
         def list_part(first, count):
             return offsets[:, first // LIST_ROWS : (first + count) // LIST_ROWS]
@@ -358,12 +366,7 @@ def tile_list_tgn_rnnP_kernel(
         woven_columns = woven[:].rearrange("p (c t) -> p c t", t=PACK)
 
         def weave(k, cols, copy):
-            copy(out=woven_columns[:, cols, k - TILES_A_PASS], in_=pages[k % PAGES][:, cols])
-
-        def weave_twice(k):
-            t = k - TILES_A_PASS
-            page = pages[k % PAGES][:]
-            nc.scalar.copy(out=woven_columns[:, :, t : t + 2], in_=page.unsqueeze(2).to_broadcast([P, T, 2]))
+            copy(out=woven_columns[:, cols, element(k)], in_=pages[k % PAGES][:, cols])
 
         def quantise_woven(cols):
             nc.vector.quantize_mx(
@@ -412,10 +415,10 @@ def tile_list_tgn_rnnP_kernel(
         )
         nc.vector.tensor_copy(summed[0][:], h_rows[0][:].indirect(offsets[:]))
 
-        nc.tensor.transpose(word_banks[0][:, 0:P], bn_rows[:], ident[:])
+        nc.tensor.transpose(rows_bank[:, 0:P], bn_rows[:], ident[:])
         wgo_cols = w_bf[:].bitcast(F32)[:, BANK : BANK + J // P]
-        nc.scalar.copy(out=wgo_cols, in_=word_banks[0][:, WGO_FROM:P])
-        nc.scalar.copy(out=bias[:], in_=word_banks[0][:, ROWS_FROM:WGO_FROM])
+        nc.scalar.copy(out=wgo_cols, in_=rows_bank[:, WGO_FROM:P])
+        nc.scalar.copy(out=bias[:], in_=rows_bank[:, ROWS_FROM:WGO_FROM])
         for h in range(HALVES):
             for b in range(BLOCKS):
                 column = BLOCKS * h + b
@@ -430,12 +433,6 @@ def tile_list_tgn_rnnP_kernel(
         for a in range(PASSES):
             round_x(0, a)
             quantise_x(0, a)
-
-        def quarter_tanh(k, q):
-            bank = turn_banks[2 * k + q % 2]
-            product(k, q * QUARTER, QUARTER, bank)
-            activate(k, q * QUARTER, QUARTER, bank)
-
         quarter_tanh(0, 0)
         add_picked(0, QUARTER)
         scatter(0, 0, QUARTER)
@@ -474,13 +471,13 @@ def tile_list_tgn_rnnP_kernel(
             round_w(2, 2, step)
             quantise_w(2, 2, step)
         add_page()
-        end = J - QUARTER
+        last_quarter = J - QUARTER
         quarter_tanh(0, QUARTERS - 1)
         quarter_tanh(1, QUARTERS - 1)
-        add_picked(end, QUARTER)
-        gather_add(1, end, QUARTER)
+        add_picked(last_quarter, QUARTER)
+        gather_add(1, last_quarter, QUARTER)
         for k in range(2):
-            scatter(k, end, QUARTER)
+            scatter(k, last_quarter, QUARTER)
             store_page(k)
         load_h(4)
 
@@ -519,8 +516,8 @@ def tile_list_tgn_rnnP_kernel(
                 turn(k - PAGES)
             scatter(k, 0, J)
             store_page(k)
-        weave(last - 2, slice(0, T), copy_s)
-        weave_twice(last - 1)
+        for k in (last - 2, last - 1):
+            weave(k, slice(0, T), copy_s)
         pieces = [slice(first, end) for first, end in zip(WOVEN_EDGES, WOVEN_EDGES[1:])]
         first_piece, shared_piece, *scalar_pieces = pieces
         weave(last, first_piece, copy_v)

@@ -94,7 +94,7 @@ def tile_list_tgn_rnnP_kernel(
         }
         early_tanh = keep.tile([P, 2 * (J - QUARTER)], F32, name="early_tanh", align_bytes=64)
         plain_codes, woven_codes = tiles(PASSES, [P, T], I32, "y_codes")
-        woven_scales = keep.tile([P, T], U8, name="woven_scales", align_bytes=64)
+        woven_scales = keep.tile([P, BANK], U8, name="woven_scales", align_bytes=64)
         plain_scales = keep.tile([P, BANK], U8, name="y_scales0", align_bytes=64)
         banks = [psum.tile([P, BANK], F32, name="bank" + str(i)) for i in range(HALVES + 1 + BLOCKS)]
         copy_s, copy_v = nc.scalar.copy, nc.vector.tensor_copy
@@ -369,9 +369,11 @@ def tile_list_tgn_rnnP_kernel(
             copy(out=woven_columns[:, cols, element(k)], in_=pages[k % PAGES][:, cols])
 
         def quantise_woven(cols):
+            group = cols.start // BANK
+            first = group * BANK
             nc.vector.quantize_mx(
                 out=woven_codes[:, cols].bitcast(FP8X4),
-                scales=woven_scales[:, cols],
+                scales=woven_scales[SCALE_ROWS * group : P, cols.start - first : cols.stop - first],
                 in_=woven[:, PACK * cols.start : PACK * cols.stop],
             )
             nc.sync.dma_start(out=codes_out(1)[:, cols], in_=woven_codes[:, cols])
@@ -527,8 +529,10 @@ def tile_list_tgn_rnnP_kernel(
             weave(last, cols, copy_s)
         for cols in pieces:
             quantise_woven(cols)
-        for quadrant in range(QUADRANTS):
+        for quadrant in (0, 2, 1, 3):
             nc.sync.dma_start(
-                out=out_2[1, SCALE_ROWS * quadrant : SCALE_ROWS * (quadrant + 1), :].bitcast(I32),
-                in_=woven_scales[QUADRANT * quadrant : QUADRANT * quadrant + SCALE_ROWS, :].bitcast(I32),
+                out=out_2[1, SCALE_ROWS * quadrant : SCALE_ROWS * (quadrant + 1), :]
+                .bitcast(I32)
+                .rearrange("r (g c) -> g r c", g=GROUPS),
+                in_=woven_scales[QUADRANT * quadrant : QUADRANT * quadrant + SCALE_ROWS * GROUPS, :].bitcast(I32),
             )

@@ -35,7 +35,6 @@ LIST_ROWS = 16
 QUARTERS = 4
 QUARTER = J // QUARTERS
 PAGES = 3
-W1_STEP = 2
 ROWS_FROM = P - J // P - TILES_A_PASS
 WGO_FROM = P - J // P
 SCALES_FROM = P - QUADRANT
@@ -72,7 +71,7 @@ def tile_list_tgn_rnnP_kernel(
         weight = keep.tile([P, J], F32, name="weight", align_bytes=64)
         x_half = tiles(PASSES, [P, PACK * BANK], F32, "x_half")
         x_rest = tiles(2, [P, PACK * BANK], F32, "x_rest")
-        dealt_raw = [x_half[0], x_half[1], x_rest[0], x_rest[1]]
+        dealt_raw = [x_half[0], x_rest[0], x_rest[1], x_half[1]]
         dealt_codes = tiles(OPERANDS, [P, BANK], U32, "dealt_codes")
         dealt_scales = tiles(OPERANDS, [P, BANK], U8, "dealt_scales")
         woven = keep.tile([P, PACK * T], BF16, name="woven", align_bytes=64)
@@ -82,7 +81,8 @@ def tile_list_tgn_rnnP_kernel(
         slots = tiles(3, [P, 3 * J], F32, "slots")
         wn_raw = [slot[:, J : 2 * J] for slot in slots]
         un_raw = [slot[:, 2 * J : 3 * J] for slot in slots]
-        w_bf = keep.tile([P, PACK * BANK], BF16, name="w_bf", align_bytes=64)
+        pair_raw = [slots[m][:, J : 3 * J].rearrange("p (t a c) -> p t a c", t=PACK, a=PASSES) for m in range(2)]
+        w_bf = keep.tile([P, PACK * (BANK + QUARTER)], BF16, name="w_bf", align_bytes=64)
         w_codes = tiles(3, [P, BANK], U32, "w_codes")
         w_scales = tiles(3, [P, BANK], U8, "w_scales")
         h_rows = tiles(3, [P, T], F32, "h_rows")
@@ -112,11 +112,8 @@ def tile_list_tgn_rnnP_kernel(
                 in_=src.rearrange("p t (c i) -> p c t i", i=RUN),
             )
 
-        def head_buffer(step, piece):
-            return x_bf[(PASSES * step + piece) % len(x_bf)]
-
-        def x_step(q):
-            return q if q < W1_STEP else q + 1
+        def x_staged(q, a):
+            return x_bf[(PASSES * q + a) % len(x_bf)][:]
 
         def x_raw(q, a):
             if q < 2:
@@ -128,12 +125,12 @@ def tile_list_tgn_rnnP_kernel(
                 nc.sync.dma_start(out=x_raw(q, a), in_=pass_rows(x, a, slice(q * QUARTER, (q + 1) * QUARTER)))
 
         def round_x(q, a):
-            interleave(head_buffer(x_step(q), a)[:], x_raw(q, a), copy_v if (q, a) == (0, 1) else copy_s)
+            interleave(x_staged(q, a), x_raw(q, a), copy_v if (q, a) == (0, 1) else copy_s)
 
         def quantise_x(q, a):
             cols = slice(q * QUARTER, (q + 1) * QUARTER)
             nc.vector.quantize_mx(
-                out=x_codes[a][:, cols].bitcast(FP8X4), scales=x_scales[a][:, cols], in_=head_buffer(x_step(q), a)[:]
+                out=x_codes[a][:, cols].bitcast(FP8X4), scales=x_scales[a][:, cols], in_=x_staged(q, a)
             )
 
         def load_w(k):
@@ -145,17 +142,28 @@ def tile_list_tgn_rnnP_kernel(
                     in_=pass_rows(source, operand % PASSES, slice(k * P, (k + 1) * P)),
                 )
 
+        def load_pair():
+            for m, source in enumerate((un, wn)):
+                for a in range(PASSES):
+                    nc.sync.dma_start(out=pair_raw[m][:, :, a, :], in_=pass_rows(source, a, slice(0, 2 * P)))
+
         def w_piece(k, pieces, step):
             width = BANK // pieces
             first = (step + pieces // 2) % pieces * width
             if k in late_staged and step == 1:
                 return slice(first, first + width), late_staged[k][:]
             if k == 1:
-                return slice(first, first + width), head_buffer(W1_STEP, step)[:]
+                return slice(first, first + width), w_bf[:, PACK * BANK : PACK * (BANK + QUARTER)]
             return slice(first, first + width), w_bf[:, PACK * first : PACK * (first + width)]
 
         def round_w(k, pieces, step):
             staged = w_piece(k, pieces, step)[1]
+            if k < 2:
+                nc.scalar.copy(
+                    out=staged.rearrange("p (a c i t) -> p a c t i", a=PASSES, i=RUN, t=PACK),
+                    in_=pair_raw[step][:, :, :, k * P : (k + 1) * P].rearrange("p t a (c i) -> p a c t i", i=RUN),
+                )
+                return
             interleave(staged, by_row((un_raw, wn_raw)[step][k % len(slots)]))
 
         def quantise_w(k, pieces, step):
@@ -209,8 +217,6 @@ def tile_list_tgn_rnnP_kernel(
             nc.sync.dma_start(out=h_rows[k % len(h_rows)][:], in_=tile_rows(hT, k))
 
         def tanh_part(k, first, count):
-            if k == 0 and first == QUARTER:
-                return wn_raw[1][:, 0:count]
             if k < 2 and first < J - QUARTER:
                 place = k * (J - QUARTER) + first
                 return early_tanh[:, place : place + count]
@@ -289,10 +295,18 @@ def tile_list_tgn_rnnP_kernel(
                 op=ALU.add,
             )
 
+        def picked_h(first, count):
+            if first == J - QUARTER:
+                return x_raw(1, 1)[:, 0, :]
+            return summed[0][:, first : first + count]
+
+        def pick_h(first, count):
+            nc.vector.tensor_copy(picked_h(first, count), h_rows[0][:].indirect(list_part(first, count)))
+
         def add_picked(first, count):
             nc.vector.tensor_tensor(
                 out=sum_part(0, first, count),
-                in0=summed[0][:, first : first + count],
+                in0=picked_h(first, count),
                 in1=tanh_part(0, first, count),
                 op=ALU.add,
             )
@@ -390,8 +404,8 @@ def tile_list_tgn_rnnP_kernel(
         nc.sync.dma_start(out=tab_w[:], in_=table)
         nc.vector.memset(planes_s[:].bitcast(I32), 0)
         nc.vector.memset(pages[0][:], 0.0)
-        load_h(0)
-        load_w(0)
+        load_pair()
+        load_x(0)
         nc.vector.tensor_copy(picked_s[:], tab_s[:].indirect(offsets[:]))
         rows = PASSES * SCALE_ROWS
         for quadrant in (0, 2, 1, 3):
@@ -401,9 +415,8 @@ def tile_list_tgn_rnnP_kernel(
                 .rearrange("r (a j) -> r a j", a=PASSES),
                 in_=picked_s[SCALES_FROM + rows * quadrant : SCALES_FROM + rows * (quadrant + 1), :].bitcast(I32),
             )
-        load_x(0)
+        load_h(0)
         load_x(1)
-        load_w(1)
         load_h(1)
         load_x(2)
         load_x(3)
@@ -415,10 +428,9 @@ def tile_list_tgn_rnnP_kernel(
             out=parted_w[:].bitcast(U16).rearrange("p (d j) -> p d j", d=PASSES),
             in_=picked_w[:].bitcast(U16).rearrange("p (j d) -> p d j", d=PASSES),
         )
-        nc.vector.tensor_copy(summed[0][:], h_rows[0][:].indirect(offsets[:]))
 
         nc.tensor.transpose(rows_bank[:, 0:P], bn_rows[:], ident[:])
-        wgo_cols = w_bf[:].bitcast(F32)[:, BANK : BANK + J // P]
+        wgo_cols = w_bf[:].bitcast(F32)[:, 2 * BANK - PACK : 2 * BANK + PACK]
         nc.scalar.copy(out=wgo_cols, in_=rows_bank[:, WGO_FROM:P])
         nc.scalar.copy(out=bias[:], in_=rows_bank[:, ROWS_FROM:WGO_FROM])
         for h in range(HALVES):
@@ -429,33 +441,31 @@ def tile_list_tgn_rnnP_kernel(
                 )
             nc.scalar.copy(out=weight[:, h * BANK : (h + 1) * BANK], in_=sum_banks[h][:])
 
-        for step in range(2):
-            round_w(0, 2, step)
-            quantise_w(0, 2, step)
+        for k, step in ((0, 0), (1, 0), (0, 1)):
+            round_w(k, 2, step)
+            quantise_w(k, 2, step)
         for a in range(PASSES):
             round_x(0, a)
             quantise_x(0, a)
+        round_w(1, 2, 1)
+        quantise_w(1, 2, 1)
+        add_page()
         quarter_tanh(0, 0)
-        add_picked(0, QUARTER)
+        quarter_tanh(1, 0)
+        pick_h(QUARTER, BANK)
+        gather_add(0, 0, QUARTER)
         scatter(0, 0, QUARTER)
         for a in range(PASSES):
             round_x(1, a)
             quantise_x(1, a)
+        pick_h(J - QUARTER, QUARTER)
         load_w(3)
         load_dealt(0)
-        load_dealt(1)
-        load_h(3)
-        nc.sync.dma_start(out=dealt_bias[:], in_=bn[K_PASS:N].rearrange("(p t) -> p t", t=PACK))
-        for step in range(2):
-            round_w(1, 2, step)
-            quantise_w(1, 2, step)
-        add_page()
         quarter_tanh(0, 1)
-        add_picked(QUARTER, QUARTER)
-        scatter(0, QUARTER, QUARTER)
-        quarter_tanh(1, 0)
         gather_add(1, 0, QUARTER)
+        add_picked(QUARTER, QUARTER)
         scatter(1, 0, QUARTER)
+        scatter(0, QUARTER, QUARTER)
         for q in (1, 2):
             round_x(q + 1, 0)
             quantise_x(q + 1, 0)
@@ -468,7 +478,10 @@ def tile_list_tgn_rnnP_kernel(
             gather_add(1, q * QUARTER, QUARTER)
             quantise_x(q + 1, 1)
             scatter(1, q * QUARTER, QUARTER)
-            load_dealt(q + 1)
+            load_dealt(q)
+            if q == 1:
+                load_h(3)
+                nc.sync.dma_start(out=dealt_bias[:], in_=bn[K_PASS:N].rearrange("(p t) -> p t", t=PACK))
         for step in range(2):
             round_w(2, 2, step)
             quantise_w(2, 2, step)
@@ -477,6 +490,7 @@ def tile_list_tgn_rnnP_kernel(
         quarter_tanh(0, QUARTERS - 1)
         quarter_tanh(1, QUARTERS - 1)
         add_picked(last_quarter, QUARTER)
+        load_dealt(3)
         gather_add(1, last_quarter, QUARTER)
         for k in range(2):
             scatter(k, last_quarter, QUARTER)

from contextlib import ExitStack

import concourse.mybir as mybir
from concourse.masks import make_identity

K, M, N, T, J = 1024, 1024, 1024, 2048, 1024
FLOPS = 2 * (K + M) * N * J

F32 = mybir.dt.float32
BF16 = mybir.dt.bfloat16
I32 = mybir.dt.int32
U32 = mybir.dt.uint32
U16 = mybir.dt.uint16
U8 = mybir.dt.uint8
FP8X4 = mybir.dt.float8_e4m3fn_x4
FP4X4 = mybir.dt.float4_e2m1fn_x4
ALU = mybir.AluOpType
ACT = mybir.ActivationFunctionType

P = 128
PACK = 4
K_PASS = P * PACK
PASSES = K // K_PASS
BANK = 512
TILES = N // P
TILES_A_PASS = K_PASS // P
OPERANDS = 2 * PASSES
HALVES = J // BANK
GROUPS = T // BANK
BLOCKS = BANK // P
QUADRANT = 32
QUADRANTS = P // QUADRANT
SCALE_ROWS = 4
LIST_ROWS = 16
QUARTERS = 4
QUARTER = J // QUARTERS
PAGES = 3
ROWS_FROM = P - J // P - TILES_A_PASS
WGO_FROM = P - J // P
SCALES_FROM = P - QUADRANT
RUN = 4
OPERAND_ORDER = (2, 3, 0, 1)
DEALT_ELEMENT = (2, 0, 1, 3)
PAGES_A_STORE = 2
VECTOR_WEAVES = 2 * BANK - P
WOVEN_EDGES = (0, BANK, 2 * BANK, 3 * BANK, T - BANK // 2, T)


def tile_list_tgn_rnnP_kernel(
    tc, x, tab_words, tab_scales, wn, un, bn, hT, wgo, offs, out_0, out_1, out_2
):
    nc = tc.nc
    with ExitStack() as ctx:
        keep = ctx.enter_context(tc.tile_pool(name="keep", bufs=1))
        psum = ctx.enter_context(tc.psum_pool(name="psum", bufs=1))

        def tiles(count, shape, dtype, name):
            return [keep.tile(shape, dtype, name=name + str(i), align_bytes=64) for i in range(count)]

        offsets = keep.tile([P, J // LIST_ROWS], U16, name="offsets")
        tab_w = keep.tile([P, T], I32, name="tab_w", align_bytes=64)
        tab_s = keep.tile([P, T], U8, name="tab_s", align_bytes=64)
        picked_s = keep.tile([P, J], U8, name="picked_s", align_bytes=64)
        planes_s = keep.tile([P, PASSES * J], U8, name="planes_s", align_bytes=64)
        picked_w = keep.tile([P, J], U32, name="picked_w", align_bytes=64)
        parted_w = keep.tile([P, PASSES * 2 * J], U8, name="parted_w", align_bytes=64)
        ident = keep.tile([P, P], F32, name="ident", align_bytes=64)
        bn_rows = keep.tile([P, P], F32, name="bn_rows", align_bytes=64)
        bias = keep.tile([P, TILES_A_PASS], F32, name="bias", align_bytes=64)
        dealt_bias = keep.tile([P, PACK], F32, name="dealt_bias", align_bytes=64)
        weight = keep.tile([P, J], F32, name="weight", align_bytes=64)
        x_half = tiles(PASSES, [P, PACK * BANK], F32, "x_half")
        x_rest = tiles(2, [P, PACK * BANK], F32, "x_rest")
        dealt_raw = [x_half[0], x_rest[0], x_rest[1], x_half[1]]
        dealt_codes = tiles(OPERANDS, [P, BANK], U32, "dealt_codes")
        dealt_scales = tiles(OPERANDS, [P, BANK], U8, "dealt_scales")
        woven = keep.tile([P, PACK * T], BF16, name="woven", align_bytes=64)
        x_bf = tiles(2 * PASSES, [P, PACK * QUARTER], BF16, "x_bf")
        x_codes = tiles(PASSES, [P, J], U32, "x_codes")
        x_scales = tiles(PASSES, [P, J], U8, "x_scales")
        slots = tiles(3, [P, 3 * J], F32, "slots")
        wn_raw = [slot[:, J : 2 * J] for slot in slots]
        un_raw = [slot[:, 2 * J : 3 * J] for slot in slots]
        pair_raw = [slots[m][:, J : 3 * J].rearrange("p (t a c) -> p t a c", t=PACK, a=PASSES) for m in range(2)]
        w_bf = keep.tile([P, PACK * (BANK + QUARTER)], BF16, name="w_bf", align_bytes=64)
        w_codes = tiles(3, [P, BANK], U32, "w_codes")
        w_scales = tiles(3, [P, BANK], U8, "w_scales")
        h_rows = tiles(3, [P, T], F32, "h_rows")
        summed = tiles(2, [P, J], F32, "summed")
        pages = tiles(1, [P, T], F32, "pages")
        late_staged = {
            k: keep.tile([P, PACK * QUARTER], BF16, name="late_staged" + str(k), tag="page" + str(k), align_bytes=64)
            for k in (1, 2)
        }
        early_tanh = keep.tile([P, 2 * (J - QUARTER)], F32, name="early_tanh", align_bytes=64)
        plain_codes, woven_codes = tiles(PASSES, [P, T], I32, "y_codes")
        woven_scales = keep.tile([P, BANK], U8, name="woven_scales", align_bytes=64)
        plain_scales = keep.tile([P, BANK], U8, name="y_scales0", align_bytes=64)
        banks = [psum.tile([P, BANK], F32, name="bank" + str(i)) for i in range(HALVES + 1 + BLOCKS)]
        copy_s, copy_v = nc.scalar.copy, nc.vector.tensor_copy
        sum_banks, rows_bank, turn_banks = banks[0:HALVES], banks[HALVES], banks[HALVES + 1 :]

        def by_row(flat):
            return flat.rearrange("p (t c) -> p t c", t=PACK)

        def pass_rows(source, a, cols):
            return source[a * K_PASS : (a + 1) * K_PASS, cols].rearrange("(p t) c -> p t c", t=PACK)

        def interleave(dst, src, copy=copy_s):
            copy(
                out=dst.rearrange("p (c i t) -> p c t i", i=RUN, t=PACK),
                in_=src.rearrange("p t (c i) -> p c t i", i=RUN),
            )

        def x_staged(q, a):
            return x_bf[(PASSES * q + a) % len(x_bf)][:]

        def x_raw(q, a):
            if q < 2:
                return by_row(x_half[a][:])[:, :, q * QUARTER : (q + 1) * QUARTER]
            return by_row(x_rest[q - 2][:, a * J : (a + 1) * J])

        def load_x(q):
            for a in range(PASSES):
                nc.sync.dma_start(out=x_raw(q, a), in_=pass_rows(x, a, slice(q * QUARTER, (q + 1) * QUARTER)))

        def round_x(q, a):
            interleave(x_staged(q, a), x_raw(q, a), copy_v if (q, a) == (0, 1) else copy_s)

        def quantise_x(q, a):
            cols = slice(q * QUARTER, (q + 1) * QUARTER)
            nc.vector.quantize_mx(
                out=x_codes[a][:, cols].bitcast(FP8X4), scales=x_scales[a][:, cols], in_=x_staged(q, a)
            )

        def load_w(k):
            for operand in OPERAND_ORDER:
                source = (wn, un)[operand // PASSES]
                raw = by_row((wn_raw, un_raw)[operand // PASSES][k % len(slots)])
                nc.sync.dma_start(
                    out=raw[:, :, operand % PASSES * P : (operand % PASSES + 1) * P],
                    in_=pass_rows(source, operand % PASSES, slice(k * P, (k + 1) * P)),
                )

        def load_pair():
            for m, source in enumerate((un, wn)):
                for a in range(PASSES):
                    nc.sync.dma_start(out=pair_raw[m][:, :, a, :], in_=pass_rows(source, a, slice(0, 2 * P)))

        def w_piece(k, pieces, step):
            width = BANK // pieces
            first = (step + pieces // 2) % pieces * width
            if k in late_staged and step == 1:
                return slice(first, first + width), late_staged[k][:]
            if k == 1:
                return slice(first, first + width), w_bf[:, PACK * BANK : PACK * (BANK + QUARTER)]
            return slice(first, first + width), w_bf[:, PACK * first : PACK * (first + width)]

        def round_w(k, pieces, step):
            staged = w_piece(k, pieces, step)[1]
            if k < 2:
                nc.scalar.copy(
                    out=staged.rearrange("p (a c i t) -> p a c t i", a=PASSES, i=RUN, t=PACK),
                    in_=pair_raw[step][:, :, :, k * P : (k + 1) * P].rearrange("p t a (c i) -> p a c t i", i=RUN),
                )
                return
            interleave(staged, by_row((un_raw, wn_raw)[step][k % len(slots)]))

        def quantise_w(k, pieces, step):
            cols, staged = w_piece(k, pieces, step)
            nc.vector.quantize_mx(
                out=w_codes[k % len(w_codes)][:, cols].bitcast(FP8X4),
                scales=w_scales[k % len(w_scales)][:, cols],
                in_=staged,
            )

        def element(k):
            return DEALT_ELEMENT[k - TILES_A_PASS]

        def tile_rows(source, k):
            if k < TILES_A_PASS:
                return source[k * P : (k + 1) * P, :]
            return pass_rows(source, 1, slice(0, T))[:, element(k), :]

        def load_dealt(i):
            operand = OPERAND_ORDER[i]
            source = (wn, un)[operand // PASSES]
            nc.sync.dma_start(out=by_row(dealt_raw[i][:]), in_=pass_rows(source, operand % PASSES, slice(K_PASS, N)))

        def dealt_staged(i):
            if i == 0:
                return slots[0][:, 0:J].bitcast(BF16)
            if i == 1:
                return early_tanh[:, 0:J].bitcast(BF16)
            return dealt_raw[i - 2][:, 0:J].bitcast(BF16)

        def round_dealt(i):
            nc.scalar.copy(
                out=dealt_staged(i).rearrange("p (t m j) -> p m j t", t=PACK, j=PACK),
                in_=dealt_raw[i][:].rearrange("p (j m t) -> p m j t", t=PACK, j=PACK),
            )

        def quantise_dealt(i):
            operand = OPERAND_ORDER[i]
            nc.vector.quantize_mx(
                out=dealt_codes[operand][:].bitcast(FP8X4), scales=dealt_scales[operand][:], in_=dealt_staged(i)
            )

        def stationary(k, operand):
            if k < TILES_A_PASS:
                cols = slice(operand * P, (operand + 1) * P)
                return w_codes[k % len(w_codes)][:, cols], w_scales[k % len(w_scales)][:, cols]
            cols = slice(element(k) * P, (element(k) + 1) * P)
            return dealt_codes[operand][:, cols], dealt_scales[operand][:, cols]

        def load_h(k):
            nc.sync.dma_start(out=h_rows[k % len(h_rows)][:], in_=tile_rows(hT, k))

        def tanh_part(k, first, count):
            if k < 2 and first < J - QUARTER:
                place = k * (J - QUARTER) + first
                return early_tanh[:, place : place + count]
            if k < 2:
                return wn_raw[2][:, k * count : (k + 1) * count]
            if k == 2:
                return un_raw[0][:, first : first + count]
            if k == 3:
                return dealt_raw[1][:, J + first : J + first + count]
            return slots[1 + k % 2][:, first : first + count]

        def turned(k):
            if k == 0:
                return dealt_raw[3][:, J : 2 * J].bitcast(BF16)
            if k == TILES_A_PASS - 1:
                return woven[:, 0:T]
            return slots[1 + k % 2][:, J : 2 * J].bitcast(BF16)

        def product(k, first, count, bank):
            passes = []
            for operand in OPERAND_ORDER:
                width = P if operand >= PASSES and count < BANK else count
                passes.extend((operand, start, width) for start in range(first, first + count, width))
            for i, (operand, start, width) in enumerate(passes):
                a = operand % PASSES
                if operand < PASSES:
                    rhs = x_codes[a][:, start : start + width].bitcast(FP8X4)
                    rhs_scale = x_scales[a][:, start : start + width]
                else:
                    rhs = parted_w[:, 2 * (a * J + start) : 2 * (a * J + start + width)].bitcast(FP4X4)
                    rhs_scale = planes_s[:, a * J + start : a * J + start + width]
                nc.tensor.matmul_mx(
                    out=bank[:, start - first : start - first + width],
                    lhsT=stationary(k, operand)[0].bitcast(FP8X4),
                    lhsT_scale=stationary(k, operand)[1],
                    rhs=rhs,
                    rhs_scale=rhs_scale,
                    start=(i == 0),
                    stop=(i == len(passes) - 1),
                )

        def activate(k, first, count, bank):
            if k < TILES_A_PASS:
                row_bias = bias[:, k : k + 1]
            else:
                row_bias = dealt_bias[:, element(k) : element(k) + 1]
            nc.scalar.activation(out=tanh_part(k, first, count), in_=bank[:, 0:count], func=ACT.Tanh, bias=row_bias)

        def multiply(k):
            for h in range(HALVES):
                product(k, h * BANK, BANK, sum_banks[h])
                activate(k, h * BANK, BANK, sum_banks[h])

        def quarter_tanh(k, q):
            bank = turn_banks[2 * k + q % 2]
            product(k, q * QUARTER, QUARTER, bank)
            activate(k, q * QUARTER, QUARTER, bank)

        def list_part(first, count):
            return offsets[:, first // LIST_ROWS : (first + count) // LIST_ROWS]

        def sum_part(k, first, count):
            if k == 1 and QUARTER <= first < J - QUARTER:
                return x_raw(first // QUARTER + 1, 1)[:, 0, :]
            if k == 2:
                return wn_raw[0][:, first : first + count]
            if k == 3:
                return dealt_raw[3][:, first : first + count]
            return summed[k % 2][:, first : first + count]

        def gather_add(k, first, count):
            nc.vector.tensor_tensor(
                out=sum_part(k, first, count),
                in0=h_rows[k % len(h_rows)][:].indirect(list_part(first, count)),
                in1=tanh_part(k, first, count),
                op=ALU.add,
            )

        def picked_h(first, count):
            if first == J - QUARTER:
                return x_raw(1, 1)[:, 0, :]
            return summed[0][:, first : first + count]

        def pick_h(first, count):
            nc.vector.tensor_copy(picked_h(first, count), h_rows[0][:].indirect(list_part(first, count)))

        def add_picked(first, count):
            nc.vector.tensor_tensor(
                out=sum_part(0, first, count),
                in0=picked_h(first, count),
                in1=tanh_part(0, first, count),
                op=ALU.add,
            )

        def scatter(k, first, count):
            cols = slice(first, first + count)
            nc.vector.tensor_tensor(
                out=pages[k % PAGES][:].indirect(list_part(first, count)),
                in0=sum_part(k, first, count),
                in1=weight[:, cols],
                op=ALU.mult,
            )

        def add_page():
            name = "page" + str(len(pages))
            pages.append(keep.tile([P, T], F32, name=name, tag=name, align_bytes=64))
            nc.gpsimd.memset(pages[-1][:], 0.0)

        def store_page(k):
            nc.sync.dma_start(out=tile_rows(out_0, k), in_=pages[k % PAGES][:])

        def turn(k):
            for b in range(BLOCKS):
                bank = sum_banks[-1] if k > 0 and b == BLOCKS - 1 else turn_banks[b]
                for g in range(GROUPS):
                    first = g * BANK + b * P
                    nc.tensor.transpose(bank[:, g * P : (g + 1) * P], pages[k % PAGES][:, first : first + P], ident[:])
                nc.scalar.copy(
                    out=turned(k)[:, b * BANK : (b + 1) * BANK].rearrange("p (u r e) -> p u r e", u=2, e=2),
                    in_=bank[:].rearrange("p (r u e) -> p u r e", u=2, e=2),
                )

        def staged_y(k):
            return slots[1 + k % 2][:, 2 * J : 3 * J].bitcast(BF16)

        def turn_words(k):
            words = turned(k).bitcast(F32)
            span = BLOCKS // len(sum_banks)
            for i, bank in enumerate(sum_banks):
                for s in range(2 * span):
                    first = (2 * span * i + s) * P
                    nc.tensor.transpose(bank[:, s * P : (s + 1) * P], words[:, first : first + P], ident[:])
                staged = staged_y(k)[:, BANK * span * i : BANK * span * (i + 1)]
                nc.scalar.copy(
                    out=staged.bitcast(F32).rearrange("p (b c u) -> p b c u", b=span, u=2),
                    in_=bank[:].rearrange("p (b u c) -> p b c u", b=span, u=2),
                )

        def codes_out(a):
            return out_1[a].rearrange("p t b -> p (t b)").bitcast(I32)

        def quantise_plain(k):
            nc.vector.quantize_mx(
                out=plain_codes[:, k * BANK : (k + 1) * BANK].bitcast(FP8X4),
                scales=plain_scales[SCALE_ROWS * k : P, :],
                in_=staged_y(k),
            )
            if (k + 1) % PAGES_A_STORE == 0:
                held = slice(k + 1 - PAGES_A_STORE, k + 1)
                by_page = codes_out(0).rearrange("(k q) t -> q k t", q=QUADRANT)
                for g in (0, 2, 1, 3):
                    codes = plain_codes[QUADRANT * g : QUADRANT * (g + 1), :].rearrange("q (k c) -> q k c", k=TILES_A_PASS)
                    nc.sync.dma_start(out=by_page[:, held, g * BANK : (g + 1) * BANK], in_=codes[:, held, :])
            if k == TILES_A_PASS - 1:
                for g in range(GROUPS):
                    nc.sync.dma_start(
                        out=out_2[0, :, g * BANK : (g + 1) * BANK].bitcast(I32),
                        in_=plain_scales[QUADRANT * g : QUADRANT * g + SCALE_ROWS * TILES_A_PASS, :].bitcast(I32),
                    )

        woven_columns = woven[:].rearrange("p (c t) -> p c t", t=PACK)

        def weave(k, cols, copy):
            copy(out=woven_columns[:, cols, element(k)], in_=pages[k % PAGES][:, cols])

        def quantise_woven(cols):
            group = cols.start // BANK
            first = group * BANK
            nc.vector.quantize_mx(
                out=woven_codes[:, cols].bitcast(FP8X4),
                scales=woven_scales[SCALE_ROWS * group : P, cols.start - first : cols.stop - first],
                in_=woven[:, PACK * cols.start : PACK * cols.stop],
            )
            nc.sync.dma_start(out=codes_out(1)[:, cols], in_=woven_codes[:, cols])

        make_identity(nc, ident[:])
        nc.vector.memset(bn_rows[0:ROWS_FROM, :], 0.0)
        nc.vector.memset(tab_s[0:SCALES_FROM, :].bitcast(I32), 0)
        nc.scalar.activation(out=bias[0:ROWS_FROM, 0:1], in_=bn_rows[0:ROWS_FROM, 0:1], func=ACT.Tanh)
        nc.sync.dma_start(offsets[:], offs)
        nc.sync.dma_start(out=tab_s[SCALES_FROM:P, :].bitcast(I32), in_=tab_scales.bitcast(I32).rearrange("a q t -> q a t"))
        table = tab_words[0].rearrange("p t b -> p (t b)").bitcast(I32)
        nc.sync.dma_start(out=bn_rows[ROWS_FROM:WGO_FROM, :], in_=bn[0:K_PASS].rearrange("(i p) -> i p", p=P))
        nc.sync.dma_start(out=bn_rows[WGO_FROM:P, :], in_=wgo[0].rearrange("(i p) -> i p", p=P))
        nc.sync.dma_start(out=tab_w[:], in_=table)
        nc.vector.memset(planes_s[:].bitcast(I32), 0)
        nc.vector.memset(pages[0][:], 0.0)
        load_pair()
        load_x(0)
        nc.vector.tensor_copy(picked_s[:], tab_s[:].indirect(offsets[:]))
        rows = PASSES * SCALE_ROWS
        for quadrant in (0, 2, 1, 3):
            nc.sync.dma_start(
                out=planes_s[QUADRANT * quadrant : QUADRANT * quadrant + SCALE_ROWS, :]
                .bitcast(I32)
                .rearrange("r (a j) -> r a j", a=PASSES),
                in_=picked_s[SCALES_FROM + rows * quadrant : SCALES_FROM + rows * (quadrant + 1), :].bitcast(I32),
            )
        load_h(0)
        load_x(1)
        load_h(1)
        load_x(2)
        load_x(3)
        load_w(2)
        load_h(2)

        nc.vector.tensor_copy(picked_w[:], tab_w[:].bitcast(U32).indirect(offsets[:]))
        nc.vector.tensor_copy(
            out=parted_w[:].bitcast(U16).rearrange("p (d j) -> p d j", d=PASSES),
            in_=picked_w[:].bitcast(U16).rearrange("p (j d) -> p d j", d=PASSES),
        )

        nc.tensor.transpose(rows_bank[:, 0:P], bn_rows[:], ident[:])
        wgo_cols = w_bf[:].bitcast(F32)[:, 2 * BANK - PACK : 2 * BANK + PACK]
        nc.scalar.copy(out=wgo_cols, in_=rows_bank[:, WGO_FROM:P])
        nc.scalar.copy(out=bias[:], in_=rows_bank[:, ROWS_FROM:WGO_FROM])
        for h in range(HALVES):
            for b in range(BLOCKS):
                column = BLOCKS * h + b
                nc.tensor.transpose(
                    sum_banks[h][:, b * P : (b + 1) * P], wgo_cols[:, column : column + 1].to_broadcast([P, P]), ident[:]
                )
            nc.scalar.copy(out=weight[:, h * BANK : (h + 1) * BANK], in_=sum_banks[h][:])

        for k, step in ((0, 0), (1, 0), (0, 1)):
            round_w(k, 2, step)
            quantise_w(k, 2, step)
        for a in range(PASSES):
            round_x(0, a)
            quantise_x(0, a)
        round_w(1, 2, 1)
        quantise_w(1, 2, 1)
        add_page()
        quarter_tanh(0, 0)
        quarter_tanh(1, 0)
        pick_h(QUARTER, BANK)
        gather_add(0, 0, QUARTER)
        scatter(0, 0, QUARTER)
        for a in range(PASSES):
            round_x(1, a)
            quantise_x(1, a)
        pick_h(J - QUARTER, QUARTER)
        load_w(3)
        load_dealt(0)
        quarter_tanh(0, 1)
        gather_add(1, 0, QUARTER)
        add_picked(QUARTER, QUARTER)
        scatter(1, 0, QUARTER)
        scatter(0, QUARTER, QUARTER)
        for q in (1, 2):
            round_x(q + 1, 0)
            quantise_x(q + 1, 0)
            if q == 2:
                quarter_tanh(0, q)
                add_picked(q * QUARTER, QUARTER)
                scatter(0, q * QUARTER, QUARTER)
            round_x(q + 1, 1)
            quarter_tanh(1, q)
            gather_add(1, q * QUARTER, QUARTER)
            quantise_x(q + 1, 1)
            scatter(1, q * QUARTER, QUARTER)
            load_dealt(q)
            if q == 1:
                load_h(3)
                nc.sync.dma_start(out=dealt_bias[:], in_=bn[K_PASS:N].rearrange("(p t) -> p t", t=PACK))
        for step in range(2):
            round_w(2, 2, step)
            quantise_w(2, 2, step)
        add_page()
        last_quarter = J - QUARTER
        quarter_tanh(0, QUARTERS - 1)
        quarter_tanh(1, QUARTERS - 1)
        add_picked(last_quarter, QUARTER)
        load_dealt(3)
        gather_add(1, last_quarter, QUARTER)
        for k in range(2):
            scatter(k, last_quarter, QUARTER)
            store_page(k)
        load_h(4)

        round_w(3, 2, 0)
        multiply(2)
        round_w(3, 2, 1)
        gather_add(2, 0, J)
        load_h(5)
        quantise_w(3, 1, 0)
        scatter(2, 0, J)
        store_page(2)

        for i in range(OPERANDS - 1):
            round_dealt(i)
            quantise_dealt(i)
        multiply(3)
        round_dealt(OPERANDS - 1)
        gather_add(3, 0, J)
        load_h(6)
        quantise_dealt(OPERANDS - 1)
        turn(0)
        scatter(3, 0, J)
        store_page(3)

        last = TILES - 1
        for k in range(TILES_A_PASS, TILES):
            multiply(k)
            gather_add(k, 0, J)
            if k + len(h_rows) < TILES:
                load_h(k + len(h_rows))
            turn_words(k - TILES_A_PASS)
            quantise_plain(k - TILES_A_PASS)
            if k == last:
                weave(last - PAGES, slice(0, T), copy_s)
            else:
                turn(k - PAGES)
            scatter(k, 0, J)
            store_page(k)
        for k in (last - 2, last - 1):
            weave(k, slice(0, T), copy_s)
        pieces = [slice(first, end) for first, end in zip(WOVEN_EDGES, WOVEN_EDGES[1:])]
        first_piece, shared_piece, *scalar_pieces = pieces
        weave(last, first_piece, copy_v)
        weave(last, slice(shared_piece.start, VECTOR_WEAVES), copy_v)
        weave(last, slice(VECTOR_WEAVES, shared_piece.stop), copy_s)
        for cols in scalar_pieces:
            weave(last, cols, copy_s)
        for cols in pieces:
            quantise_woven(cols)
        for quadrant in (0, 2, 1, 3):
            nc.sync.dma_start(
                out=out_2[1, SCALE_ROWS * quadrant : SCALE_ROWS * (quadrant + 1), :]
                .bitcast(I32)
                .rearrange("r (g c) -> g r c", g=GROUPS),
                in_=woven_scales[QUADRANT * quadrant : QUADRANT * quadrant + SCALE_ROWS * GROUPS, :].bitcast(I32),
            )
